import numpy as np
import ml_dtypes


def mxq(x, axis, fmt="e4m3"):
    dtype, down = {"e4m3": (ml_dtypes.float8_e4m3fn, 7), "e5m2": (ml_dtypes.float8_e5m2, 14)}[fmt]
    v = np.moveaxis(np.asarray(x, np.float32).astype(ml_dtypes.bfloat16).astype(np.float64), axis, -1)
    blocks = v.reshape(v.shape[:-1] + (-1, 32))
    amax = np.abs(blocks).max(-1, keepdims=True)
    byte = np.maximum(np.where(amax > 0, np.frexp(amax)[1] - 1 + 127, 0) - down, 1)
    scale = np.exp2(byte - 127.0)
    codes = (blocks / scale).astype(np.float32).astype(dtype).astype(np.float64)
    return np.moveaxis((codes * scale).reshape(v.shape), -1, axis)


WIDE = False


def mx_kscale(k):
    if not WIDE:
        return np.ones(k)
    levels = np.array([10, -10, 5, -5, 0])
    if k % 512:
        return np.exp2(np.random.permutation(np.resize(levels, k // 32))).repeat(32)
    a = np.empty((k // 512, 16))
    for p in range(k // 512):
        a[p, :8] = np.random.permutation(np.resize(levels, 8))
        for g in range(8):
            far = levels[np.abs(levels - a[p, g]) >= 10]
            a[p, g + 8] = far[np.random.randint(len(far))]
    return np.exp2(a.ravel()).repeat(32)


def f64(x):
    return np.asarray(x).astype(np.float64)


def striped(idx):
    return np.tile(idx.reshape(-1, 16).T, (8, 1)).astype(np.uint16)


def unstriped(offs):
    return offs[:16].T.reshape(-1).astype(np.int64)


E2M1 = np.array([0.0, 0.5, 1.0, 1.5, 2.0, 3.0, 4.0, 6.0, -0.0, -0.5, -1.0, -1.5, -2.0, -3.0, -4.0, -6.0])


def pack_weight(w, fmt):
    k, n = w.shape
    w = f64(np.asarray(w, np.float32).astype(ml_dtypes.bfloat16)).reshape(k // 32, 32, n)
    amax = np.abs(w).max(1)
    if fmt == "e4m3":
        byte = np.frexp(amax)[1] - 1 + 127 - 7
    else:
        mant, ex = np.frexp(amax / 6.0)
        byte = np.where(mant > 0.5, ex, ex - 1) + 127
    byte = np.clip(np.where(amax > 0, byte, 1), 1, 254)
    scaled = (w * np.exp2(127.0 - byte)[:, None, :]).reshape(k, n).astype(np.float32)
    by_word = np.ascontiguousarray(scaled.reshape(k // 512, 128, 4, n).transpose(0, 1, 3, 2))
    if fmt == "e4m3":
        words = by_word.astype(ml_dtypes.float8_e4m3fn).view(np.uint8)
    else:
        c = by_word.astype(ml_dtypes.float4_e2m1fn).view(np.uint8) & 0xF
        words = (c[..., 0::2] | (c[..., 1::2] << 4)).reshape(k // 512, 128, 2 * n)
    return np.ascontiguousarray(words), np.ascontiguousarray(byte.astype(np.uint8).reshape(k // 512, 16, n))


def unpack_weight(words, scales, fmt):
    g, _, n = scales.shape
    words = np.ascontiguousarray(words).reshape(g, 128, n, -1)
    if fmt == "e4m3":
        vals = words.view(ml_dtypes.float8_e4m3fn).astype(np.float64)
    else:
        nib = np.empty((g, 128, n, 4), np.uint8)
        nib[..., 0::2] = words & 0xF
        nib[..., 1::2] = words >> 4
        vals = E2M1[nib]
    vals = vals * np.repeat(np.exp2(scales.astype(np.float64) - 127.0), 8, axis=1)[..., None]
    return vals.transpose(0, 1, 3, 2).reshape(g * 512, n)


def gelu(v):
    return 0.5 * v * (1.0 + np.tanh(np.sqrt(2.0 / np.pi) * (v + 0.044715 * v**3)))


K, H, N, T, S, T2, P = 1536, 1024, 512, 4096, 1024, 2048, 1024

def setup_inputs():
    n = np.random.standard_normal
    s = mx_kscale(K)[:, None]
    u = mx_kscale(H)[:, None]
    tab_words, tab_scales = pack_weight(n((K, T)) * s, "e4m3")
    w4_words, w4_scales = pack_weight(1.5 * n((K, H)) / np.sqrt(K) / s, "e2m1")
    return {
        "tab_words": tab_words, "tab_scales": tab_scales,
        "offs": striped(np.random.permutation(T)[:S]),
        "w4_words": w4_words, "w4_scales": w4_scales,
        "wgs": np.exp(0.3 * n((128, S))).astype(np.float32),
        "page0": (1.5 * n((H, T2))).astype(np.float32),
        "offs2": striped(np.random.permutation(T2)[:S]),
        "offs3": striped(np.random.permutation(T2)[:P]),
        "gain": (np.exp(0.3 * n(H)) * u[:, 0]).astype(np.float32),
        "wb": (2.0 * n((H, N)) / np.sqrt(H) / u).astype(np.float32),
    }

def reference(tab_words, tab_scales, offs, w4_words, w4_scales, wgs, page0, offs2, offs3, gain, wb):
    v = unpack_weight(tab_words, tab_scales, "e4m3")[:, unstriped(offs)]
    h = unpack_weight(w4_words, w4_scales, "e2m1").T @ v
    page = f64(page0).copy()
    page[:, unstriped(offs2)] = np.tile(f64(wgs), (H // 128, 1)) * h
    x = page[:, unstriped(offs3)]
    z = x / (1.0 + np.abs(x)) * f64(gain)[:, None]
    out = mxq(f64(wb), 0, "e4m3").T @ mxq(z, 0, "e4m3")
    return out

@@ -1,0 +1,299 @@
+from contextlib import ExitStack
+
+import concourse.mybir as mybir
+
+K, H, N, T, S, T2, M = 1536, 1024, 512, 4096, 1024, 2048, 1024
+FLOPS = 2 * K * H * S + 2 * H * N * M
+
+F32 = mybir.dt.float32
+BF16 = mybir.dt.bfloat16
+I32 = mybir.dt.int32
+U32 = mybir.dt.uint32
+U16 = mybir.dt.uint16
+U8 = mybir.dt.uint8
+FP8X4 = mybir.dt.float8_e4m3fn_x4
+FP4X4 = mybir.dt.float4_e2m1fn_x4
+MULT = mybir.AluOpType.mult
+ACT = mybir.ActivationFunctionType
+
+P = 128
+PACK = 4
+PASS = P * PACK
+A = K // PASS
+B = H // PASS
+HALF = 512
+QUARTER = 256
+STRIPE = 16
+
+
+def tile_list_seller_trust_cache_kernel(
+    tc, tab_words, tab_scales, offs, w4_words, w4_scales, wgs, page0, offs2, offs3, gain, wb, out
+):
+    nc = tc.nc
+    with ExitStack() as ctx:
+        keep = ctx.enter_context(tc.tile_pool(name="keep", bufs=1))
+        pages = ctx.enter_context(tc.tile_pool(name="pages", bufs=4))
+        work = ctx.enter_context(tc.tile_pool(name="work", bufs=3))
+        two = ctx.enter_context(tc.tile_pool(name="two", bufs=2))
+        four = ctx.enter_context(tc.tile_pool(name="four", bufs=4))
+        psum = ctx.enter_context(tc.psum_pool(name="psum", bufs=1))
+
+        list1 = keep.tile([P, S // STRIPE], U16, name="list1")
+        list2 = keep.tile([P, S // STRIPE], U16, name="list2")
+        list3 = keep.tile([P, M // STRIPE], U16, name="list3")
+
+        def cols(lst, lo, hi):
+            return lst[:, lo // STRIPE : hi // STRIPE]
+
+        tab_scale_win = keep.tile([P, T], U8, name="tab_scale_win", align_bytes=64)
+        w_scale_raw = keep.tile([P, A, H], U8, name="w_scale_raw", align_bytes=64)
+        v_scale = [keep.tile([P, S], U8, name="v_scale%d" % a, align_bytes=64) for a in range(A)]
+        nc.vector.memset(tab_scale_win[:].bitcast(I32), 0)
+        nc.vector.memset(w_scale_raw[:].bitcast(I32), 0)
+        for a in range(1, A):
+            nc.vector.memset(v_scale[a][:].bitcast(I32), 0)
+
+        warm = keep.tile([P, 1], F32, name="warm")
+        nc.gpsimd.memset(warm[:], 1.0)
+        nc.scalar.activation(warm[:], warm[:], ACT.Abs_reciprocal_sqrt)
+
+        tab = [keep.tile([P, T], I32, name="tab%d" % a, tag="big%d" % a, align_bytes=64) for a in range(A)]
+
+        def load_tab(a):
+            nc.sync.dma_start(out=tab[a][:], in_=tab_words[a].rearrange("p n t -> p (n t)").bitcast(I32))
+
+        w_raw = [keep.tile([P, A, PASS // 2], I32, name="w_raw%d" % b, align_bytes=64) for b in range(B)]
+        w_words_i32 = w4_words.rearrange("a p n -> p a n").bitcast(I32)
+
+        def load_w(b):
+            nc.sync.dma_start(out=w_raw[b][:], in_=w_words_i32[:, :, b * 256 : (b + 1) * 256])
+
+        wg = [keep.tile([P, S], F32, name="wg%d" % t) for t in range(PACK)]
+        wgs_rows = wgs.rearrange("(u t e) j -> t u e j", t=PACK, e=2)
+
+        def load_wg(t):
+            for q in range(4):
+                nc.sync.dma_start(out=wg[t][32 * q : 32 * q + 32, :], in_=wgs_rows[t])
+
+        page_rows = page0.rearrange("(b u t e) c -> b t u e c", b=B, t=PACK, e=2)
+        page = {}
+
+        def load_page(i):
+            page[i] = pages.tile([P, T2], F32, name="page")
+            nc.sync.dma_start(out=page[i][:], in_=page_rows[i // PACK, i % PACK])
+
+        gain_rows = gain.rearrange("(b u w) -> u b w", b=B, w=2 * PACK)
+        gain_sb = keep.tile([P, B, 2 * PACK], F32, name="gain_sb")
+
+        load_tab(0)
+        nc.sync.dma_start(list1[:], offs)
+        for q in range(4):
+            nc.sync.dma_start(
+                out=tab_scale_win[32 * q : 32 * q + 4 * A, :].bitcast(I32),
+                in_=tab_scales[:, 4 * q : 4 * q + 4, :].bitcast(I32),
+            )
+        load_w(0)
+        load_tab(1)
+        for q in range(4):
+            nc.sync.dma_start(
+                out=w_scale_raw[32 * q : 32 * q + 4, :, :].bitcast(I32),
+                in_=w4_scales[:, 4 * q : 4 * q + 4, :].rearrange("a r n -> r a n").bitcast(I32),
+            )
+        load_tab(2)
+        nc.sync.dma_start(list2[:], offs2)
+        load_page(0)
+        load_wg(0)
+        nc.sync.dma_start(list3[:], offs3)
+        load_page(1)
+        load_wg(1)
+        load_w(1)
+        for e in range(2):
+            nc.sync.dma_start(out=gain_sb[e:P:2, :, 0 : 2 * PACK - 1], in_=gain_rows[:, :, e : e + 2 * PACK - 1])
+        load_page(2)
+        load_wg(2)
+        load_page(3)
+        load_wg(3)
+        for i in range(4, 4):
+            load_page(i)
+
+        nc.vector.tensor_copy(v_scale[0][:], tab_scale_win[:].indirect(list1[:]))
+        for a in range(1, A):
+            nc.scalar.dma_start(
+                out=v_scale[a][0:112, :].bitcast(I32), in_=v_scale[0][4 * a : 4 * a + 112, :].bitcast(I32)
+            )
+
+        w_codes = [keep.tile([P, A, PACK, 2 * P], U8, name="w_codes%d" % b, align_bytes=64) for b in range(B)]
+        w_scale = [keep.tile([P, A, PACK, P], U8, name="w_scale%d" % b, align_bytes=64) for b in range(B)]
+
+        def permute_w_codes(b):
+            nc.vector.tensor_copy(
+                w_codes[b][:].bitcast(I32), w_raw[b][:].rearrange("p a (u t) -> p a t u", t=PACK)
+            )
+
+        def permute_w_scale(b):
+            nc.vector.tensor_copy(
+                w_scale[b][:].bitcast(U16),
+                w_scale_raw[:, :, b * PASS : (b + 1) * PASS].bitcast(U16).rearrange("p a (u t) -> p a t u", t=PACK),
+            )
+
+        v_codes = {}
+
+        def gather_words(a, lo, hi):
+            tile = keep.tile([P, hi - lo], U32, name="v_codes%d_%d" % (a, lo), align_bytes=64)
+            nc.vector.tensor_copy(tile[:], tab[a][:].bitcast(U32).indirect(cols(list1, lo, hi)))
+            for c in range(lo, hi, HALF):
+                v_codes[a, c // HALF] = tile[:, c - lo : c - lo + HALF]
+
+        gather_words(0, 0, S)
+        permute_w_codes(0)
+        gather_words(1, 0, S)
+        permute_w_scale(0)
+        permute_w_scale(1)
+        gather_words(2, 0, HALF)
+        gather_words(2, HALF, S)
+
+        def bank(n, name):
+            return psum.tile([P, HALF], F32, name=name, tag="bank%d" % n)
+
+        tiles = B * PACK
+        last = tiles - 1
+        slots = keep.tile([P, (tiles + 1) * S], F32, name="slots", align_bytes=64)
+        slots_bf = slots[:].bitcast(BF16)
+        h = [slots[:, i * S : (i + 1) * S] for i in range(tiles)]
+        z_all = slots_bf[:, 2 * S :].rearrange("p (i m) -> p i m", m=2 * S)
+
+        def first_product(i):
+            b, t = divmod(i, PACK)
+            for half in range(2):
+                acc = bank((2 * i + half) % 8, "acc_h")
+                for a in range(A):
+                    nc.tensor.matmul_mx(
+                        out=acc[:],
+                        lhsT=w_codes[b][:, a, t, :].bitcast(FP4X4),
+                        lhsT_scale=w_scale[b][:, a, t, :],
+                        rhs=v_codes[a, half].bitcast(FP8X4),
+                        rhs_scale=v_scale[a][:, half * HALF : (half + 1) * HALF],
+                        start=(a == 0),
+                        stop=(a == A - 1),
+                    )
+                nc.scalar.copy(h[i][:, half * HALF : (half + 1) * HALF], acc[:])
+
+        def scatter(i, lo, hi):
+            nc.vector.tensor_tensor(
+                page[i][:].indirect(cols(list2, lo, hi)), h[i][:, lo:hi], wg[i % PACK][:, lo:hi], MULT
+            )
+
+        x = {}
+        d = {}
+
+        def gather_page(i, lo, hi):
+            if lo == 0:
+                x[i] = work.tile([P, M], F32, name="x")
+                d[i] = work.tile([P, M], F32, name="d")
+            nc.vector.tensor_copy(x[i][:, lo:hi], page[i][:].indirect(cols(list3, lo, hi)))
+            nc.scalar.activation(d[i][:, lo:hi], x[i][:, lo:hi], ACT.Abs)
+            nc.scalar.activation(d[i][:, lo:hi], d[i][:, lo:hi], ACT.Abs_reciprocal_sqrt, bias=1.0)
+            nc.scalar.activation(d[i][:, lo:hi], d[i][:, lo:hi], ACT.Square)
+
+        def softsign(i, lo, hi):
+            b, t = divmod(i, PACK)
+            z = slots_bf[:, 2 * S * (i + 1) + lo : 2 * S * (i + 1) + hi]
+            nc.vector.scalar_tensor_tensor(z, x[i][:, lo:hi], gain_sb[:, b, 2 * t : 2 * t + 1], d[i][:, lo:hi], MULT, MULT)
+
+        def interleave(src, width, on_vector):
+            pool = two if width == HALF else four
+            dst = pool.tile([P, width, PACK], BF16, name="woven", align_bytes=64)
+            move = nc.vector.tensor_copy if on_vector else nc.scalar.copy
+            move(dst[:].rearrange("p (c i) t -> p c t i", i=4), src.rearrange("p t (c i) -> p c t i", i=4))
+            return dst
+
+        def quantize(woven, width, name):
+            codes = keep.tile([P, width], U32, name=name + "_codes", align_bytes=64)
+            scale = keep.tile([P, width], U8, name=name + "_scale", align_bytes=64)
+            nc.vector.quantize_mx(
+                out=codes[:].bitcast(FP8X4), scales=scale[:], in_=woven[:].rearrange("p w t -> p (w t)")
+            )
+            return codes, scale
+
+        wb_rows = wb.rearrange("(b u t e) n -> b t u e n", b=B, t=PACK, e=2)
+        wb_q = {}
+
+        def prepare_wb(b):
+            raw = keep.tile([P, PACK * N], F32, name="wb_raw", tag="big%d" % b, align_bytes=64)
+            for t in range(PACK):
+                nc.sync.dma_start(out=raw[:, t * N : (t + 1) * N], in_=wb_rows[b, t])
+            wb_q[b] = quantize(interleave(raw[:].rearrange("p (t n) -> p t n", t=PACK), N, False), N, "wb%d" % b)
+
+        z_q = {}
+
+        def weave_z(b, lo, hi, on_vector):
+            return interleave(z_all[:, b * PACK : (b + 1) * PACK, lo:hi], hi - lo, on_vector)
+
+        def quantize_z(b, lo, hi, woven):
+            codes, scale = quantize(woven, hi - lo, "z%d_%d" % (b, lo))
+            for c in range(lo, hi, QUARTER):
+                z_q[b, c // QUARTER] = (codes[:, c - lo : c - lo + QUARTER], scale[:, c - lo : c - lo + QUARTER])
+
+        out_rows = out.rearrange("(n p) m -> p n m", p=P)
+
+        def second_product(quarter, banks):
+            per_bank = N // P // len(banks)
+            for g, number in enumerate(banks):
+                acc = bank(number, "acc_out")
+                for s in range(per_bank):
+                    n = g * per_bank + s
+                    for b in range(B):
+                        nc.tensor.matmul_mx(
+                            out=acc[:, s * QUARTER : (s + 1) * QUARTER],
+                            lhsT=wb_q[b][0][:, n * P : (n + 1) * P].bitcast(FP8X4),
+                            lhsT_scale=wb_q[b][1][:, n * P : (n + 1) * P],
+                            rhs=z_q[b, quarter][0].bitcast(FP8X4),
+                            rhs_scale=z_q[b, quarter][1],
+                            start=(b == 0),
+                            stop=(b == B - 1),
+                        )
+                res = four.tile([P, HALF], F32, name="res")
+                width = per_bank * QUARTER
+                if quarter == 3 and g % 2 == 1:
+                    nc.vector.tensor_copy(res[:, :width], acc[:, :width])
+                else:
+                    nc.scalar.copy(res[:, :width], acc[:, :width])
+                nc.sync.dma_start(
+                    out=out_rows[:, g * per_bank : (g + 1) * per_bank, quarter * QUARTER : (quarter + 1) * QUARTER],
+                    in_=res[:, :width].rearrange("p (s w) -> p s w", s=per_bank),
+                )
+
+        first_product(0)
+        first_product(1)
+        scatter(0, 0, HALF)
+        scatter(0, HALF, S)
+        gather_page(0, 0, M)
+        permute_w_codes(1)
+        for i in range(1, tiles):
+            if i + 1 < tiles:
+                first_product(i + 1)
+            if i + 3 < tiles:
+                load_page(i + 3)
+            scatter(i, 0, S)
+            if i < last:
+                softsign(i - 1, 0, M)
+                gather_page(i, 0, M)
+            if i in (2, 3):
+                prepare_wb(i - 2)
+            if i in (5, 6):
+                lo = (i - 5) * HALF
+                quantize_z(0, lo, lo + HALF, weave_z(0, lo, lo + HALF, False))
+
+        for quarter in range(4):
+            gather_page(last, quarter * QUARTER, (quarter + 1) * QUARTER)
+        softsign(last - 1, 0, M)
+        quarter_banks = [(0, 1), (2, 3), (0, 1), (4, 5, 6, 7)]
+        woven = {}
+        for quarter in range(4):
+            lo, hi = quarter * QUARTER, (quarter + 1) * QUARTER
+            softsign(last, lo, hi)
+            woven[quarter] = weave_z(1, lo, hi, quarter % 2 == 0)
+        for quarter in range(4):
+            lo, hi = quarter * QUARTER, (quarter + 1) * QUARTER
+            quantize_z(1, lo, hi, woven[quarter])
+            second_product(quarter, quarter_banks[quarter])

@@ -24,6 +24,7 @@ B = H // PASS
 HALF = 512
 QUARTER = 256
 STRIPE = 16
+PAGE_BUFS = 4
 
 
 def tile_list_seller_trust_cache_kernel(
@@ -32,10 +33,7 @@ def tile_list_seller_trust_cache_kernel(
     nc = tc.nc
     with ExitStack() as ctx:
         keep = ctx.enter_context(tc.tile_pool(name="keep", bufs=1))
-        pages = ctx.enter_context(tc.tile_pool(name="pages", bufs=4))
-        work = ctx.enter_context(tc.tile_pool(name="work", bufs=3))
-        two = ctx.enter_context(tc.tile_pool(name="two", bufs=2))
-        four = ctx.enter_context(tc.tile_pool(name="four", bufs=4))
+        pages = ctx.enter_context(tc.tile_pool(name="pages", bufs=PAGE_BUFS))
         psum = ctx.enter_context(tc.psum_pool(name="psum", bufs=1))
 
         list1 = keep.tile([P, S // STRIPE], U16, name="list1")
@@ -53,10 +51,6 @@ def tile_list_seller_trust_cache_kernel(
         for a in range(1, A):
             nc.vector.memset(v_scale[a][:].bitcast(I32), 0)
 
-        warm = keep.tile([P, 1], F32, name="warm")
-        nc.gpsimd.memset(warm[:], 1.0)
-        nc.scalar.activation(warm[:], warm[:], ACT.Abs_reciprocal_sqrt)
-
         tab = [keep.tile([P, T], I32, name="tab%d" % a, tag="big%d" % a, align_bytes=64) for a in range(A)]
 
         def load_tab(a):
@@ -68,12 +62,12 @@ def tile_list_seller_trust_cache_kernel(
         def load_w(b):
             nc.sync.dma_start(out=w_raw[b][:], in_=w_words_i32[:, :, b * 256 : (b + 1) * 256])
 
-        wg = [keep.tile([P, S], F32, name="wg%d" % t) for t in range(PACK)]
+        wg = [keep.tile([P, S], F32, name="wg%d" % t, tag="wg%d" % t, align_bytes=64) for t in range(PACK)]
         wgs_rows = wgs.rearrange("(u t e) j -> t u e j", t=PACK, e=2)
 
-        def load_wg(t):
-            for q in range(4):
-                nc.sync.dma_start(out=wg[t][32 * q : 32 * q + 32, :], in_=wgs_rows[t])
+        def load_wg(t, lo, hi):
+            for q in (0, 2, 1, 3):
+                nc.sync.dma_start(out=wg[t][32 * q : 32 * q + 32, lo:hi], in_=wgs_rows[t][:, :, lo:hi])
 
         page_rows = page0.rearrange("(b u t e) c -> b t u e c", b=B, t=PACK, e=2)
         page = {}
@@ -99,22 +93,21 @@ def tile_list_seller_trust_cache_kernel(
                 out=w_scale_raw[32 * q : 32 * q + 4, :, :].bitcast(I32),
                 in_=w4_scales[:, 4 * q : 4 * q + 4, :].rearrange("a r n -> r a n").bitcast(I32),
             )
-        load_tab(2)
         nc.sync.dma_start(list2[:], offs2)
+        load_tab(2)
         load_page(0)
-        load_wg(0)
+        load_wg(0, 0, HALF)
+        load_wg(0, HALF, S)
         nc.sync.dma_start(list3[:], offs3)
-        load_page(1)
-        load_wg(1)
         load_w(1)
+        load_page(1)
+        load_wg(1, 0, S)
         for e in range(2):
             nc.sync.dma_start(out=gain_sb[e:P:2, :, 0 : 2 * PACK - 1], in_=gain_rows[:, :, e : e + 2 * PACK - 1])
         load_page(2)
-        load_wg(2)
+        load_wg(2, 0, S)
         load_page(3)
-        load_wg(3)
-        for i in range(4, 4):
-            load_page(i)
+        load_wg(3, 0, S)
 
         nc.vector.tensor_copy(v_scale[0][:], tab_scale_win[:].indirect(list1[:]))
         for a in range(1, A):
@@ -127,13 +120,16 @@ def tile_list_seller_trust_cache_kernel(
 
         def permute_w_codes(b):
             nc.vector.tensor_copy(
-                w_codes[b][:].bitcast(I32), w_raw[b][:].rearrange("p a (u t) -> p a t u", t=PACK)
+                w_codes[b][:].bitcast(I32).rearrange("p a t (c i) -> p a c t i", i=4),
+                w_raw[b][:].rearrange("p a (c i t) -> p a c t i", i=4, t=PACK),
             )
 
         def permute_w_scale(b):
             nc.vector.tensor_copy(
-                w_scale[b][:].bitcast(U16),
-                w_scale_raw[:, :, b * PASS : (b + 1) * PASS].bitcast(U16).rearrange("p a (u t) -> p a t u", t=PACK),
+                w_scale[b][:].bitcast(U16).rearrange("p a t (c i) -> p a c t i", i=8),
+                w_scale_raw[:, :, b * PASS : (b + 1) * PASS]
+                .bitcast(U16)
+                .rearrange("p a (c i t) -> p a c t i", i=8, t=PACK),
             )
 
         v_codes = {}
@@ -157,15 +153,17 @@ def tile_list_seller_trust_cache_kernel(
 
         tiles = B * PACK
         last = tiles - 1
-        slots = keep.tile([P, (tiles + 1) * S], F32, name="slots", align_bytes=64)
-        slots_bf = slots[:].bitcast(BF16)
-        h = [slots[:, i * S : (i + 1) * S] for i in range(tiles)]
-        z_all = slots_bf[:, 2 * S :].rearrange("p (i m) -> p i m", m=2 * S)
+        slots = [keep.tile([P, PACK * S], F32, name="slots%d" % b, align_bytes=64) for b in range(B)]
+        recip = [keep.tile([P, PACK * M], F32, name="recip%d" % b, tag="big%d" % (b + 1), align_bytes=64) for b in range(B)]
+
+        def row_tile(pair, i, lo, hi):
+            b, t = divmod(i, PACK)
+            return pair[b][:, t * S + lo : t * S + hi]
 
         def first_product(i):
             b, t = divmod(i, PACK)
             for half in range(2):
-                acc = bank((2 * i + half) % 8, "acc_h")
+                acc = bank(half, "acc_h")
                 for a in range(A):
                     nc.tensor.matmul_mx(
                         out=acc[:],
@@ -176,36 +174,22 @@ def tile_list_seller_trust_cache_kernel(
                         start=(a == 0),
                         stop=(a == A - 1),
                     )
-                nc.scalar.copy(h[i][:, half * HALF : (half + 1) * HALF], acc[:])
+                nc.scalar.copy(row_tile(slots, i, half * HALF, (half + 1) * HALF), acc[:])
 
         def scatter(i, lo, hi):
             nc.vector.tensor_tensor(
-                page[i][:].indirect(cols(list2, lo, hi)), h[i][:, lo:hi], wg[i % PACK][:, lo:hi], MULT
+                page[i][:].indirect(cols(list2, lo, hi)), row_tile(slots, i, lo, hi), wg[i % PACK][:, lo:hi], MULT
             )
 
-        x = {}
-        d = {}
-
         def gather_page(i, lo, hi):
-            if lo == 0:
-                x[i] = work.tile([P, M], F32, name="x")
-                d[i] = work.tile([P, M], F32, name="d")
-            nc.vector.tensor_copy(x[i][:, lo:hi], page[i][:].indirect(cols(list3, lo, hi)))
-            nc.scalar.activation(d[i][:, lo:hi], x[i][:, lo:hi], ACT.Abs)
-            nc.scalar.activation(d[i][:, lo:hi], d[i][:, lo:hi], ACT.Abs_reciprocal_sqrt, bias=1.0)
-            nc.scalar.activation(d[i][:, lo:hi], d[i][:, lo:hi], ACT.Square)
-
-        def softsign(i, lo, hi):
             b, t = divmod(i, PACK)
-            z = slots_bf[:, 2 * S * (i + 1) + lo : 2 * S * (i + 1) + hi]
-            nc.vector.scalar_tensor_tensor(z, x[i][:, lo:hi], gain_sb[:, b, 2 * t : 2 * t + 1], d[i][:, lo:hi], MULT, MULT)
-
-        def interleave(src, width, on_vector):
-            pool = two if width == HALF else four
-            dst = pool.tile([P, width, PACK], BF16, name="woven", align_bytes=64)
-            move = nc.vector.tensor_copy if on_vector else nc.scalar.copy
-            move(dst[:].rearrange("p (c i) t -> p c t i", i=4), src.rearrange("p t (c i) -> p c t i", i=4))
-            return dst
+            x = row_tile(slots, i, lo, hi)
+            d = row_tile(recip, i, lo, hi)
+            nc.vector.tensor_copy(x, page[i][:].indirect(cols(list3, lo, hi)))
+            nc.scalar.activation(d, x, ACT.Abs)
+            nc.scalar.activation(d, d, ACT.Abs_reciprocal_sqrt, bias=1.0)
+            nc.scalar.activation(d, d, ACT.Square)
+            nc.scalar.activation(x, x, ACT.Copy, scale=gain_sb[:, b, 2 * t : 2 * t + 1])
 
         def quantize(woven, width, name):
             codes = keep.tile([P, width], U32, name=name + "_codes", align_bytes=64)
@@ -216,18 +200,33 @@ def tile_list_seller_trust_cache_kernel(
             return codes, scale
 
         wb_rows = wb.rearrange("(b u t e) n -> b t u e n", b=B, t=PACK, e=2)
+        wb_raw = keep.tile([P, B * PACK * N], F32, name="wb_raw", tag="big0", align_bytes=64)
         wb_q = {}
 
-        def prepare_wb(b):
-            raw = keep.tile([P, PACK * N], F32, name="wb_raw", tag="big%d" % b, align_bytes=64)
+        def load_wb(b):
             for t in range(PACK):
-                nc.sync.dma_start(out=raw[:, t * N : (t + 1) * N], in_=wb_rows[b, t])
-            wb_q[b] = quantize(interleave(raw[:].rearrange("p (t n) -> p t n", t=PACK), N, False), N, "wb%d" % b)
+                nc.sync.dma_start(out=wb_raw[:, (b * PACK + t) * N : (b * PACK + t + 1) * N], in_=wb_rows[b, t])
+
+        def prepare_wb(b):
+            woven = keep.tile([P, N, PACK], BF16, name="wb_woven%d" % b, align_bytes=64)
+            nc.scalar.copy(
+                woven[:].rearrange("p (c i) t -> p c t i", i=4),
+                wb_raw[:, b * PACK * N : (b + 1) * PACK * N].rearrange("p (t c i) -> p c t i", t=PACK, i=4),
+            )
+            wb_q[b] = quantize(woven, N, "wb%d" % b)
 
         z_q = {}
 
-        def weave_z(b, lo, hi, on_vector):
-            return interleave(z_all[:, b * PACK : (b + 1) * PACK, lo:hi], hi - lo, on_vector)
+        def softsign(b, lo, hi, tag):
+            woven = keep.tile([P, hi - lo, PACK], BF16, name="z_woven", tag=tag, align_bytes=64)
+
+            def four_rows(pair):
+                return pair[b][:].rearrange("p (t m) -> p t m", t=PACK)[:, :, lo:hi].rearrange("p t (c i) -> p c t i", i=2)
+
+            nc.vector.tensor_tensor(
+                woven[:].rearrange("p (c i) t -> p c t i", i=2), four_rows(slots), four_rows(recip), MULT
+            )
+            return woven
 
         def quantize_z(b, lo, hi, woven):
             codes, scale = quantize(woven, hi - lo, "z%d_%d" % (b, lo))
@@ -235,65 +234,67 @@ def tile_list_seller_trust_cache_kernel(
                 z_q[b, c // QUARTER] = (codes[:, c - lo : c - lo + QUARTER], scale[:, c - lo : c - lo + QUARTER])
 
         out_rows = out.rearrange("(n p) m -> p n m", p=P)
+        out_acc = {}
 
-        def second_product(quarter, banks):
-            per_bank = N // P // len(banks)
-            for g, number in enumerate(banks):
-                acc = bank(number, "acc_out")
-                for s in range(per_bank):
-                    n = g * per_bank + s
-                    for b in range(B):
-                        nc.tensor.matmul_mx(
-                            out=acc[:, s * QUARTER : (s + 1) * QUARTER],
-                            lhsT=wb_q[b][0][:, n * P : (n + 1) * P].bitcast(FP8X4),
-                            lhsT_scale=wb_q[b][1][:, n * P : (n + 1) * P],
-                            rhs=z_q[b, quarter][0].bitcast(FP8X4),
-                            rhs_scale=z_q[b, quarter][1],
-                            start=(b == 0),
-                            stop=(b == B - 1),
-                        )
-                res = four.tile([P, HALF], F32, name="res")
-                width = per_bank * QUARTER
-                if quarter == 3 and g % 2 == 1:
-                    nc.vector.tensor_copy(res[:, :width], acc[:, :width])
+        def second_product(b, quarter):
+            for g in range(2):
+                if b == 0:
+                    out_acc[quarter, g] = bank(2 * quarter + g, "acc_out")
+                acc = out_acc[quarter, g]
+                for s in range(2):
+                    n = 2 * g + s
+                    nc.tensor.matmul_mx(
+                        out=acc[:, s * QUARTER : (s + 1) * QUARTER],
+                        lhsT=wb_q[b][0][:, n * P : (n + 1) * P].bitcast(FP8X4),
+                        lhsT_scale=wb_q[b][1][:, n * P : (n + 1) * P],
+                        rhs=z_q[b, quarter][0].bitcast(FP8X4),
+                        rhs_scale=z_q[b, quarter][1],
+                        start=(b == 0 and s == 0),
+                        stop=(b == B - 1 and s == 1),
+                    )
+
+        def store(quarter):
+            for g in range(2):
+                res = keep.tile([P, HALF], F32, name="res%d_%d" % (quarter, g))
+                if quarter == 3 and g == 1:
+                    nc.vector.tensor_copy(res[:], out_acc[quarter, g][:])
                 else:
-                    nc.scalar.copy(res[:, :width], acc[:, :width])
+                    nc.scalar.copy(res[:], out_acc[quarter, g][:])
                 nc.sync.dma_start(
-                    out=out_rows[:, g * per_bank : (g + 1) * per_bank, quarter * QUARTER : (quarter + 1) * QUARTER],
-                    in_=res[:, :width].rearrange("p (s w) -> p s w", s=per_bank),
+                    out=out_rows[:, 2 * g : 2 * g + 2, quarter * QUARTER : (quarter + 1) * QUARTER],
+                    in_=res[:].rearrange("p (s w) -> p s w", s=2),
                 )
 
-        first_product(0)
-        first_product(1)
+        for i in range(PACK):
+            first_product(i)
         scatter(0, 0, HALF)
         scatter(0, HALF, S)
-        gather_page(0, 0, M)
         permute_w_codes(1)
+        for i in range(PACK, tiles):
+            first_product(i)
+        for b in range(B):
+            load_wb(b)
+        gather_page(0, 0, M)
         for i in range(1, tiles):
-            if i + 1 < tiles:
-                first_product(i + 1)
-            if i + 3 < tiles:
-                load_page(i + 3)
+            if i + PAGE_BUFS - 1 < tiles:
+                load_page(i + PAGE_BUFS - 1)
             scatter(i, 0, S)
+            if i in (4, 5):
+                lo = (i - 4) * HALF
+                woven = softsign(0, lo, lo + HALF, "wg%d" % (i - 4))
             if i < last:
-                softsign(i - 1, 0, M)
                 gather_page(i, 0, M)
+            if i in (4, 5):
+                quantize_z(0, lo, lo + HALF, woven)
+                second_product(0, 2 * (i - 4))
+                second_product(0, 2 * (i - 4) + 1)
             if i in (2, 3):
                 prepare_wb(i - 2)
-            if i in (5, 6):
-                lo = (i - 5) * HALF
-                quantize_z(0, lo, lo + HALF, weave_z(0, lo, lo + HALF, False))
 
         for quarter in range(4):
             gather_page(last, quarter * QUARTER, (quarter + 1) * QUARTER)
-        softsign(last - 1, 0, M)
-        quarter_banks = [(0, 1), (2, 3), (0, 1), (4, 5, 6, 7)]
-        woven = {}
         for quarter in range(4):
             lo, hi = quarter * QUARTER, (quarter + 1) * QUARTER
-            softsign(last, lo, hi)
-            woven[quarter] = weave_z(1, lo, hi, quarter % 2 == 0)
-        for quarter in range(4):
-            lo, hi = quarter * QUARTER, (quarter + 1) * QUARTER
-            quantize_z(1, lo, hi, woven[quarter])
-            second_product(quarter, quarter_banks[quarter])
+            quantize_z(1, lo, hi, softsign(1, lo, hi, "z_tail%d" % quarter))
+            second_product(1, quarter)
+            store(quarter)

@@ -34,6 +34,7 @@ def tile_list_seller_trust_cache_kernel(
     with ExitStack() as ctx:
         keep = ctx.enter_context(tc.tile_pool(name="keep", bufs=1))
         pages = ctx.enter_context(tc.tile_pool(name="pages", bufs=PAGE_BUFS))
+        work = ctx.enter_context(tc.tile_pool(name="work", bufs=2))
         psum = ctx.enter_context(tc.psum_pool(name="psum", bufs=1))
 
         list1 = keep.tile([P, S // STRIPE], U16, name="list1")
@@ -98,10 +99,10 @@ def tile_list_seller_trust_cache_kernel(
         load_page(0)
         load_wg(0, 0, HALF)
         load_wg(0, HALF, S)
-        nc.sync.dma_start(list3[:], offs3)
-        load_w(1)
         load_page(1)
         load_wg(1, 0, S)
+        nc.sync.dma_start(list3[:], offs3)
+        load_w(1)
         for e in range(2):
             nc.sync.dma_start(out=gain_sb[e:P:2, :, 0 : 2 * PACK - 1], in_=gain_rows[:, :, e : e + 2 * PACK - 1])
         load_page(2)
@@ -154,11 +155,18 @@ def tile_list_seller_trust_cache_kernel(
         tiles = B * PACK
         last = tiles - 1
         slots = [keep.tile([P, PACK * S], F32, name="slots%d" % b, align_bytes=64) for b in range(B)]
-        recip = [keep.tile([P, PACK * M], F32, name="recip%d" % b, tag="big%d" % (b + 1), align_bytes=64) for b in range(B)]
+        pieces = [(0, 256), (256, 512), (512, 768), (768, 896), (896, 1024)]
+        recip_pieces = [[(0, M)], pieces]
+        recip = {(0, 0): keep.tile([P, PACK * M], F32, name="recip0", tag="big1", align_bytes=64)}
+        for lo, hi in pieces:
+            recip[1, lo] = keep.tile([P, PACK * (hi - lo)], F32, name="recip1", tag="recip1_%d" % lo, align_bytes=64)
 
         def row_tile(pair, i, lo, hi):
             b, t = divmod(i, PACK)
             return pair[b][:, t * S + lo : t * S + hi]
+
+        def h_slot(i):
+            return i ^ 1 if i < last - 1 else i
 
         def first_product(i):
             b, t = divmod(i, PACK)
@@ -174,28 +182,48 @@ def tile_list_seller_trust_cache_kernel(
                         start=(a == 0),
                         stop=(a == A - 1),
                     )
-                nc.scalar.copy(row_tile(slots, i, half * HALF, (half + 1) * HALF), acc[:])
+                nc.scalar.copy(row_tile(slots, h_slot(i), half * HALF, (half + 1) * HALF), acc[:])
 
         def scatter(i, lo, hi):
             nc.vector.tensor_tensor(
-                page[i][:].indirect(cols(list2, lo, hi)), row_tile(slots, i, lo, hi), wg[i % PACK][:, lo:hi], MULT
+                page[i][:].indirect(cols(list2, lo, hi)),
+                row_tile(slots, h_slot(i), lo, hi),
+                wg[i % PACK][:, lo:hi],
+                MULT,
             )
+
+        gain_root = keep.tile([P, B, PACK], F32, name="gain_root")
+        gain_sign = keep.tile([P, B, PACK], F32, name="gain_sign")
+
+        def split_gain():
+            rows = gain_sb[:, :, 0 : 2 * PACK : 2]
+            nc.scalar.activation(gain_root[:], rows, ACT.Abs)
+            nc.scalar.activation(gain_root[:], gain_root[:], ACT.Sqrt)
+            nc.scalar.activation(gain_sign[:], rows, ACT.Sign)
+            nc.scalar.activation(gain_sign[:], gain_sign[:], ACT.Sign, bias=0.5)
 
         def gather_page(i, lo, hi):
             b, t = divmod(i, PACK)
             x = row_tile(slots, i, lo, hi)
-            d = row_tile(recip, i, lo, hi)
+            root = work.tile([P, hi - lo], F32, name="root")
             nc.vector.tensor_copy(x, page[i][:].indirect(cols(list3, lo, hi)))
-            nc.scalar.activation(d, x, ACT.Abs)
-            nc.scalar.activation(d, d, ACT.Abs_reciprocal_sqrt, bias=1.0)
-            nc.scalar.activation(d, d, ACT.Square)
-            nc.scalar.activation(x, x, ACT.Copy, scale=gain_sb[:, b, 2 * t : 2 * t + 1])
+            nc.scalar.activation(root[:], x, ACT.Abs)
+            nc.scalar.activation(root[:], root[:], ACT.Abs_reciprocal_sqrt, bias=1.0)
+            for first, end in recip_pieces[b]:
+                if lo <= first and end <= hi:
+                    width = end - first
+                    nc.scalar.activation(
+                        recip[b, first][:, t * width : (t + 1) * width],
+                        root[:, first - lo : end - lo],
+                        ACT.Square,
+                        scale=gain_root[:, b, t : t + 1],
+                    )
 
-        def quantize(woven, width, name):
-            codes = keep.tile([P, width], U32, name=name + "_codes", align_bytes=64)
+        def quantize(woven, width, name, tag=None):
+            codes = keep.tile([P, width], U32, name=name + "_codes", tag=tag or name, align_bytes=64)
             scale = keep.tile([P, width], U8, name=name + "_scale", align_bytes=64)
             nc.vector.quantize_mx(
-                out=codes[:].bitcast(FP8X4), scales=scale[:], in_=woven[:].rearrange("p w t -> p (w t)")
+                out=codes[:].bitcast(FP8X4), scales=scale[:], in_=woven.rearrange("p w t -> p (w t)")
             )
             return codes, scale
 
@@ -208,93 +236,120 @@ def tile_list_seller_trust_cache_kernel(
                 nc.sync.dma_start(out=wb_raw[:, (b * PACK + t) * N : (b * PACK + t + 1) * N], in_=wb_rows[b, t])
 
         def prepare_wb(b):
+            for t in range(PACK):
+                rows = wb_raw[:, (b * PACK + t) * N : (b * PACK + t + 1) * N]
+                nc.scalar.activation(rows, rows, ACT.Copy, scale=gain_sign[:, b, t : t + 1])
             woven = keep.tile([P, N, PACK], BF16, name="wb_woven%d" % b, align_bytes=64)
             nc.scalar.copy(
                 woven[:].rearrange("p (c i) t -> p c t i", i=4),
                 wb_raw[:, b * PACK * N : (b + 1) * PACK * N].rearrange("p (t c i) -> p c t i", t=PACK, i=4),
             )
-            wb_q[b] = quantize(woven, N, "wb%d" % b)
+            wb_q[b] = quantize(woven[:], N, "wb%d" % b)
 
         z_q = {}
 
         def softsign(b, lo, hi, tag):
             woven = keep.tile([P, hi - lo, PACK], BF16, name="z_woven", tag=tag, align_bytes=64)
 
-            def four_rows(pair):
-                return pair[b][:].rearrange("p (t m) -> p t m", t=PACK)[:, :, lo:hi].rearrange("p t (c i) -> p c t i", i=2)
+            def four_rows(tile, first, end):
+                return tile[:].rearrange("p (t m) -> p t m", t=PACK)[:, :, first:end].rearrange("p t (c i) -> p c t i", i=2)
 
+            d = four_rows(recip[0, 0], lo, hi) if b == 0 else four_rows(recip[1, lo], 0, hi - lo)
             nc.vector.tensor_tensor(
-                woven[:].rearrange("p (c i) t -> p c t i", i=2), four_rows(slots), four_rows(recip), MULT
+                woven[:].rearrange("p (c i) t -> p c t i", i=2), four_rows(slots[b], lo, hi), d, MULT
             )
             return woven
 
-        def quantize_z(b, lo, hi, woven):
-            codes, scale = quantize(woven, hi - lo, "z%d_%d" % (b, lo))
-            for c in range(lo, hi, QUARTER):
-                z_q[b, c // QUARTER] = (codes[:, c - lo : c - lo + QUARTER], scale[:, c - lo : c - lo + QUARTER])
+        def quantize_z(b, lo, hi, woven, tag=None):
+            codes, scale = quantize(woven, hi - lo, "z%d_%d" % (b, lo), tag)
+            for first, end in pieces:
+                if lo <= first and end <= hi:
+                    z_q[b, first] = (codes[:, first - lo : end - lo], scale[:, first - lo : end - lo])
 
         out_rows = out.rearrange("(n p) m -> p n m", p=P)
         out_acc = {}
+        staged = keep.tile([P, 8 * HALF], F32, name="staged", tag="big2", align_bytes=64)
 
-        def second_product(b, quarter):
-            for g in range(2):
+        def banks_of(lo, hi):
+            per_bank = HALF // (hi - lo)
+            return [(lo // P + g, range(g * per_bank, (g + 1) * per_bank)) for g in range(N // P // per_bank)]
+
+        def second_product(b, lo, hi):
+            width = hi - lo
+            for number, blocks in banks_of(lo, hi):
                 if b == 0:
-                    out_acc[quarter, g] = bank(2 * quarter + g, "acc_out")
-                acc = out_acc[quarter, g]
-                for s in range(2):
-                    n = 2 * g + s
+                    out_acc[number] = bank(number, "acc_out")
+                for s, n in enumerate(blocks):
                     nc.tensor.matmul_mx(
-                        out=acc[:, s * QUARTER : (s + 1) * QUARTER],
+                        out=out_acc[number][:, s * width : (s + 1) * width],
                         lhsT=wb_q[b][0][:, n * P : (n + 1) * P].bitcast(FP8X4),
                         lhsT_scale=wb_q[b][1][:, n * P : (n + 1) * P],
-                        rhs=z_q[b, quarter][0].bitcast(FP8X4),
-                        rhs_scale=z_q[b, quarter][1],
+                        rhs=z_q[b, lo][0].bitcast(FP8X4),
+                        rhs_scale=z_q[b, lo][1],
                         start=(b == 0 and s == 0),
-                        stop=(b == B - 1 and s == 1),
+                        stop=(b == B - 1 and n == blocks[-1]),
                     )
 
-        def store(quarter):
-            for g in range(2):
-                res = keep.tile([P, HALF], F32, name="res%d_%d" % (quarter, g))
-                if quarter == 3 and g == 1:
-                    nc.vector.tensor_copy(res[:], out_acc[quarter, g][:])
+        def store(lo, hi):
+            for number, blocks in banks_of(lo, hi):
+                res = staged[:, number * HALF : (number + 1) * HALF]
+                if number in (5, 7):
+                    nc.vector.tensor_copy(res, out_acc[number][:])
                 else:
-                    nc.scalar.copy(res[:], out_acc[quarter, g][:])
-                nc.sync.dma_start(
-                    out=out_rows[:, 2 * g : 2 * g + 2, quarter * QUARTER : (quarter + 1) * QUARTER],
-                    in_=res[:].rearrange("p (s w) -> p s w", s=2),
+                    nc.scalar.copy(res, out_acc[number][:])
+                queue = nc.scalar if number == 6 else nc.sync
+                queue.dma_start(
+                    out=out_rows[:, blocks[0] : blocks[-1] + 1, lo:hi],
+                    in_=res.rearrange("p (s w) -> p s w", s=len(blocks)),
                 )
 
         for i in range(PACK):
             first_product(i)
         scatter(0, 0, HALF)
         scatter(0, HALF, S)
+        scatter(1, 0, S)
         permute_w_codes(1)
         for i in range(PACK, tiles):
             first_product(i)
         for b in range(B):
             load_wb(b)
+        split_gain()
         gather_page(0, 0, M)
-        for i in range(1, tiles):
-            if i + PAGE_BUFS - 1 < tiles:
-                load_page(i + PAGE_BUFS - 1)
+        gather_page(1, 0, M)
+        for i in (2, 4):
+            load_page(i + 2)
+            load_page(i + 3)
             scatter(i, 0, S)
-            if i in (4, 5):
-                lo = (i - 4) * HALF
-                woven = softsign(0, lo, lo + HALF, "wg%d" % (i - 4))
-            if i < last:
-                gather_page(i, 0, M)
-            if i in (4, 5):
-                quantize_z(0, lo, lo + HALF, woven)
-                second_product(0, 2 * (i - 4))
-                second_product(0, 2 * (i - 4) + 1)
-            if i in (2, 3):
-                prepare_wb(i - 2)
+            scatter(i + 1, 0, S)
+            gather_page(i, 0, M)
+            gather_page(i + 1, 0, M)
+            prepare_wb(i // 2 - 1)
 
+        def finish(b, lo, hi, woven, tag):
+            quantize_z(b, lo, hi, woven, tag=tag)
+            for first, end in pieces:
+                if lo <= first and end <= hi:
+                    second_product(b, first, end)
+                    if b == B - 1:
+                        store(first, end)
+
+        scatter(last - 1, 0, S)
+        early = [softsign(0, 0, HALF, "wg2")]
+        gather_page(last - 1, 0, M)
+        early.append(softsign(0, HALF, M, "wg1"))
+        scatter(last, 0, S)
+        finish(0, 0, HALF, early[0][:], "wg3")
         for quarter in range(4):
             gather_page(last, quarter * QUARTER, (quarter + 1) * QUARTER)
-        for quarter in range(4):
-            lo, hi = quarter * QUARTER, (quarter + 1) * QUARTER
-            quantize_z(1, lo, hi, softsign(1, lo, hi, "z_tail%d" % quarter))
-            second_product(1, quarter)
-            store(quarter)
+
+        for lo, hi in pieces[:2]:
+            woven = softsign(1, lo, hi, "z_tail%d" % lo)
+            finish(0, HALF + lo, HALF + hi, early[1][:, lo:hi, :], "recip1_%d" % lo)
+            finish(1, lo, hi, woven[:], None)
+        waiting = None
+        for lo, hi in pieces[2:]:
+            woven = softsign(1, lo, hi, "z_tail%d" % lo)
+            if waiting:
+                finish(*waiting, "recip1_%d" % lo)
+            waiting = (1, lo, hi, woven[:])
+        finish(*waiting, None)

@@ -34,7 +34,7 @@ def tile_list_seller_trust_cache_kernel(
     with ExitStack() as ctx:
         keep = ctx.enter_context(tc.tile_pool(name="keep", bufs=1))
         pages = ctx.enter_context(tc.tile_pool(name="pages", bufs=PAGE_BUFS))
-        work = ctx.enter_context(tc.tile_pool(name="work", bufs=2))
+        work = ctx.enter_context(tc.tile_pool(name="work", bufs=1))
         psum = ctx.enter_context(tc.psum_pool(name="psum", bufs=1))
 
         list1 = keep.tile([P, S // STRIPE], U16, name="list1")
@@ -105,10 +105,10 @@ def tile_list_seller_trust_cache_kernel(
         load_w(1)
         for e in range(2):
             nc.sync.dma_start(out=gain_sb[e:P:2, :, 0 : 2 * PACK - 1], in_=gain_rows[:, :, e : e + 2 * PACK - 1])
-        load_page(2)
-        load_wg(2, 0, S)
         load_page(3)
         load_wg(3, 0, S)
+        load_page(2)
+        load_wg(2, 0, S)
 
         nc.vector.tensor_copy(v_scale[0][:], tab_scale_win[:].indirect(list1[:]))
         for a in range(1, A):
@@ -154,7 +154,9 @@ def tile_list_seller_trust_cache_kernel(
 
         tiles = B * PACK
         last = tiles - 1
-        slots = [keep.tile([P, PACK * S], F32, name="slots%d" % b, align_bytes=64) for b in range(B)]
+        arena = keep.tile([P, (tiles + 1) * S], F32, name="arena", align_bytes=64)
+        slots = [arena[:, 0 : PACK * S], arena[:, (PACK + 1) * S :]]
+        flat_z = arena[:, PACK * S : (PACK + 1) * S].bitcast(BF16).rearrange("p (t m) -> p t m", t=PACK)
         pieces = [(0, 256), (256, 512), (512, 768), (768, 896), (896, 1024)]
         recip_pieces = [[(0, M)], pieces]
         recip = {(0, 0): keep.tile([P, PACK * M], F32, name="recip0", tag="big1", align_bytes=64)}
@@ -165,29 +167,32 @@ def tile_list_seller_trust_cache_kernel(
             b, t = divmod(i, PACK)
             return pair[b][:, t * S + lo : t * S + hi]
 
-        def h_slot(i):
-            return i ^ 1 if i < last - 1 else i
+        h_start = [S, 0, PACK * S - HALF, 2 * S, 6 * S, (PACK + 1) * S - HALF, 7 * S, 8 * S]
+
+        def h_tile(i, lo, hi):
+            return arena[:, h_start[i] + lo : h_start[i] + hi]
 
         def first_product(i):
             b, t = divmod(i, PACK)
             for half in range(2):
-                acc = bank(half, "acc_h")
-                for a in range(A):
+                acc = bank((2 * i + half) % 8, "acc_h")
+                order = list(range(A)) if i == 0 else [A - 1] + list(range(A - 1))
+                for a in order:
                     nc.tensor.matmul_mx(
                         out=acc[:],
                         lhsT=w_codes[b][:, a, t, :].bitcast(FP4X4),
                         lhsT_scale=w_scale[b][:, a, t, :],
                         rhs=v_codes[a, half].bitcast(FP8X4),
                         rhs_scale=v_scale[a][:, half * HALF : (half + 1) * HALF],
-                        start=(a == 0),
-                        stop=(a == A - 1),
+                        start=(a == order[0]),
+                        stop=(a == order[-1]),
                     )
-                nc.scalar.copy(row_tile(slots, h_slot(i), half * HALF, (half + 1) * HALF), acc[:])
+                nc.scalar.copy(h_tile(i, half * HALF, (half + 1) * HALF), acc[:])
 
         def scatter(i, lo, hi):
             nc.vector.tensor_tensor(
                 page[i][:].indirect(cols(list2, lo, hi)),
-                row_tile(slots, h_slot(i), lo, hi),
+                h_tile(i, lo, hi),
                 wg[i % PACK][:, lo:hi],
                 MULT,
             )
@@ -202,13 +207,17 @@ def tile_list_seller_trust_cache_kernel(
             nc.scalar.activation(gain_sign[:], rows, ACT.Sign)
             nc.scalar.activation(gain_sign[:], gain_sign[:], ACT.Sign, bias=0.5)
 
+        roots = {}
+
         def gather_page(i, lo, hi):
             b, t = divmod(i, PACK)
             x = row_tile(slots, i, lo, hi)
-            root = work.tile([P, hi - lo], F32, name="root")
+            if lo == 0:
+                roots[i] = work.tile([P, M], F32, name="root")
+            root = roots[i][:, lo:hi]
             nc.vector.tensor_copy(x, page[i][:].indirect(cols(list3, lo, hi)))
-            nc.scalar.activation(root[:], x, ACT.Abs)
-            nc.scalar.activation(root[:], root[:], ACT.Abs_reciprocal_sqrt, bias=1.0)
+            nc.scalar.activation(root, x, ACT.Abs)
+            nc.scalar.activation(root, root, ACT.Abs_reciprocal_sqrt, bias=1.0)
             for first, end in recip_pieces[b]:
                 if lo <= first and end <= hi:
                     width = end - first
@@ -244,7 +253,7 @@ def tile_list_seller_trust_cache_kernel(
                 woven[:].rearrange("p (c i) t -> p c t i", i=4),
                 wb_raw[:, b * PACK * N : (b + 1) * PACK * N].rearrange("p (t c i) -> p c t i", t=PACK, i=4),
             )
-            wb_q[b] = quantize(woven[:], N, "wb%d" % b)
+            wb_q[b] = woven
 
         z_q = {}
 
@@ -252,11 +261,26 @@ def tile_list_seller_trust_cache_kernel(
             woven = keep.tile([P, hi - lo, PACK], BF16, name="z_woven", tag=tag, align_bytes=64)
 
             def four_rows(tile, first, end):
-                return tile[:].rearrange("p (t m) -> p t m", t=PACK)[:, :, first:end].rearrange("p t (c i) -> p c t i", i=2)
+                return tile.rearrange("p (t m) -> p t m", t=PACK)[:, :, first:end].rearrange("p t (c i) -> p c t i", i=2)
 
-            d = four_rows(recip[0, 0], lo, hi) if b == 0 else four_rows(recip[1, lo], 0, hi - lo)
+            d = four_rows(recip[0, 0][:], lo, hi) if b == 0 else four_rows(recip[1, lo][:], 0, hi - lo)
             nc.vector.tensor_tensor(
                 woven[:].rearrange("p (c i) t -> p c t i", i=2), four_rows(slots[b], lo, hi), d, MULT
+            )
+            return woven
+
+        def softsign_pair(t):
+            nc.gpsimd.tensor_tensor(
+                flat_z[:, t : t + 2, :],
+                slots[0].rearrange("p (t m) -> p t m", t=PACK)[:, t : t + 2, HALF:M],
+                recip[0, 0][:].rearrange("p (t m) -> p t m", t=PACK)[:, t : t + 2, HALF:M],
+                MULT,
+            )
+
+        def weave_pairs():
+            woven = keep.tile([P, HALF, PACK], BF16, name="late_woven", align_bytes=64)
+            nc.scalar.copy(
+                woven[:].rearrange("p (c i) t -> p c t i", i=4), flat_z.rearrange("p t (c i) -> p c t i", i=4)
             )
             return woven
 
@@ -303,7 +327,7 @@ def tile_list_seller_trust_cache_kernel(
                     in_=res.rearrange("p (s w) -> p s w", s=len(blocks)),
                 )
 
-        for i in range(PACK):
+        for i in (0, 1, 3, 2):
             first_product(i)
         scatter(0, 0, HALF)
         scatter(0, HALF, S)
@@ -316,14 +340,20 @@ def tile_list_seller_trust_cache_kernel(
         split_gain()
         gather_page(0, 0, M)
         gather_page(1, 0, M)
-        for i in (2, 4):
-            load_page(i + 2)
-            load_page(i + 3)
-            scatter(i, 0, S)
-            scatter(i + 1, 0, S)
-            gather_page(i, 0, M)
-            gather_page(i + 1, 0, M)
-            prepare_wb(i // 2 - 1)
+        prepare_wb(0)
+        for k, (first, second) in enumerate([(3, 2), (4, 5)]):
+            load_page(4 + 2 * k)
+            load_page(5 + 2 * k)
+            scatter(first, 0, S)
+            if k == 1:
+                wb_q[0] = quantize(wb_q[0][:], N, "wb0", "wg0")
+            scatter(second, 0, S)
+            softsign_pair(2 * k)
+            gather_page(first, 0, M)
+            gather_page(second, 0, M)
+            if k == 0:
+                prepare_wb(1)
+        late = weave_pairs()
 
         def finish(b, lo, hi, woven, tag):
             quantize_z(b, lo, hi, woven, tag=tag)
@@ -333,10 +363,11 @@ def tile_list_seller_trust_cache_kernel(
                     if b == B - 1:
                         store(first, end)
 
+        early = [softsign(0, 0, HALF, "wg1")]
         scatter(last - 1, 0, S)
-        early = [softsign(0, 0, HALF, "wg2")]
+        wb_q[1] = quantize(wb_q[1][:], N, "wb1", "wg2")
         gather_page(last - 1, 0, M)
-        early.append(softsign(0, HALF, M, "wg1"))
+        early.append(late)
         scatter(last, 0, S)
         finish(0, 0, HALF, early[0][:], "wg3")
         for quarter in range(4):

@@ -25,6 +25,7 @@ HALF = 512
 QUARTER = 256
 STRIPE = 16
 PAGE_BUFS = 4
+PAIR_COLS = 832
 
 
 def tile_list_seller_trust_cache_kernel(
@@ -116,11 +117,13 @@ def tile_list_seller_trust_cache_kernel(
                 out=v_scale[a][0:112, :].bitcast(I32), in_=v_scale[0][4 * a : 4 * a + 112, :].bitcast(I32)
             )
 
-        w_codes = [keep.tile([P, A, PACK, 2 * P], U8, name="w_codes%d" % b, align_bytes=64) for b in range(B)]
+        w_codes = {}
         w_scale = [keep.tile([P, A, PACK, P], U8, name="w_scale%d" % b, align_bytes=64) for b in range(B)]
 
         def permute_w_codes(b):
-            nc.vector.tensor_copy(
+            w_codes[b] = keep.tile([P, A, PACK, 2 * P], U8, name="w_codes", tag="w_codes%d" % b, align_bytes=64)
+            engine = nc.vector if b == 0 else nc.gpsimd
+            engine.tensor_copy(
                 w_codes[b][:].bitcast(I32).rearrange("p a t (c i) -> p a c t i", i=4),
                 w_raw[b][:].rearrange("p a (c i t) -> p a c t i", i=4, t=PACK),
             )
@@ -154,9 +157,11 @@ def tile_list_seller_trust_cache_kernel(
 
         tiles = B * PACK
         last = tiles - 1
-        arena = keep.tile([P, (tiles + 1) * S], F32, name="arena", align_bytes=64)
-        slots = [arena[:, 0 : PACK * S], arena[:, (PACK + 1) * S :]]
-        flat_z = arena[:, PACK * S : (PACK + 1) * S].bitcast(BF16).rearrange("p (t m) -> p t m", t=PACK)
+        arena = keep.tile([P, (tiles + 3) * S], F32, name="arena", align_bytes=64)
+        slots = [arena[:, 0 : 4 * S], arena[:, 6 * S : 10 * S]]
+        flat_z = arena[:, 4 * S : 6 * S].bitcast(BF16).rearrange("p (t m) -> p t m", t=PACK)
+        rest = M - PAIR_COLS
+        flat_rest = arena[:, 10 * S : 10 * S + 2 * rest].bitcast(BF16).rearrange("p (t m) -> p t m", t=PACK)
         pieces = [(0, 256), (256, 512), (512, 768), (768, 896), (896, 1024)]
         recip_pieces = [[(0, M)], pieces]
         recip = {(0, 0): keep.tile([P, PACK * M], F32, name="recip0", tag="big1", align_bytes=64)}
@@ -167,9 +172,13 @@ def tile_list_seller_trust_cache_kernel(
             b, t = divmod(i, PACK)
             return pair[b][:, t * S + lo : t * S + hi]
 
-        h_start = [S, 0, PACK * S - HALF, 2 * S, 6 * S, (PACK + 1) * S - HALF, 7 * S, 8 * S]
+        h_start = [S, 0, 4 * S - HALF, 2 * S, 7 * S, 6 * S - HALF, 10 * S, 9 * S]
+
+        h_first = keep.tile([P, S], F32, name="h_first", tag="w_codes1", align_bytes=64)
 
         def h_tile(i, lo, hi):
+            if i == 0:
+                return h_first[:, lo:hi]
             return arena[:, h_start[i] + lo : h_start[i] + hi]
 
         def first_product(i):
@@ -269,20 +278,16 @@ def tile_list_seller_trust_cache_kernel(
             )
             return woven
 
-        def softsign_pair(t):
+        def softsign_flat(dst, t, count, lo, hi):
             nc.gpsimd.tensor_tensor(
-                flat_z[:, t : t + 2, :],
-                slots[0].rearrange("p (t m) -> p t m", t=PACK)[:, t : t + 2, HALF:M],
-                recip[0, 0][:].rearrange("p (t m) -> p t m", t=PACK)[:, t : t + 2, HALF:M],
+                dst,
+                slots[0].rearrange("p (t m) -> p t m", t=PACK)[:, t : t + count, lo:hi],
+                recip[0, 0][:].rearrange("p (t m) -> p t m", t=PACK)[:, t : t + count, lo:hi],
                 MULT,
             )
 
-        def weave_pairs():
-            woven = keep.tile([P, HALF, PACK], BF16, name="late_woven", align_bytes=64)
-            nc.scalar.copy(
-                woven[:].rearrange("p (c i) t -> p c t i", i=4), flat_z.rearrange("p t (c i) -> p c t i", i=4)
-            )
-            return woven
+        def weave(dst, src):
+            nc.scalar.copy(dst.rearrange("p (c i) t -> p c t i", i=4), src.rearrange("p t (c i) -> p c t i", i=4))
 
         def quantize_z(b, lo, hi, woven, tag=None):
             codes, scale = quantize(woven, hi - lo, "z%d_%d" % (b, lo), tag)
@@ -348,12 +353,14 @@ def tile_list_seller_trust_cache_kernel(
             if k == 1:
                 wb_q[0] = quantize(wb_q[0][:], N, "wb0", "wg0")
             scatter(second, 0, S)
-            softsign_pair(2 * k)
+            softsign_flat(flat_z[:, 2 * k : 2 * k + 2, 0:PAIR_COLS], 2 * k, 2, 0, PAIR_COLS)
             gather_page(first, 0, M)
             gather_page(second, 0, M)
             if k == 0:
                 prepare_wb(1)
-        late = weave_pairs()
+        early = [keep.tile([P, HALF, PACK], BF16, name="early%d" % half, align_bytes=64) for half in range(2)]
+        weave(early[0][:], flat_z[:, :, 0:HALF])
+        weave(early[1][:, 0 : PAIR_COLS - HALF, :], flat_z[:, :, HALF:PAIR_COLS])
 
         def finish(b, lo, hi, woven, tag):
             quantize_z(b, lo, hi, woven, tag=tag)
@@ -363,11 +370,11 @@ def tile_list_seller_trust_cache_kernel(
                     if b == B - 1:
                         store(first, end)
 
-        early = [softsign(0, 0, HALF, "wg1")]
         scatter(last - 1, 0, S)
         wb_q[1] = quantize(wb_q[1][:], N, "wb1", "wg2")
+        softsign_flat(flat_rest, 0, PACK, PAIR_COLS, M)
         gather_page(last - 1, 0, M)
-        early.append(late)
+        weave(early[1][:, PAIR_COLS - HALF :, :], flat_rest)
         scatter(last, 0, S)
         finish(0, 0, HALF, early[0][:], "wg3")
         for quarter in range(4):

@@ -17,15 +17,28 @@ MULT = mybir.AluOpType.mult
 ACT = mybir.ActivationFunctionType
 
 P = 128
+QUAD = 32
 PACK = 4
 PASS = P * PACK
 A = K // PASS
 B = H // PASS
+TILES = B * PACK
+LAST = TILES - 1
+BANKS = 8
 HALF = 512
 QUARTER = 256
 STRIPE = 16
 PAGE_BUFS = 4
 PAIR_COLS = 832
+PIECES = [(0, 256), (256, 512), (512, 768), (768, 896), (896, 1024)]
+
+
+def pieces_in(lo, hi):
+    return [(first, end) for first, end in PIECES if lo <= first and end <= hi]
+
+
+def by_tile(ap):
+    return ap.rearrange("p (t m) -> p t m", t=PACK)
 
 
 def tile_list_seller_trust_cache_kernel(
@@ -42,7 +55,7 @@ def tile_list_seller_trust_cache_kernel(
         list2 = keep.tile([P, S // STRIPE], U16, name="list2")
         list3 = keep.tile([P, M // STRIPE], U16, name="list3")
 
-        def cols(lst, lo, hi):
+        def entries(lst, lo, hi):
             return lst[:, lo // STRIPE : hi // STRIPE]
 
         tab_scale_win = keep.tile([P, T], U8, name="tab_scale_win", align_bytes=64)
@@ -58,18 +71,19 @@ def tile_list_seller_trust_cache_kernel(
         def load_tab(a):
             nc.sync.dma_start(out=tab[a][:], in_=tab_words[a].rearrange("p n t -> p (n t)").bitcast(I32))
 
-        w_raw = [keep.tile([P, A, PASS // 2], I32, name="w_raw%d" % b, align_bytes=64) for b in range(B)]
+        pairs = PASS // 2
+        w_raw = [keep.tile([P, A, pairs], I32, name="w_raw%d" % b, align_bytes=64) for b in range(B)]
         w_words_i32 = w4_words.rearrange("a p n -> p a n").bitcast(I32)
 
         def load_w(b):
-            nc.sync.dma_start(out=w_raw[b][:], in_=w_words_i32[:, :, b * 256 : (b + 1) * 256])
+            nc.sync.dma_start(out=w_raw[b][:], in_=w_words_i32[:, :, b * pairs : (b + 1) * pairs])
 
         wg = [keep.tile([P, S], F32, name="wg%d" % t, tag="wg%d" % t, align_bytes=64) for t in range(PACK)]
         wgs_rows = wgs.rearrange("(u t e) j -> t u e j", t=PACK, e=2)
 
         def load_wg(t, lo, hi):
             for q in (0, 2, 1, 3):
-                nc.sync.dma_start(out=wg[t][32 * q : 32 * q + 32, lo:hi], in_=wgs_rows[t][:, :, lo:hi])
+                nc.sync.dma_start(out=wg[t][QUAD * q : QUAD * (q + 1), lo:hi], in_=wgs_rows[t][:, :, lo:hi])
 
         page_rows = page0.rearrange("(b u t e) c -> b t u e c", b=B, t=PACK, e=2)
         page = {}
@@ -85,14 +99,14 @@ def tile_list_seller_trust_cache_kernel(
         nc.sync.dma_start(list1[:], offs)
         for q in range(4):
             nc.sync.dma_start(
-                out=tab_scale_win[32 * q : 32 * q + 4 * A, :].bitcast(I32),
+                out=tab_scale_win[QUAD * q : QUAD * q + 4 * A, :].bitcast(I32),
                 in_=tab_scales[:, 4 * q : 4 * q + 4, :].bitcast(I32),
             )
         load_w(0)
         load_tab(1)
         for q in range(4):
             nc.sync.dma_start(
-                out=w_scale_raw[32 * q : 32 * q + 4, :, :].bitcast(I32),
+                out=w_scale_raw[QUAD * q : QUAD * q + 4, :, :].bitcast(I32),
                 in_=w4_scales[:, 4 * q : 4 * q + 4, :].rearrange("a r n -> r a n").bitcast(I32),
             )
         nc.sync.dma_start(list2[:], offs2)
@@ -120,15 +134,14 @@ def tile_list_seller_trust_cache_kernel(
         w_codes = {}
         w_scale = [keep.tile([P, A, PACK, P], U8, name="w_scale%d" % b, align_bytes=64) for b in range(B)]
 
-        def permute_w_codes(b):
+        def order_w_codes(b, engine):
             w_codes[b] = keep.tile([P, A, PACK, 2 * P], U8, name="w_codes", tag="w_codes%d" % b, align_bytes=64)
-            engine = nc.vector if b == 0 else nc.gpsimd
             engine.tensor_copy(
                 w_codes[b][:].bitcast(I32).rearrange("p a t (c i) -> p a c t i", i=4),
                 w_raw[b][:].rearrange("p a (c i t) -> p a c t i", i=4, t=PACK),
             )
 
-        def permute_w_scale(b):
+        def order_w_scale(b):
             nc.vector.tensor_copy(
                 w_scale[b][:].bitcast(U16).rearrange("p a t (c i) -> p a c t i", i=8),
                 w_scale_raw[:, :, b * PASS : (b + 1) * PASS]
@@ -139,53 +152,48 @@ def tile_list_seller_trust_cache_kernel(
         v_codes = {}
 
         def gather_words(a, lo, hi):
-            tile = keep.tile([P, hi - lo], U32, name="v_codes%d_%d" % (a, lo), align_bytes=64)
-            nc.vector.tensor_copy(tile[:], tab[a][:].bitcast(U32).indirect(cols(list1, lo, hi)))
+            picked = keep.tile([P, hi - lo], U32, name="v_codes%d_%d" % (a, lo), align_bytes=64)
+            nc.vector.tensor_copy(picked[:], tab[a][:].bitcast(U32).indirect(entries(list1, lo, hi)))
             for c in range(lo, hi, HALF):
-                v_codes[a, c // HALF] = tile[:, c - lo : c - lo + HALF]
+                v_codes[a, c // HALF] = picked[:, c - lo : c - lo + HALF]
 
         gather_words(0, 0, S)
-        permute_w_codes(0)
+        order_w_codes(0, nc.vector)
         gather_words(1, 0, S)
-        permute_w_scale(0)
-        permute_w_scale(1)
+        order_w_scale(0)
+        order_w_scale(1)
         gather_words(2, 0, HALF)
         gather_words(2, HALF, S)
 
         def bank(n, name):
             return psum.tile([P, HALF], F32, name=name, tag="bank%d" % n)
 
-        tiles = B * PACK
-        last = tiles - 1
-        arena = keep.tile([P, (tiles + 3) * S], F32, name="arena", align_bytes=64)
-        slots = [arena[:, 0 : 4 * S], arena[:, 6 * S : 10 * S]]
-        flat_z = arena[:, 4 * S : 6 * S].bitcast(BF16).rearrange("p (t m) -> p t m", t=PACK)
-        rest = M - PAIR_COLS
-        flat_rest = arena[:, 10 * S : 10 * S + 2 * rest].bitcast(BF16).rearrange("p (t m) -> p t m", t=PACK)
-        pieces = [(0, 256), (256, 512), (512, 768), (768, 896), (896, 1024)]
-        recip_pieces = [[(0, M)], pieces]
+        arena = keep.tile([P, (TILES + 2) * S], F32, name="arena", align_bytes=64)
+        z_start, z_end = PACK * S, (PACK + 2) * S
+        x_pass = [arena[:, :z_start], arena[:, z_end:]]
+        flat_z = by_tile(arena[:, z_start:z_end].bitcast(BF16))
+        h_start = {1: 0, 2: z_start - HALF, 3: 2 * S, 4: z_end + S, 5: z_end - HALF, 6: z_end + 2 * S}
+
+        recip_ranges = [[(0, M)], PIECES]
         recip = {(0, 0): keep.tile([P, PACK * M], F32, name="recip0", tag="big1", align_bytes=64)}
-        for lo, hi in pieces:
+        for lo, hi in PIECES:
             recip[1, lo] = keep.tile([P, PACK * (hi - lo)], F32, name="recip1", tag="recip1_%d" % lo, align_bytes=64)
 
-        def row_tile(pair, i, lo, hi):
-            b, t = divmod(i, PACK)
-            return pair[b][:, t * S + lo : t * S + hi]
+        h_own = {
+            0: keep.tile([P, S], F32, name="h_first", tag="w_codes1", align_bytes=64),
+            LAST: keep.tile([P, S], F32, name="h_last", tag="h_last", align_bytes=64),
+        }
 
-        h_start = [S, 0, 4 * S - HALF, 2 * S, 7 * S, 6 * S - HALF, 10 * S, 9 * S]
-
-        h_first = keep.tile([P, S], F32, name="h_first", tag="w_codes1", align_bytes=64)
-
-        def h_tile(i, lo, hi):
-            if i == 0:
-                return h_first[:, lo:hi]
+        def h_cols(i, lo, hi):
+            if i in h_own:
+                return h_own[i][:, lo:hi]
             return arena[:, h_start[i] + lo : h_start[i] + hi]
 
         def first_product(i):
             b, t = divmod(i, PACK)
+            order = list(range(A)) if i == 0 else [A - 1] + list(range(A - 1))
             for half in range(2):
-                acc = bank((2 * i + half) % 8, "acc_h")
-                order = list(range(A)) if i == 0 else [A - 1] + list(range(A - 1))
+                acc = bank((2 * i + half) % BANKS, "acc_h")
                 for a in order:
                     nc.tensor.matmul_mx(
                         out=acc[:],
@@ -196,38 +204,35 @@ def tile_list_seller_trust_cache_kernel(
                         start=(a == order[0]),
                         stop=(a == order[-1]),
                     )
-                nc.scalar.copy(h_tile(i, half * HALF, (half + 1) * HALF), acc[:])
+                nc.scalar.copy(h_cols(i, half * HALF, (half + 1) * HALF), acc[:])
 
         def scatter(i, lo, hi):
             nc.vector.tensor_tensor(
-                page[i][:].indirect(cols(list2, lo, hi)),
-                h_tile(i, lo, hi),
-                wg[i % PACK][:, lo:hi],
-                MULT,
+                page[i][:].indirect(entries(list2, lo, hi)), h_cols(i, lo, hi), wg[i % PACK][:, lo:hi], MULT
             )
 
         gain_root = keep.tile([P, B, PACK], F32, name="gain_root")
         gain_sign = keep.tile([P, B, PACK], F32, name="gain_sign")
 
         def split_gain():
-            rows = gain_sb[:, :, 0 : 2 * PACK : 2]
-            nc.scalar.activation(gain_root[:], rows, ACT.Abs)
+            gains = gain_sb[:, :, 0 : 2 * PACK : 2]
+            nc.scalar.activation(gain_root[:], gains, ACT.Abs)
             nc.scalar.activation(gain_root[:], gain_root[:], ACT.Sqrt)
-            nc.scalar.activation(gain_sign[:], rows, ACT.Sign)
+            nc.scalar.activation(gain_sign[:], gains, ACT.Sign)
             nc.scalar.activation(gain_sign[:], gain_sign[:], ACT.Sign, bias=0.5)
 
         roots = {}
 
         def gather_page(i, lo, hi):
             b, t = divmod(i, PACK)
-            x = row_tile(slots, i, lo, hi)
+            x = x_pass[b][:, t * M + lo : t * M + hi]
             if lo == 0:
                 roots[i] = work.tile([P, M], F32, name="root")
             root = roots[i][:, lo:hi]
-            nc.vector.tensor_copy(x, page[i][:].indirect(cols(list3, lo, hi)))
+            nc.vector.tensor_copy(x, page[i][:].indirect(entries(list3, lo, hi)))
             nc.scalar.activation(root, x, ACT.Abs)
             nc.scalar.activation(root, root, ACT.Abs_reciprocal_sqrt, bias=1.0)
-            for first, end in recip_pieces[b]:
+            for first, end in recip_ranges[b]:
                 if lo <= first and end <= hi:
                     width = end - first
                     nc.scalar.activation(
@@ -237,8 +242,13 @@ def tile_list_seller_trust_cache_kernel(
                         scale=gain_root[:, b, t : t + 1],
                     )
 
-        def quantize(woven, width, name, tag=None):
-            codes = keep.tile([P, width], U32, name=name + "_codes", tag=tag or name, align_bytes=64)
+        def weave(woven, flat):
+            nc.scalar.copy(
+                woven.rearrange("p (c i) t -> p c t i", i=4), flat.rearrange("p t (c i) -> p c t i", i=4)
+            )
+
+        def quantize(woven, width, name, behind):
+            codes = keep.tile([P, width], U32, name=name + "_codes", tag=behind or name, align_bytes=64)
             scale = keep.tile([P, width], U8, name=name + "_scale", align_bytes=64)
             nc.vector.quantize_mx(
                 out=codes[:].bitcast(FP8X4), scales=scale[:], in_=woven.rearrange("p w t -> p (w t)")
@@ -246,64 +256,44 @@ def tile_list_seller_trust_cache_kernel(
             return codes, scale
 
         wb_rows = wb.rearrange("(b u t e) n -> b t u e n", b=B, t=PACK, e=2)
-        wb_raw = keep.tile([P, B * PACK * N], F32, name="wb_raw", tag="big0", align_bytes=64)
+        wb_raw = keep.tile([P, TILES * N], F32, name="wb_raw", tag="big0", align_bytes=64)
+        wb_woven = {}
         wb_q = {}
 
-        def load_wb(b):
-            for t in range(PACK):
-                nc.sync.dma_start(out=wb_raw[:, (b * PACK + t) * N : (b * PACK + t + 1) * N], in_=wb_rows[b, t])
-
-        def prepare_wb(b):
+        def weave_wb(b):
             for t in range(PACK):
                 rows = wb_raw[:, (b * PACK + t) * N : (b * PACK + t + 1) * N]
                 nc.scalar.activation(rows, rows, ACT.Copy, scale=gain_sign[:, b, t : t + 1])
-            woven = keep.tile([P, N, PACK], BF16, name="wb_woven%d" % b, align_bytes=64)
-            nc.scalar.copy(
-                woven[:].rearrange("p (c i) t -> p c t i", i=4),
-                wb_raw[:, b * PACK * N : (b + 1) * PACK * N].rearrange("p (t c i) -> p c t i", t=PACK, i=4),
-            )
-            wb_q[b] = woven
+            wb_woven[b] = keep.tile([P, N, PACK], BF16, name="wb_woven", tag="wb_woven%d" % b, align_bytes=64)
+            weave(wb_woven[b][:], by_tile(wb_raw[:, b * PACK * N : (b + 1) * PACK * N]))
 
-        z_q = {}
-
-        def softsign(b, lo, hi, tag):
-            woven = keep.tile([P, hi - lo, PACK], BF16, name="z_woven", tag=tag, align_bytes=64)
-
-            def four_rows(tile, first, end):
-                return tile.rearrange("p (t m) -> p t m", t=PACK)[:, :, first:end].rearrange("p t (c i) -> p c t i", i=2)
-
-            d = four_rows(recip[0, 0][:], lo, hi) if b == 0 else four_rows(recip[1, lo][:], 0, hi - lo)
-            nc.vector.tensor_tensor(
-                woven[:].rearrange("p (c i) t -> p c t i", i=2), four_rows(slots[b], lo, hi), d, MULT
-            )
-            return woven
-
-        def softsign_flat(dst, t, count, lo, hi):
+        def z_on_gpsimd(flat, t, count, lo, hi):
             nc.gpsimd.tensor_tensor(
-                dst,
-                slots[0].rearrange("p (t m) -> p t m", t=PACK)[:, t : t + count, lo:hi],
-                recip[0, 0][:].rearrange("p (t m) -> p t m", t=PACK)[:, t : t + count, lo:hi],
+                flat,
+                by_tile(x_pass[0])[:, t : t + count, lo:hi],
+                by_tile(recip[0, 0][:])[:, t : t + count, lo:hi],
                 MULT,
             )
 
-        def weave(dst, src):
-            nc.scalar.copy(dst.rearrange("p (c i) t -> p c t i", i=4), src.rearrange("p t (c i) -> p c t i", i=4))
-
-        def quantize_z(b, lo, hi, woven, tag=None):
-            codes, scale = quantize(woven, hi - lo, "z%d_%d" % (b, lo), tag)
-            for first, end in pieces:
-                if lo <= first and end <= hi:
-                    z_q[b, first] = (codes[:, first - lo : end - lo], scale[:, first - lo : end - lo])
+        def z_on_vector(lo, hi):
+            woven = keep.tile([P, hi - lo, PACK], BF16, name="z_tail%d" % lo, align_bytes=64)
+            nc.vector.tensor_tensor(
+                woven[:].rearrange("p (c i) t -> p c t i", i=2),
+                by_tile(x_pass[1])[:, :, lo:hi].rearrange("p t (c i) -> p c t i", i=2),
+                by_tile(recip[1, lo][:]).rearrange("p t (c i) -> p c t i", i=2),
+                MULT,
+            )
+            return woven[:]
 
         out_rows = out.rearrange("(n p) m -> p n m", p=P)
         out_acc = {}
-        staged = keep.tile([P, 8 * HALF], F32, name="staged", tag="big2", align_bytes=64)
+        staged = keep.tile([P, BANKS * HALF], F32, name="staged", tag="big2", align_bytes=64)
 
         def banks_of(lo, hi):
             per_bank = HALF // (hi - lo)
             return [(lo // P + g, range(g * per_bank, (g + 1) * per_bank)) for g in range(N // P // per_bank)]
 
-        def second_product(b, lo, hi):
+        def second_product(b, lo, hi, codes, scale):
             width = hi - lo
             for number, blocks in banks_of(lo, hi):
                 if b == 0:
@@ -313,8 +303,8 @@ def tile_list_seller_trust_cache_kernel(
                         out=out_acc[number][:, s * width : (s + 1) * width],
                         lhsT=wb_q[b][0][:, n * P : (n + 1) * P].bitcast(FP8X4),
                         lhsT_scale=wb_q[b][1][:, n * P : (n + 1) * P],
-                        rhs=z_q[b, lo][0].bitcast(FP8X4),
-                        rhs_scale=z_q[b, lo][1],
+                        rhs=codes.bitcast(FP8X4),
+                        rhs_scale=scale,
                         start=(b == 0 and s == 0),
                         stop=(b == B - 1 and n == blocks[-1]),
                     )
@@ -322,72 +312,73 @@ def tile_list_seller_trust_cache_kernel(
         def store(lo, hi):
             for number, blocks in banks_of(lo, hi):
                 res = staged[:, number * HALF : (number + 1) * HALF]
-                if number in (5, 7):
+                if number >= BANKS - 4 and number % 2 == 1:
                     nc.vector.tensor_copy(res, out_acc[number][:])
                 else:
                     nc.scalar.copy(res, out_acc[number][:])
-                queue = nc.scalar if number == 6 else nc.sync
+                queue = nc.scalar if number == BANKS - 2 else nc.sync
                 queue.dma_start(
                     out=out_rows[:, blocks[0] : blocks[-1] + 1, lo:hi],
                     in_=res.rearrange("p (s w) -> p s w", s=len(blocks)),
                 )
+
+        def finish(b, lo, hi, woven, behind):
+            codes, scale = quantize(woven, hi - lo, "z%d_%d" % (b, lo), behind)
+            for first, end in pieces_in(lo, hi):
+                second_product(b, first, end, codes[:, first - lo : end - lo], scale[:, first - lo : end - lo])
+                if b == B - 1:
+                    store(first, end)
 
         for i in (0, 1, 3, 2):
             first_product(i)
         scatter(0, 0, HALF)
         scatter(0, HALF, S)
         scatter(1, 0, S)
-        permute_w_codes(1)
-        for i in range(PACK, tiles):
+        order_w_codes(1, nc.gpsimd)
+        for i in range(PACK, TILES):
             first_product(i)
-        for b in range(B):
-            load_wb(b)
+        for i in range(TILES):
+            nc.sync.dma_start(out=wb_raw[:, i * N : (i + 1) * N], in_=wb_rows[i // PACK, i % PACK])
         split_gain()
         gather_page(0, 0, M)
         gather_page(1, 0, M)
-        prepare_wb(0)
-        for k, (first, second) in enumerate([(3, 2), (4, 5)]):
-            load_page(4 + 2 * k)
-            load_page(5 + 2 * k)
+
+        def pair(first, second, ready):
+            load_page(ready + PAGE_BUFS)
+            load_page(ready + PAGE_BUFS + 1)
             scatter(first, 0, S)
-            if k == 1:
-                wb_q[0] = quantize(wb_q[0][:], N, "wb0", "wg0")
             scatter(second, 0, S)
-            softsign_flat(flat_z[:, 2 * k : 2 * k + 2, 0:PAIR_COLS], 2 * k, 2, 0, PAIR_COLS)
+            z_on_gpsimd(flat_z[:, ready : ready + 2, 0:PAIR_COLS], ready, 2, 0, PAIR_COLS)
             gather_page(first, 0, M)
             gather_page(second, 0, M)
-            if k == 0:
-                prepare_wb(1)
-        early = [keep.tile([P, HALF, PACK], BF16, name="early%d" % half, align_bytes=64) for half in range(2)]
-        weave(early[0][:], flat_z[:, :, 0:HALF])
-        weave(early[1][:, 0 : PAIR_COLS - HALF, :], flat_z[:, :, HALF:PAIR_COLS])
 
-        def finish(b, lo, hi, woven, tag):
-            quantize_z(b, lo, hi, woven, tag=tag)
-            for first, end in pieces:
-                if lo <= first and end <= hi:
-                    second_product(b, first, end)
-                    if b == B - 1:
-                        store(first, end)
+        weave_wb(0)
+        pair(3, 2, 0)
+        weave_wb(1)
+        pair(4, 5, 2)
+        z0 = [keep.tile([P, HALF, PACK], BF16, name="z0_half%d" % half, align_bytes=64) for half in range(2)]
+        weave(z0[0][:], flat_z[:, :, 0:HALF])
+        weave(z0[1][:, 0 : PAIR_COLS - HALF, :], flat_z[:, :, HALF:PAIR_COLS])
 
-        scatter(last - 1, 0, S)
-        wb_q[1] = quantize(wb_q[1][:], N, "wb1", "wg2")
-        softsign_flat(flat_rest, 0, PACK, PAIR_COLS, M)
-        gather_page(last - 1, 0, M)
-        weave(early[1][:, PAIR_COLS - HALF :, :], flat_rest)
-        scatter(last, 0, S)
-        finish(0, 0, HALF, early[0][:], "wg3")
-        for quarter in range(4):
-            gather_page(last, quarter * QUARTER, (quarter + 1) * QUARTER)
+        scatter(LAST - 1, 0, S)
+        wb_q[0] = quantize(wb_woven[0][:], N, "wb0", "wg%d" % ((LAST - 1) % PACK))
+        flat_rest = keep.tile([P, PACK, M - PAIR_COLS], BF16, name="flat_rest", tag="wb_woven0", align_bytes=64)
+        z_on_gpsimd(flat_rest[:], 0, PACK, PAIR_COLS, M)
+        gather_page(LAST - 1, 0, M)
+        weave(z0[1][:, PAIR_COLS - HALF :, :], flat_rest[:])
+        scatter(LAST, 0, S)
+        wb_q[1] = quantize(wb_woven[1][:], N, "wb1", "wg%d" % (LAST % PACK))
+        for lo in range(0, M, QUARTER):
+            gather_page(LAST, lo, lo + QUARTER)
+        finish(0, 0, HALF, z0[0][:], "h_last")
 
-        for lo, hi in pieces[:2]:
-            woven = softsign(1, lo, hi, "z_tail%d" % lo)
-            finish(0, HALF + lo, HALF + hi, early[1][:, lo:hi, :], "recip1_%d" % lo)
-            finish(1, lo, hi, woven[:], None)
-        waiting = None
-        for lo, hi in pieces[2:]:
-            woven = softsign(1, lo, hi, "z_tail%d" % lo)
-            if waiting:
-                finish(*waiting, "recip1_%d" % lo)
-            waiting = (1, lo, hi, woven[:])
-        finish(*waiting, None)
+        for lo, hi in PIECES[:2]:
+            woven = z_on_vector(lo, hi)
+            finish(0, HALF + lo, HALF + hi, z0[1][:, lo:hi, :], "recip1_%d" % lo)
+            finish(1, lo, hi, woven, None)
+        woven = z_on_vector(*PIECES[2])
+        for (lo, hi), following in zip(PIECES[2:], PIECES[3:]):
+            woven_next = z_on_vector(*following)
+            finish(1, lo, hi, woven, "recip1_%d" % following[0])
+            woven = woven_next
+        finish(1, *PIECES[-1], woven, None)

@@ -27,6 +27,14 @@ LAST = TILES - 1
 BANKS = 8
 HALF = 512
 QUARTER = 256
+ROWS = A * 16
+ROW0 = 48
+AT_PAGES = 4 * T
+AT_WG = AT_PAGES + 4 * 4 * T2
+AT_W1 = AT_WG + PACK * 4 * S
+AT_PLANES1 = AT_W1 + A * 2 * PASS
+AT_GAIN = AT_PLANES1 + A * PASS
+AT_END = AT_GAIN + 64
 STRIPE = 16
 PAGE_BUFS = 4
 PAIR_COLS = 832
@@ -47,7 +55,7 @@ def tile_list_seller_trust_cache_kernel(
     nc = tc.nc
     with ExitStack() as ctx:
         keep = ctx.enter_context(tc.tile_pool(name="keep", bufs=1))
-        pages = ctx.enter_context(tc.tile_pool(name="pages", bufs=PAGE_BUFS))
+        placed = ctx.enter_context(tc.tile_pool(name="placed", bufs=1))
         work = ctx.enter_context(tc.tile_pool(name="work", bufs=1))
         psum = ctx.enter_context(tc.psum_pool(name="psum", bufs=1))
 
@@ -59,109 +67,122 @@ def tile_list_seller_trust_cache_kernel(
             return lst[:, lo // STRIPE : hi // STRIPE]
 
         tab_scale_win = keep.tile([P, T], U8, name="tab_scale_win", align_bytes=64)
-        w_scale_raw = keep.tile([P, A, H], U8, name="w_scale_raw", align_bytes=64)
-        v_scale = [keep.tile([P, S], U8, name="v_scale%d" % a, align_bytes=64) for a in range(A)]
-        nc.vector.memset(tab_scale_win[:].bitcast(I32), 0)
-        nc.vector.memset(w_scale_raw[:].bitcast(I32), 0)
-        for a in range(1, A):
-            nc.vector.memset(v_scale[a][:].bitcast(I32), 0)
+        w_scale_raw = keep.tile([P, H], U8, name="w_scale_raw", align_bytes=64)
+        planes = keep.tile([P, A, S + PASS], U8, name="planes", align_bytes=64)
+        for rows in (slice(0, ROW0), slice(ROW0 + ROWS, P)):
+            nc.vector.memset(tab_scale_win[rows, :].bitcast(I32), 0)
+            nc.vector.memset(w_scale_raw[rows, :].bitcast(I32), 0)
+        nc.vector.memset(planes[:].bitcast(I32), 0)
 
-        tab = [keep.tile([P, T], I32, name="tab%d" % a, tag="big%d" % a, align_bytes=64) for a in range(A)]
+        tab = [
+            placed.tile([P, AT_END // 4], I32, name="tab0", offset=0, align_bytes=64)[:, :T],
+            keep.tile([P, T], I32, name="tab1", tag="big1", align_bytes=64)[:],
+            keep.tile([P, T], I32, name="tab2", tag="big2", align_bytes=64)[:],
+        ]
 
         def load_tab(a):
-            nc.sync.dma_start(out=tab[a][:], in_=tab_words[a].rearrange("p n t -> p (n t)").bitcast(I32))
+            nc.sync.dma_start(out=tab[a], in_=tab_words[a].rearrange("p n t -> p (n t)").bitcast(I32))
 
         pairs = PASS // 2
-        w_raw = [keep.tile([P, A, pairs], I32, name="w_raw%d" % b, align_bytes=64) for b in range(B)]
+        w_raw = [
+            keep.tile([P, A, pairs], I32, name="w_raw0", align_bytes=64)[:],
+            placed.tile([P, A, pairs], I32, name="w_raw1", offset=AT_W1, align_bytes=64)[:],
+        ]
         w_words_i32 = w4_words.rearrange("a p n -> p a n").bitcast(I32)
 
         def load_w(b):
-            nc.sync.dma_start(out=w_raw[b][:], in_=w_words_i32[:, :, b * pairs : (b + 1) * pairs])
+            nc.sync.dma_start(out=w_raw[b], in_=w_words_i32[:, :, b * pairs : (b + 1) * pairs])
 
-        wg = [keep.tile([P, S], F32, name="wg%d" % t, tag="wg%d" % t, align_bytes=64) for t in range(PACK)]
+        wg = [
+            placed.tile([P, S], F32, name="wg%d" % t, tag="wg%d" % t, offset=AT_WG + 4 * S * t, align_bytes=64)
+            for t in range(PACK)
+        ]
         wgs_rows = wgs.rearrange("(u t e) j -> t u e j", t=PACK, e=2)
 
-        def load_wg(t, lo, hi):
+        wg_first = keep.tile([P, HALF], F32, name="wg_first", align_bytes=64)
+
+        def load_wg(t, lo, hi, tile=None):
             for q in (0, 2, 1, 3):
-                nc.sync.dma_start(out=wg[t][QUAD * q : QUAD * (q + 1), lo:hi], in_=wgs_rows[t][:, :, lo:hi])
+                nc.sync.dma_start(out=(tile or wg[t])[QUAD * q : QUAD * (q + 1), lo:hi], in_=wgs_rows[t][:, :, lo:hi])
 
         page_rows = page0.rearrange("(b u t e) c -> b t u e c", b=B, t=PACK, e=2)
         page = {}
 
         def load_page(i):
-            page[i] = pages.tile([P, T2], F32, name="page")
+            page[i] = placed.tile([P, T2], F32, name="page", bufs=PAGE_BUFS, offset=AT_PAGES, align_bytes=64)
             nc.sync.dma_start(out=page[i][:], in_=page_rows[i // PACK, i % PACK])
 
         gain_rows = gain.rearrange("(b u w) -> u b w", b=B, w=2 * PACK)
-        gain_sb = keep.tile([P, B, 2 * PACK], F32, name="gain_sb")
+        gain_sb = placed.tile([P, B, 2 * PACK], F32, name="gain_sb", offset=AT_GAIN, align_bytes=64)
 
         load_tab(0)
+        for tile, rows in ((tab_scale_win, tab_scales), (w_scale_raw, w4_scales)):
+            nc.sync.dma_start(
+                out=tile[ROW0 : ROW0 + ROWS, :].bitcast(I32), in_=rows.rearrange("a q n -> q a n").bitcast(I32)
+            )
         nc.sync.dma_start(list1[:], offs)
-        for q in range(4):
-            nc.sync.dma_start(
-                out=tab_scale_win[QUAD * q : QUAD * q + 4 * A, :].bitcast(I32),
-                in_=tab_scales[:, 4 * q : 4 * q + 4, :].bitcast(I32),
-            )
         load_w(0)
-        load_tab(1)
-        for q in range(4):
-            nc.sync.dma_start(
-                out=w_scale_raw[QUAD * q : QUAD * q + 4, :, :].bitcast(I32),
-                in_=w4_scales[:, 4 * q : 4 * q + 4, :].rearrange("a r n -> r a n").bitcast(I32),
-            )
         nc.sync.dma_start(list2[:], offs2)
+        nc.sync.dma_start(list3[:], offs3)
+        load_tab(1)
+        load_wg(0, 0, HALF, wg_first)
         load_tab(2)
         load_page(0)
-        load_wg(0, 0, HALF)
         load_wg(0, HALF, S)
         load_page(1)
         load_wg(1, 0, S)
-        nc.sync.dma_start(list3[:], offs3)
         load_w(1)
         for e in range(2):
             nc.sync.dma_start(out=gain_sb[e:P:2, :, 0 : 2 * PACK - 1], in_=gain_rows[:, :, e : e + 2 * PACK - 1])
-        load_page(3)
-        load_wg(3, 0, S)
-        load_page(2)
-        load_wg(2, 0, S)
 
-        nc.vector.tensor_copy(v_scale[0][:], tab_scale_win[:].indirect(list1[:]))
-        for a in range(1, A):
-            nc.scalar.dma_start(
-                out=v_scale[a][0:112, :].bitcast(I32), in_=v_scale[0][4 * a : 4 * a + 112, :].bitcast(I32)
-            )
+        v_scale = keep.tile([P, S], U8, name="v_scale", tag="v_codes0_0", align_bytes=64)
+        staged_scales = keep.tile([P, S + H], U8, name="staged_scales", align_bytes=64)
+        nc.vector.tensor_copy(v_scale[:], tab_scale_win[:].indirect(list1[:]))
+        nc.vector.tensor_copy(staged_scales[:, :S].bitcast(I32), v_scale[:].bitcast(I32))
+        nc.vector.tensor_copy(
+            staged_scales[:, S:].bitcast(U16).rearrange("p (b t c i) -> p b c t i", b=B, t=PACK, i=8),
+            w_scale_raw[:].bitcast(U16).rearrange("p (b c i t) -> p b c t i", b=B, i=8, t=PACK),
+        )
+
+        def move_scales(queue, target, lo, hi):
+            for q in (0, 2, 1, 3):
+                first = ROW0 + 4 * A * q
+                queue.dma_start(
+                    out=target[QUAD * q : QUAD * q + 4, :, :].bitcast(I32),
+                    in_=staged_scales[first : first + 4 * A, lo:hi].bitcast(I32),
+                )
+
+        move_scales(nc.scalar, planes, 0, S + PASS)
 
         w_codes = {}
-        w_scale = [keep.tile([P, A, PACK, P], U8, name="w_scale%d" % b, align_bytes=64) for b in range(B)]
 
         def order_w_codes(b, engine):
             w_codes[b] = keep.tile([P, A, PACK, 2 * P], U8, name="w_codes", tag="w_codes%d" % b, align_bytes=64)
             engine.tensor_copy(
                 w_codes[b][:].bitcast(I32).rearrange("p a t (c i) -> p a c t i", i=4),
-                w_raw[b][:].rearrange("p a (c i t) -> p a c t i", i=4, t=PACK),
-            )
-
-        def order_w_scale(b):
-            nc.vector.tensor_copy(
-                w_scale[b][:].bitcast(U16).rearrange("p a t (c i) -> p a c t i", i=8),
-                w_scale_raw[:, :, b * PASS : (b + 1) * PASS]
-                .bitcast(U16)
-                .rearrange("p a (c i t) -> p a c t i", i=8, t=PACK),
+                w_raw[b].rearrange("p a (c i t) -> p a c t i", i=4, t=PACK),
             )
 
         v_codes = {}
 
         def gather_words(a, lo, hi):
-            picked = keep.tile([P, hi - lo], U32, name="v_codes%d_%d" % (a, lo), align_bytes=64)
-            nc.vector.tensor_copy(picked[:], tab[a][:].bitcast(U32).indirect(entries(list1, lo, hi)))
+            picked = keep.tile([P, hi - lo], U32, name="picked", tag="v_codes%d_%d" % (a, lo), align_bytes=64)
+            nc.vector.tensor_copy(picked[:], tab[a].bitcast(U32).indirect(entries(list1, lo, hi)))
             for c in range(lo, hi, HALF):
                 v_codes[a, c // HALF] = picked[:, c - lo : c - lo + HALF]
 
-        gather_words(0, 0, S)
         order_w_codes(0, nc.vector)
+        gather_words(0, 0, S)
+        planes1 = placed.tile([P, A, PASS], U8, name="planes1", offset=AT_PLANES1, align_bytes=64)
+        nc.vector.memset(planes1[:].bitcast(I32), 0)
+        w_scale = [planes[:, :, S:], planes1[:]]
+        move_scales(nc.sync, planes1, S + PASS, S + H)
+        load_page(3)
+        load_wg(3, 0, S)
+        load_page(2)
+        load_wg(2, 0, S)
+        load_wg(0, 0, HALF)
         gather_words(1, 0, S)
-        order_w_scale(0)
-        order_w_scale(1)
         gather_words(2, 0, HALF)
         gather_words(2, HALF, S)
 
@@ -198,17 +219,18 @@ def tile_list_seller_trust_cache_kernel(
                     nc.tensor.matmul_mx(
                         out=acc[:],
                         lhsT=w_codes[b][:, a, t, :].bitcast(FP4X4),
-                        lhsT_scale=w_scale[b][:, a, t, :],
+                        lhsT_scale=w_scale[b][:, a, t * P : (t + 1) * P],
                         rhs=v_codes[a, half].bitcast(FP8X4),
-                        rhs_scale=v_scale[a][:, half * HALF : (half + 1) * HALF],
+                        rhs_scale=planes[:, a, half * HALF : (half + 1) * HALF],
                         start=(a == order[0]),
                         stop=(a == order[-1]),
                     )
                 nc.scalar.copy(h_cols(i, half * HALF, (half + 1) * HALF), acc[:])
 
         def scatter(i, lo, hi):
+            weights = wg_first if (i, lo) == (0, 0) else wg[i % PACK]
             nc.vector.tensor_tensor(
-                page[i][:].indirect(entries(list2, lo, hi)), h_cols(i, lo, hi), wg[i % PACK][:, lo:hi], MULT
+                page[i][:].indirect(entries(list2, lo, hi)), h_cols(i, lo, hi), weights[:, lo:hi], MULT
             )
 
         gain_root = keep.tile([P, B, PACK], F32, name="gain_root")
@@ -247,8 +269,13 @@ def tile_list_seller_trust_cache_kernel(
                 woven.rearrange("p (c i) t -> p c t i", i=4), flat.rearrange("p t (c i) -> p c t i", i=4)
             )
 
+        wg_at = {"wg%d" % t: AT_WG + 4 * S * t for t in range(PACK)}
+
         def quantize(woven, width, name, behind):
-            codes = keep.tile([P, width], U32, name=name + "_codes", tag=behind or name, align_bytes=64)
+            if behind in wg_at:
+                codes = placed.tile([P, width], U32, name=name + "_codes", tag=behind, offset=wg_at[behind], align_bytes=64)
+            else:
+                codes = keep.tile([P, width], U32, name=name + "_codes", tag=behind or name, align_bytes=64)
             scale = keep.tile([P, width], U8, name=name + "_scale", align_bytes=64)
             nc.vector.quantize_mx(
                 out=codes[:].bitcast(FP8X4), scales=scale[:], in_=woven.rearrange("p w t -> p (w t)")
@@ -256,7 +283,7 @@ def tile_list_seller_trust_cache_kernel(
             return codes, scale
 
         wb_rows = wb.rearrange("(b u t e) n -> b t u e n", b=B, t=PACK, e=2)
-        wb_raw = keep.tile([P, TILES * N], F32, name="wb_raw", tag="big0", align_bytes=64)
+        wb_raw = placed.tile([P, TILES * N], F32, name="wb_raw", offset=0, align_bytes=64)
         wb_woven = {}
         wb_q = {}
 

@@ -35,9 +35,12 @@ AT_W1 = AT_WG + PACK * 4 * S
 AT_PLANES1 = AT_W1 + A * 2 * PASS
 AT_GAIN = AT_PLANES1 + A * PASS
 AT_END = AT_GAIN + 64
+AT_HW = AT_END
+AT_RECIP = AT_HW + 2 * 4 * S
+AT_Z1 = AT_RECIP + 2 * 4 * M
+AT_Z0 = AT_Z1 + 2 * PACK * M
 STRIPE = 16
 PAGE_BUFS = 4
-PAIR_COLS = 832
 PIECES = [(0, 256), (256, 512), (512, 768), (768, 896), (896, 1024)]
 
 
@@ -189,26 +192,44 @@ def tile_list_seller_trust_cache_kernel(
         def bank(n, name):
             return psum.tile([P, HALF], F32, name=name, tag="bank%d" % n)
 
-        arena = keep.tile([P, (TILES + 2) * S], F32, name="arena", align_bytes=64)
-        z_start, z_end = PACK * S, (PACK + 2) * S
-        x_pass = [arena[:, :z_start], arena[:, z_end:]]
-        flat_z = by_tile(arena[:, z_start:z_end].bitcast(BF16))
-        h_start = {1: 0, 2: z_start - HALF, 3: 2 * S, 4: z_end + S, 5: z_end - HALF, 6: z_end + 2 * S}
+        z_start, z_end = PACK * S, (PACK + 1) * S
+        x1_start = z_end + HALF
+        arena = keep.tile([P, x1_start + PACK * S], F32, name="arena", align_bytes=64)
+        x_pass = [arena[:, :z_start], arena[:, x1_start:]]
+        h_start = {1: 0, 2: z_start - HALF, 4: x1_start + S, 5: z_end - QUARTER, 6: x1_start + 2 * S}
 
-        recip_ranges = [[(0, M)], PIECES]
-        recip = {(0, 0): keep.tile([P, PACK * M], F32, name="recip0", tag="big1", align_bytes=64)}
-        for lo, hi in PIECES:
-            recip[1, lo] = keep.tile([P, PACK * (hi - lo)], F32, name="recip1", tag="recip1_%d" % lo, align_bytes=64)
+        recip0 = keep.tile([P, PACK * M], F32, name="recip0", tag="big1", align_bytes=64)
+        recip45 = placed.tile([P, 2 * M], F32, name="recip45", offset=AT_RECIP, align_bytes=64)
+        recip67 = {
+            lo: keep.tile([P, 2 * (hi - lo)], F32, name="recip67", tag="recip1_%d" % lo, align_bytes=64)
+            for lo, hi in PIECES
+        }
+
+        def recip_parts(i):
+            if i < PACK:
+                return [(0, M, recip0[:, i * M : (i + 1) * M])]
+            if i < PACK + 2:
+                return [(0, M, recip45[:, (i - PACK) * M : (i - PACK + 1) * M])]
+            t = i - PACK - 2
+            return [(lo, hi, recip67[lo][:, t * (hi - lo) : (t + 1) * (hi - lo)]) for lo, hi in PIECES]
 
         h_own = {
             0: keep.tile([P, S], F32, name="h_first", tag="w_codes1", align_bytes=64),
-            LAST: keep.tile([P, S], F32, name="h_last", tag="h_last", align_bytes=64),
+            3: placed.tile([P, S], F32, name="h3", offset=AT_HW + 2 * S, align_bytes=64),
         }
 
         def h_cols(i, lo, hi):
             if i in h_own:
                 return h_own[i][:, lo:hi]
+            if i == LAST:
+                start = x1_start + 3 * S if lo == 0 else z_end
+                return arena[:, start : start + hi - lo]
             return arena[:, h_start[i] + lo : h_start[i] + hi]
+
+        h_acc = {}
+
+        def evacuate(i, half):
+            nc.scalar.copy(h_cols(i, half * HALF, (half + 1) * HALF), h_acc[i, half][:])
 
         def first_product(i):
             b, t = divmod(i, PACK)
@@ -225,13 +246,27 @@ def tile_list_seller_trust_cache_kernel(
                         start=(a == order[0]),
                         stop=(a == order[-1]),
                     )
-                nc.scalar.copy(h_cols(i, half * HALF, (half + 1) * HALF), acc[:])
+                h_acc[i, half] = acc
+                if (i, half) != (LAST, 1):
+                    evacuate(i, half)
 
         def scatter(i, lo, hi):
             weights = wg_first if (i, lo) == (0, 0) else wg[i % PACK]
             nc.vector.tensor_tensor(
                 page[i][:].indirect(entries(list2, lo, hi)), h_cols(i, lo, hi), weights[:, lo:hi], MULT
             )
+
+        weighted = {}
+
+        def weigh(i, lo, hi):
+            if lo == 0:
+                weighted[i] = placed.tile(
+                    [P, S], F32, name="weighted%d" % i, offset=AT_HW + 4 * S * (i - LAST + 1), align_bytes=64
+                )
+            nc.gpsimd.tensor_tensor(weighted[i][:, lo:hi], h_cols(i, lo, hi), wg[i % PACK][:, lo:hi], MULT)
+
+        def scatter_weighted(i):
+            nc.vector.tensor_copy(page[i][:].indirect(list2[:]), weighted[i][:])
 
         gain_root = keep.tile([P, B, PACK], F32, name="gain_root")
         gain_sign = keep.tile([P, B, PACK], F32, name="gain_sign")
@@ -252,16 +287,15 @@ def tile_list_seller_trust_cache_kernel(
                 roots[i] = work.tile([P, M], F32, name="root")
             root = roots[i][:, lo:hi]
             nc.vector.tensor_copy(x, page[i][:].indirect(entries(list3, lo, hi)))
-            nc.scalar.activation(root, x, ACT.Abs)
-            nc.scalar.activation(root, root, ACT.Abs_reciprocal_sqrt, bias=1.0)
-            for first, end in recip_ranges[b]:
+            size = root
+            if i == PACK + 1:
+                size = placed.tile([P, M], F32, name="size5", offset=AT_Z0 + 2 * M, align_bytes=64)[:]
+            nc.scalar.activation(size, x, ACT.Abs)
+            nc.scalar.activation(root, size, ACT.Abs_reciprocal_sqrt, bias=1.0)
+            for first, end, target in recip_parts(i):
                 if lo <= first and end <= hi:
-                    width = end - first
                     nc.scalar.activation(
-                        recip[b, first][:, t * width : (t + 1) * width],
-                        root[:, first - lo : end - lo],
-                        ACT.Square,
-                        scale=gain_root[:, b, t : t + 1],
+                        target, root[:, first - lo : end - lo], ACT.Square, scale=gain_root[:, b, t : t + 1]
                     )
 
         def weave(woven, flat):
@@ -269,11 +303,9 @@ def tile_list_seller_trust_cache_kernel(
                 woven.rearrange("p (c i) t -> p c t i", i=4), flat.rearrange("p t (c i) -> p c t i", i=4)
             )
 
-        wg_at = {"wg%d" % t: AT_WG + 4 * S * t for t in range(PACK)}
-
         def quantize(woven, width, name, behind):
-            if behind in wg_at:
-                codes = placed.tile([P, width], U32, name=name + "_codes", tag=behind, offset=wg_at[behind], align_bytes=64)
+            if isinstance(behind, int):
+                codes = placed.tile([P, width], U32, name=name + "_codes", offset=behind, align_bytes=64)
             else:
                 codes = keep.tile([P, width], U32, name=name + "_codes", tag=behind or name, align_bytes=64)
             scale = keep.tile([P, width], U8, name=name + "_scale", align_bytes=64)
@@ -291,26 +323,32 @@ def tile_list_seller_trust_cache_kernel(
             for t in range(PACK):
                 rows = wb_raw[:, (b * PACK + t) * N : (b * PACK + t + 1) * N]
                 nc.scalar.activation(rows, rows, ACT.Copy, scale=gain_sign[:, b, t : t + 1])
-            wb_woven[b] = keep.tile([P, N, PACK], BF16, name="wb_woven", tag="wb_woven%d" % b, align_bytes=64)
-            weave(wb_woven[b][:], by_tile(wb_raw[:, b * PACK * N : (b + 1) * PACK * N]))
+            if b == 0:
+                wb_woven[b] = placed.tile([P, M, PACK], BF16, name="wb_woven0", offset=AT_Z1, align_bytes=64)[:, :N, :]
+            else:
+                wb_woven[b] = keep.tile([P, N, PACK], BF16, name="wb_woven1", align_bytes=64)[:]
+            weave(wb_woven[b], by_tile(wb_raw[:, b * PACK * N : (b + 1) * PACK * N]))
 
-        def z_on_gpsimd(flat, t, count, lo, hi):
-            nc.gpsimd.tensor_tensor(
-                flat,
-                by_tile(x_pass[0])[:, t : t + count, lo:hi],
-                by_tile(recip[0, 0][:])[:, t : t + count, lo:hi],
+        def z_flat(flat, lo, hi):
+            nc.gpsimd.tensor_tensor(flat, by_tile(x_pass[0])[:, :, lo:hi], by_tile(recip0[:])[:, :, lo:hi], MULT)
+
+        z1 = {}
+
+        def z_pair(engine, t, lo, hi, recip):
+            if t == 0:
+                z1[lo] = placed.tile(
+                    [P, hi - lo, PACK], BF16, name="z1_%d" % lo, offset=AT_Z1 + 2 * PACK * lo, align_bytes=64
+                )
+            engine.tensor_tensor(
+                z1[lo][:, :, t : t + 2].rearrange("p (c i) t -> p c t i", i=2),
+                by_tile(x_pass[1])[:, t : t + 2, lo:hi].rearrange("p t (c i) -> p c t i", i=2),
+                recip.rearrange("p t (c i) -> p c t i", i=2),
                 MULT,
             )
+            return z1[lo][:]
 
         def z_on_vector(lo, hi):
-            woven = keep.tile([P, hi - lo, PACK], BF16, name="z_tail%d" % lo, align_bytes=64)
-            nc.vector.tensor_tensor(
-                woven[:].rearrange("p (c i) t -> p c t i", i=2),
-                by_tile(x_pass[1])[:, :, lo:hi].rearrange("p t (c i) -> p c t i", i=2),
-                by_tile(recip[1, lo][:]).rearrange("p t (c i) -> p c t i", i=2),
-                MULT,
-            )
-            return woven[:]
+            return z_pair(nc.vector, 2, lo, hi, recip67[lo][:].rearrange("p (t m) -> p t m", t=2))
 
         out_rows = out.rearrange("(n p) m -> p n m", p=P)
         out_acc = {}
@@ -370,34 +408,47 @@ def tile_list_seller_trust_cache_kernel(
         gather_page(0, 0, M)
         gather_page(1, 0, M)
 
-        def pair(first, second, ready):
-            load_page(ready + PAGE_BUFS)
-            load_page(ready + PAGE_BUFS + 1)
-            scatter(first, 0, S)
-            scatter(second, 0, S)
-            z_on_gpsimd(flat_z[:, ready : ready + 2, 0:PAIR_COLS], ready, 2, 0, PAIR_COLS)
-            gather_page(first, 0, M)
-            gather_page(second, 0, M)
-
         weave_wb(0)
-        pair(3, 2, 0)
+        load_page(4)
+        load_page(5)
+        scatter(3, 0, S)
+        scatter(2, 0, S)
+        weigh(6, 0, S)
+        weigh(7, 0, HALF)
+        gather_page(3, 0, M)
+        gather_page(2, 0, M)
         weave_wb(1)
-        pair(4, 5, 2)
-        z0 = [keep.tile([P, HALF, PACK], BF16, name="z0_half%d" % half, align_bytes=64) for half in range(2)]
-        weave(z0[0][:], flat_z[:, :, 0:HALF])
-        weave(z0[1][:, 0 : PAIR_COLS - HALF, :], flat_z[:, :, HALF:PAIR_COLS])
+        load_page(6)
+        load_page(7)
+        scatter(4, 0, S)
+        scatter(5, 0, S)
+        evacuate(LAST, 1)
+        flat = [
+            by_tile(placed.tile([P, PACK * HALF], BF16, name="flat_a", offset=AT_WG + 4 * S, align_bytes=64)[:]),
+            by_tile(arena[:, z_start:z_end].bitcast(BF16)),
+        ]
+        for half in range(2):
+            z_flat(flat[half], half * HALF, (half + 1) * HALF)
+        weigh(7, HALF, S)
+        gather_page(4, 0, M)
+        gather_page(5, 0, M)
+        z0 = [
+            placed.tile([P, HALF, PACK], BF16, name="z0_%d" % half, offset=AT_Z0 + 4 * M * half, align_bytes=64)
+            for half in range(2)
+        ]
+        for half in range(2):
+            weave(z0[half][:], flat[half])
 
-        scatter(LAST - 1, 0, S)
-        wb_q[0] = quantize(wb_woven[0][:], N, "wb0", "wg%d" % ((LAST - 1) % PACK))
-        flat_rest = keep.tile([P, PACK, M - PAIR_COLS], BF16, name="flat_rest", tag="wb_woven0", align_bytes=64)
-        z_on_gpsimd(flat_rest[:], 0, PACK, PAIR_COLS, M)
-        gather_page(LAST - 1, 0, M)
-        weave(z0[1][:, PAIR_COLS - HALF :, :], flat_rest[:])
-        scatter(LAST, 0, S)
-        wb_q[1] = quantize(wb_woven[1][:], N, "wb1", "wg%d" % (LAST % PACK))
+        scatter_weighted(6)
+        wb_q[0] = quantize(wb_woven[0], N, "wb0", AT_HW)
+        for lo, hi in PIECES:
+            z_pair(nc.gpsimd, 0, lo, hi, recip45[:].rearrange("p (t m) -> p t m", t=2)[:, :, lo:hi])
+        gather_page(6, 0, M)
+        scatter_weighted(7)
+        wb_q[1] = quantize(wb_woven[1], N, "wb1", AT_RECIP - 2 * N)
         for lo in range(0, M, QUARTER):
             gather_page(LAST, lo, lo + QUARTER)
-        finish(0, 0, HALF, z0[0][:], "h_last")
+        finish(0, 0, HALF, z0[0][:], AT_HW + 4 * S)
 
         for lo, hi in PIECES[:2]:
             woven = z_on_vector(lo, hi)

@@ -27,20 +27,23 @@ LAST = TILES - 1
 BANKS = 8
 HALF = 512
 QUARTER = 256
+PAGE_BUFS = 4
 ROWS = A * 16
 ROW0 = 48
-AT_PAGES = 4 * T
-AT_WG = AT_PAGES + 4 * 4 * T2
+EARLY = HALF + P
+LATE = S + H - EARLY
+AT_LATE = 4 * T
+AT_PAGES = AT_LATE + A * LATE
+AT_WG = AT_PAGES + PAGE_BUFS * 4 * T2
 AT_W1 = AT_WG + PACK * 4 * S
-AT_PLANES1 = AT_W1 + A * 2 * PASS
-AT_GAIN = AT_PLANES1 + A * PASS
-AT_END = AT_GAIN + 64
+AT_GAIN = AT_W1 + A * 2 * PASS
+AT_TAB1 = AT_GAIN + 64
+AT_END = AT_TAB1 + 4 * T
 AT_HW = AT_END
 AT_RECIP = AT_HW + 2 * 4 * S
 AT_Z1 = AT_RECIP + 2 * 4 * M
 AT_Z0 = AT_Z1 + 2 * PACK * M
 STRIPE = 16
-PAGE_BUFS = 4
 PIECES = [(0, 256), (256, 512), (512, 768), (768, 896), (896, 1024)]
 
 
@@ -71,15 +74,18 @@ def tile_list_seller_trust_cache_kernel(
 
         tab_scale_win = keep.tile([P, T], U8, name="tab_scale_win", align_bytes=64)
         w_scale_raw = keep.tile([P, H], U8, name="w_scale_raw", align_bytes=64)
-        planes = keep.tile([P, A, S + PASS], U8, name="planes", align_bytes=64)
+        planes = keep.tile([P, A, EARLY], U8, name="planes", align_bytes=64)
         for rows in (slice(0, ROW0), slice(ROW0 + ROWS, P)):
             nc.vector.memset(tab_scale_win[rows, :].bitcast(I32), 0)
             nc.vector.memset(w_scale_raw[rows, :].bitcast(I32), 0)
         nc.vector.memset(planes[:].bitcast(I32), 0)
 
+        second_page = AT_PAGES + 4 * T2
         tab = [
-            placed.tile([P, AT_END // 4], I32, name="tab0", offset=0, align_bytes=64)[:, :T],
-            keep.tile([P, T], I32, name="tab1", tag="big1", align_bytes=64)[:],
+            placed.tile([P, second_page // 4], I32, name="tab0", offset=0, align_bytes=64)[:, :T],
+            placed.tile([P, (AT_END - second_page) // 4], I32, name="tab1", offset=second_page, align_bytes=64)[
+                :, (AT_TAB1 - second_page) // 4 :
+            ],
             keep.tile([P, T], I32, name="tab2", tag="big2", align_bytes=64)[:],
         ]
 
@@ -131,19 +137,16 @@ def tile_list_seller_trust_cache_kernel(
         load_wg(0, 0, HALF, wg_first)
         load_tab(2)
         load_page(0)
-        load_wg(0, HALF, S)
-        load_page(1)
-        load_wg(1, 0, S)
-        load_w(1)
-        for e in range(2):
-            nc.sync.dma_start(out=gain_sb[e:P:2, :, 0 : 2 * PACK - 1], in_=gain_rows[:, :, e : e + 2 * PACK - 1])
 
         v_scale = keep.tile([P, S], U8, name="v_scale", tag="v_codes0_0", align_bytes=64)
         staged_scales = keep.tile([P, S + H], U8, name="staged_scales", align_bytes=64)
         nc.vector.tensor_copy(v_scale[:], tab_scale_win[:].indirect(list1[:]))
-        nc.vector.tensor_copy(staged_scales[:, :S].bitcast(I32), v_scale[:].bitcast(I32))
         nc.vector.tensor_copy(
-            staged_scales[:, S:].bitcast(U16).rearrange("p (b t c i) -> p b c t i", b=B, t=PACK, i=8),
+            staged_scales[:].bitcast(I32).rearrange("p (r w) -> p r w", r=4)[:, 0:4:3, :],
+            v_scale[:].bitcast(I32).rearrange("p (r w) -> p r w", r=2),
+        )
+        nc.vector.tensor_copy(
+            staged_scales[:, HALF : HALF + H].bitcast(U16).rearrange("p (b t c i) -> p b c t i", b=B, t=PACK, i=8),
             w_scale_raw[:].bitcast(U16).rearrange("p (b c i t) -> p b c t i", b=B, i=8, t=PACK),
         )
 
@@ -155,7 +158,7 @@ def tile_list_seller_trust_cache_kernel(
                     in_=staged_scales[first : first + 4 * A, lo:hi].bitcast(I32),
                 )
 
-        move_scales(nc.scalar, planes, 0, S + PASS)
+        move_scales(nc.scalar, planes, 0, EARLY)
 
         w_codes = {}
 
@@ -176,10 +179,21 @@ def tile_list_seller_trust_cache_kernel(
 
         order_w_codes(0, nc.vector)
         gather_words(0, 0, S)
-        planes1 = placed.tile([P, A, PASS], U8, name="planes1", offset=AT_PLANES1, align_bytes=64)
-        nc.vector.memset(planes1[:].bitcast(I32), 0)
-        w_scale = [planes[:, :, S:], planes1[:]]
-        move_scales(nc.sync, planes1, S + PASS, S + H)
+        late = placed.tile([P, A, LATE], U8, name="late", offset=AT_LATE, align_bytes=64)
+        nc.vector.memset(late[:].bitcast(I32), 0)
+        move_scales(nc.sync, late, EARLY, S + H)
+
+        def scales(a, lo, hi):
+            if hi <= EARLY:
+                return planes[:, a, lo:hi]
+            return late[:, a, lo - EARLY : hi - EARLY]
+
+        load_wg(0, HALF, S)
+        load_page(1)
+        load_wg(1, 0, S)
+        load_w(1)
+        for e in range(2):
+            nc.sync.dma_start(out=gain_sb[e:P:2, :, 0 : 2 * PACK - 1], in_=gain_rows[:, :, e : e + 2 * PACK - 1])
         load_page(3)
         load_wg(3, 0, S)
         load_page(2)
@@ -198,7 +212,7 @@ def tile_list_seller_trust_cache_kernel(
         x_pass = [arena[:, :z_start], arena[:, x1_start:]]
         h_start = {1: 0, 2: z_start - HALF, 4: x1_start + S, 5: z_end - QUARTER, 6: x1_start + 2 * S}
 
-        recip0 = keep.tile([P, PACK * M], F32, name="recip0", tag="big1", align_bytes=64)
+        recip0 = placed.tile([P, PACK * M], F32, name="recip0", offset=AT_TAB1, align_bytes=64)
         recip45 = placed.tile([P, 2 * M], F32, name="recip45", offset=AT_RECIP, align_bytes=64)
         recip67 = {
             lo: keep.tile([P, 2 * (hi - lo)], F32, name="recip67", tag="recip1_%d" % lo, align_bytes=64)
@@ -240,9 +254,9 @@ def tile_list_seller_trust_cache_kernel(
                     nc.tensor.matmul_mx(
                         out=acc[:],
                         lhsT=w_codes[b][:, a, t, :].bitcast(FP4X4),
-                        lhsT_scale=w_scale[b][:, a, t * P : (t + 1) * P],
+                        lhsT_scale=scales(a, HALF + i * P, HALF + (i + 1) * P),
                         rhs=v_codes[a, half].bitcast(FP8X4),
-                        rhs_scale=planes[:, a, half * HALF : (half + 1) * HALF],
+                        rhs_scale=scales(a, half * (HALF + H), half * (HALF + H) + HALF),
                         start=(a == order[0]),
                         stop=(a == order[-1]),
                     )
@@ -355,17 +369,17 @@ def tile_list_seller_trust_cache_kernel(
         staged = keep.tile([P, BANKS * HALF], F32, name="staged", tag="big2", align_bytes=64)
 
         def banks_of(lo, hi):
-            per_bank = HALF // (hi - lo)
-            return [(lo // P + g, range(g * per_bank, (g + 1) * per_bank)) for g in range(N // P // per_bank)]
+            first = 2 * PIECES.index((lo, hi))
+            return [((first + g) % BANKS, range(2 * g, 2 * g + 2)) for g in range(2)]
 
         def second_product(b, lo, hi, codes, scale):
             width = hi - lo
             for number, blocks in banks_of(lo, hi):
                 if b == 0:
-                    out_acc[number] = bank(number, "acc_out")
+                    out_acc[lo, number] = bank(number, "acc_out")
                 for s, n in enumerate(blocks):
                     nc.tensor.matmul_mx(
-                        out=out_acc[number][:, s * width : (s + 1) * width],
+                        out=out_acc[lo, number][:, s * width : (s + 1) * width],
                         lhsT=wb_q[b][0][:, n * P : (n + 1) * P].bitcast(FP8X4),
                         lhsT_scale=wb_q[b][1][:, n * P : (n + 1) * P],
                         rhs=codes.bitcast(FP8X4),
@@ -375,14 +389,14 @@ def tile_list_seller_trust_cache_kernel(
                     )
 
         def store(lo, hi):
-            for number, blocks in banks_of(lo, hi):
-                res = staged[:, number * HALF : (number + 1) * HALF]
-                if number >= BANKS - 4 and number % 2 == 1:
-                    nc.vector.tensor_copy(res, out_acc[number][:])
+            width = 2 * (hi - lo)
+            for g, (number, blocks) in enumerate(banks_of(lo, hi)):
+                res = staged[:, PACK * lo + g * width : PACK * lo + (g + 1) * width]
+                if (lo, hi) == PIECES[-1] or ((lo, hi) == PIECES[-2] and g == 1):
+                    nc.vector.tensor_copy(res, out_acc[lo, number][:, :width])
                 else:
-                    nc.scalar.copy(res, out_acc[number][:])
-                queue = nc.scalar if number == BANKS - 2 else nc.sync
-                queue.dma_start(
+                    nc.scalar.copy(res, out_acc[lo, number][:, :width])
+                nc.sync.dma_start(
                     out=out_rows[:, blocks[0] : blocks[-1] + 1, lo:hi],
                     in_=res.rearrange("p (s w) -> p s w", s=len(blocks)),
                 )

@@ -131,11 +131,11 @@ def tile_list_seller_trust_cache_kernel(
             )
         nc.sync.dma_start(list1[:], offs)
         load_w(0)
+        load_tab(1)
         nc.sync.dma_start(list2[:], offs2)
         nc.sync.dma_start(list3[:], offs3)
-        load_tab(1)
-        load_wg(0, 0, HALF, wg_first)
         load_tab(2)
+        load_wg(0, 0, HALF, wg_first)
         load_page(0)
 
         v_scale = keep.tile([P, S], U8, name="v_scale", tag="v_codes0_0", align_bytes=64)

@@ -33,7 +33,8 @@ ROW0 = 48
 EARLY = HALF + P
 LATE = S + H - EARLY
 AT_LATE = 4 * T
-AT_PAGES = AT_LATE + A * LATE
+AT_WG0 = AT_LATE + A * LATE
+AT_PAGES = AT_WG0 + 4 * HALF
 AT_WG = AT_PAGES + PAGE_BUFS * 4 * T2
 AT_W1 = AT_WG + PACK * 4 * S
 AT_GAIN = AT_W1 + A * 2 * PASS
@@ -43,6 +44,8 @@ AT_HW = AT_END
 AT_RECIP = AT_HW + 2 * 4 * S
 AT_Z1 = AT_RECIP + 2 * 4 * M
 AT_Z0 = AT_Z1 + 2 * PACK * M
+AT_TAB2 = AT_Z0 + 2 * PACK * M
+AT_V0 = AT_TAB2 + 4 * T
 STRIPE = 16
 PIECES = [(0, 256), (256, 512), (512, 768), (768, 896), (896, 1024)]
 
@@ -73,7 +76,7 @@ def tile_list_seller_trust_cache_kernel(
             return lst[:, lo // STRIPE : hi // STRIPE]
 
         tab_scale_win = keep.tile([P, T], U8, name="tab_scale_win", align_bytes=64)
-        w_scale_raw = keep.tile([P, H], U8, name="w_scale_raw", align_bytes=64)
+        w_scale_raw = placed.tile([P, H], U8, name="w_scale_raw", offset=AT_V0 - HALF - H, align_bytes=64)
         planes = keep.tile([P, A, EARLY], U8, name="planes", align_bytes=64)
         for rows in (slice(0, ROW0), slice(ROW0 + ROWS, P)):
             nc.vector.memset(tab_scale_win[rows, :].bitcast(I32), 0)
@@ -86,11 +89,12 @@ def tile_list_seller_trust_cache_kernel(
             placed.tile([P, (AT_END - second_page) // 4], I32, name="tab1", offset=second_page, align_bytes=64)[
                 :, (AT_TAB1 - second_page) // 4 :
             ],
-            keep.tile([P, T], I32, name="tab2", tag="big2", align_bytes=64)[:],
+            placed.tile([P, T], I32, name="tab2", offset=AT_TAB2, align_bytes=64)[:],
         ]
 
-        def load_tab(a):
-            nc.sync.dma_start(out=tab[a], in_=tab_words[a].rearrange("p n t -> p (n t)").bitcast(I32))
+        def load_tab(a, lo=0, hi=T):
+            words = tab_words[a].rearrange("p n t -> p (n t)").bitcast(I32)
+            nc.sync.dma_start(out=tab[a][:, lo:hi], in_=words[:, lo:hi])
 
         pairs = PASS // 2
         w_raw = [
@@ -108,7 +112,7 @@ def tile_list_seller_trust_cache_kernel(
         ]
         wgs_rows = wgs.rearrange("(u t e) j -> t u e j", t=PACK, e=2)
 
-        wg_first = keep.tile([P, HALF], F32, name="wg_first", align_bytes=64)
+        wg_first = placed.tile([P, HALF], F32, name="wg_first", offset=AT_WG0, align_bytes=64)
 
         def load_wg(t, lo, hi, tile=None):
             for q in (0, 2, 1, 3):
@@ -124,41 +128,43 @@ def tile_list_seller_trust_cache_kernel(
         gain_rows = gain.rearrange("(b u w) -> u b w", b=B, w=2 * PACK)
         gain_sb = placed.tile([P, B, 2 * PACK], F32, name="gain_sb", offset=AT_GAIN, align_bytes=64)
 
-        load_tab(0)
+        load_tab(0, 0, T // 2)
         for tile, rows in ((tab_scale_win, tab_scales), (w_scale_raw, w4_scales)):
             nc.sync.dma_start(
                 out=tile[ROW0 : ROW0 + ROWS, :].bitcast(I32), in_=rows.rearrange("a q n -> q a n").bitcast(I32)
             )
         nc.sync.dma_start(list1[:], offs)
+        load_tab(0, T // 2, T)
         load_w(0)
         load_tab(1)
         nc.sync.dma_start(list2[:], offs2)
         nc.sync.dma_start(list3[:], offs3)
-        load_tab(2)
-        load_wg(0, 0, HALF, wg_first)
-        load_page(0)
 
-        v_scale = keep.tile([P, S], U8, name="v_scale", tag="v_codes0_0", align_bytes=64)
         staged_scales = keep.tile([P, S + H], U8, name="staged_scales", align_bytes=64)
-        nc.vector.tensor_copy(v_scale[:], tab_scale_win[:].indirect(list1[:]))
-        nc.vector.tensor_copy(
-            staged_scales[:].bitcast(I32).rearrange("p (r w) -> p r w", r=4)[:, 0:4:3, :],
-            v_scale[:].bitcast(I32).rearrange("p (r w) -> p r w", r=2),
+
+        def stage_v_scales(half, v_scale):
+            nc.vector.tensor_copy(v_scale, tab_scale_win[:].indirect(entries(list1, half * HALF, (half + 1) * HALF)))
+            first = half * (HALF + H)
+            nc.vector.tensor_copy(staged_scales[:, first : first + HALF].bitcast(I32), v_scale.bitcast(I32))
+
+        stage_v_scales(
+            0, placed.tile([P, 2 * HALF], U8, name="v_scale0", offset=AT_V0 - HALF, align_bytes=64)[:, :HALF]
         )
         nc.vector.tensor_copy(
             staged_scales[:, HALF : HALF + H].bitcast(U16).rearrange("p (b t c i) -> p b c t i", b=B, t=PACK, i=8),
             w_scale_raw[:].bitcast(U16).rearrange("p (b c i t) -> p b c t i", b=B, i=8, t=PACK),
         )
 
-        def move_scales(queue, target, lo, hi):
+        def move_scales(queues, target, lo, hi):
             for q in (0, 2, 1, 3):
                 first = ROW0 + 4 * A * q
-                queue.dma_start(
+                queues[q % 2].dma_start(
                     out=target[QUAD * q : QUAD * q + 4, :, :].bitcast(I32),
                     in_=staged_scales[first : first + 4 * A, lo:hi].bitcast(I32),
                 )
 
-        move_scales(nc.scalar, planes, 0, EARLY)
+        move_scales((nc.sync, nc.scalar), planes, 0, EARLY)
+        load_tab(2)
 
         w_codes = {}
 
@@ -172,16 +178,22 @@ def tile_list_seller_trust_cache_kernel(
         v_codes = {}
 
         def gather_words(a, lo, hi):
-            picked = keep.tile([P, hi - lo], U32, name="picked", tag="v_codes%d_%d" % (a, lo), align_bytes=64)
+            if a == 0:
+                picked = placed.tile([P, hi - lo], U32, name="picked0", offset=AT_V0, align_bytes=64)
+            else:
+                picked = keep.tile([P, hi - lo], U32, name="picked", tag="v_codes%d_%d" % (a, lo), align_bytes=64)
             nc.vector.tensor_copy(picked[:], tab[a].bitcast(U32).indirect(entries(list1, lo, hi)))
             for c in range(lo, hi, HALF):
                 v_codes[a, c // HALF] = picked[:, c - lo : c - lo + HALF]
 
-        order_w_codes(0, nc.vector)
         gather_words(0, 0, S)
+        load_wg(0, 0, HALF, wg_first)
+        load_page(0)
+        order_w_codes(0, nc.vector)
+        stage_v_scales(1, keep.tile([P, HALF], U8, name="v_scale1", align_bytes=64)[:])
         late = placed.tile([P, A, LATE], U8, name="late", offset=AT_LATE, align_bytes=64)
         nc.vector.memset(late[:].bitcast(I32), 0)
-        move_scales(nc.sync, late, EARLY, S + H)
+        move_scales((nc.sync, nc.sync), late, EARLY, S + H)
 
         def scales(a, lo, hi):
             if hi <= EARLY:
@@ -366,7 +378,7 @@ def tile_list_seller_trust_cache_kernel(
 
         out_rows = out.rearrange("(n p) m -> p n m", p=P)
         out_acc = {}
-        staged = keep.tile([P, BANKS * HALF], F32, name="staged", tag="big2", align_bytes=64)
+        staged = placed.tile([P, BANKS * HALF], F32, name="staged", offset=AT_TAB2, align_bytes=64)
 
         def banks_of(lo, hi):
             first = 2 * PIECES.index((lo, hi))

@@ -27,25 +27,34 @@ LAST = TILES - 1
 BANKS = 8
 HALF = 512
 QUARTER = 256
-PAGE_BUFS = 4
 ROWS = A * 16
 ROW0 = 48
 EARLY = HALF + P
 LATE = S + H - EARLY
 AT_LATE = 4 * T
 AT_WG0 = AT_LATE + A * LATE
-AT_PAGES = AT_WG0 + 4 * HALF
-AT_WG = AT_PAGES + PAGE_BUFS * 4 * T2
+AT_PAGE0 = AT_WG0 + 4 * HALF
+AT_PAGE1 = AT_PAGE0 + 4 * T2
+AT_WG = AT_PAGE1 + 4 * T2
 AT_W1 = AT_WG + PACK * 4 * S
 AT_GAIN = AT_W1 + A * 2 * PASS
-AT_TAB1 = AT_GAIN + 64
+AT_WB = AT_GAIN + 64
+AT_TAB1 = AT_WB + TILES * 4 * N
 AT_END = AT_TAB1 + 4 * T
-AT_HW = AT_END
-AT_RECIP = AT_HW + 2 * 4 * S
-AT_Z1 = AT_RECIP + 2 * 4 * M
-AT_Z0 = AT_Z1 + 2 * PACK * M
-AT_TAB2 = AT_Z0 + 2 * PACK * M
+AT_TAB2 = AT_END
 AT_V0 = AT_TAB2 + 4 * T
+AT_Z0 = (AT_V0 + 4 * S, AT_V0 + 4 * S + 6 * 1024)
+AT_H7 = AT_Z0[0] + 3 * 1024
+AT_WB1_CODES = AT_Z0[0] + 4 * 1024
+AT_WEIGHTED3 = AT_Z0[1] + 4 * 1024
+AT_WEIGHTED4 = AT_WEIGHTED3 + 4 * S
+AT_WB_WOVEN0 = AT_WEIGHTED4 + 4 * S
+AT_RECIP_A = AT_WB_WOVEN0 + 2 * PACK * N
+AT_RECIP_B = AT_RECIP_A + 2 * 4 * M
+AT_ROOT = AT_RECIP_B + 2 * 4 * M
+AT_Z1 = AT_ROOT + 4 * M
+AT_PAGE = [AT_PAGE0, AT_PAGE1, 0, 4 * T2, AT_TAB1, AT_TAB1 + 4 * T2, AT_TAB2, AT_TAB2 + 4 * T2]
+LAG = 768
 STRIPE = 16
 PIECES = [(0, 256), (256, 512), (512, 768), (768, 896), (896, 1024)]
 
@@ -65,7 +74,6 @@ def tile_list_seller_trust_cache_kernel(
     with ExitStack() as ctx:
         keep = ctx.enter_context(tc.tile_pool(name="keep", bufs=1))
         placed = ctx.enter_context(tc.tile_pool(name="placed", bufs=1))
-        work = ctx.enter_context(tc.tile_pool(name="work", bufs=1))
         psum = ctx.enter_context(tc.psum_pool(name="psum", bufs=1))
 
         list1 = keep.tile([P, S // STRIPE], U16, name="list1")
@@ -83,7 +91,7 @@ def tile_list_seller_trust_cache_kernel(
             nc.vector.memset(w_scale_raw[rows, :].bitcast(I32), 0)
         nc.vector.memset(planes[:].bitcast(I32), 0)
 
-        second_page = AT_PAGES + 4 * T2
+        second_page = AT_PAGE1
         tab = [
             placed.tile([P, second_page // 4], I32, name="tab0", offset=0, align_bytes=64)[:, :T],
             placed.tile([P, (AT_END - second_page) // 4], I32, name="tab1", offset=second_page, align_bytes=64)[
@@ -122,7 +130,7 @@ def tile_list_seller_trust_cache_kernel(
         page = {}
 
         def load_page(i):
-            page[i] = placed.tile([P, T2], F32, name="page", bufs=PAGE_BUFS, offset=AT_PAGES, align_bytes=64)
+            page[i] = placed.tile([P, T2], F32, name="page%d" % i, offset=AT_PAGE[i], align_bytes=64)
             nc.sync.dma_start(out=page[i][:], in_=page_rows[i // PACK, i % PACK])
 
         gain_rows = gain.rearrange("(b u w) -> u b w", b=B, w=2 * PACK)
@@ -200,57 +208,48 @@ def tile_list_seller_trust_cache_kernel(
                 return planes[:, a, lo:hi]
             return late[:, a, lo - EARLY : hi - EARLY]
 
-        load_wg(0, HALF, S)
-        load_page(1)
-        load_wg(1, 0, S)
-        load_w(1)
-        for e in range(2):
-            nc.sync.dma_start(out=gain_sb[e:P:2, :, 0 : 2 * PACK - 1], in_=gain_rows[:, :, e : e + 2 * PACK - 1])
-        load_page(3)
-        load_wg(3, 0, S)
-        load_page(2)
-        load_wg(2, 0, S)
-        load_wg(0, 0, HALF)
+        wb_rows = wb.rearrange("(b u t e) n -> b t u e n", b=B, t=PACK, e=2)
+        wb_raw = placed.tile([P, TILES * N], F32, name="wb_raw", offset=AT_WB, align_bytes=64)
+
+        def load_wb(b):
+            for i in range(b * PACK, (b + 1) * PACK):
+                nc.sync.dma_start(out=wb_raw[:, i * N : (i + 1) * N], in_=wb_rows[b, i % PACK])
+
         gather_words(1, 0, S)
         gather_words(2, 0, HALF)
         gather_words(2, HALF, S)
+        load_wg(0, HALF, S)
+        load_page(1)
+        load_wg(1, 0, S)
+        for e in range(2):
+            nc.sync.dma_start(out=gain_sb[e:P:2, :, 0 : 2 * PACK - 1], in_=gain_rows[:, :, e : e + 2 * PACK - 1])
+        for i in (2, 3):
+            load_page(i)
+            load_wg(i, 0, S)
+        load_wb(0)
+        load_wg(0, 0, HALF)
+        for i in range(PACK, TILES):
+            load_page(i)
+        load_w(1)
+        load_wb(1)
 
         def bank(n, name):
             return psum.tile([P, HALF], F32, name=name, tag="bank%d" % n)
 
-        z_start, z_end = PACK * S, (PACK + 1) * S
-        x1_start = z_end + HALF
-        arena = keep.tile([P, x1_start + PACK * S], F32, name="arena", align_bytes=64)
-        x_pass = [arena[:, :z_start], arena[:, x1_start:]]
-        h_start = {1: 0, 2: z_start - HALF, 4: x1_start + S, 5: z_end - QUARTER, 6: x1_start + 2 * S}
-
-        recip0 = placed.tile([P, PACK * M], F32, name="recip0", offset=AT_TAB1, align_bytes=64)
-        recip45 = placed.tile([P, 2 * M], F32, name="recip45", offset=AT_RECIP, align_bytes=64)
-        recip67 = {
-            lo: keep.tile([P, 2 * (hi - lo)], F32, name="recip67", tag="recip1_%d" % lo, align_bytes=64)
-            for lo, hi in PIECES
-        }
-
-        def recip_parts(i):
-            if i < PACK:
-                return [(0, M, recip0[:, i * M : (i + 1) * M])]
-            if i < PACK + 2:
-                return [(0, M, recip45[:, (i - PACK) * M : (i - PACK + 1) * M])]
-            t = i - PACK - 2
-            return [(lo, hi, recip67[lo][:, t * (hi - lo) : (t + 1) * (hi - lo)]) for lo, hi in PIECES]
-
-        h_own = {
-            0: keep.tile([P, S], F32, name="h_first", tag="w_codes1", align_bytes=64),
-            3: placed.tile([P, S], F32, name="h3", offset=AT_HW + 2 * S, align_bytes=64),
-        }
+        x_start = S + QUARTER
+        arena = keep.tile([P, x_start + TILES * M], F32, name="arena", align_bytes=64)
+        h_start = {i: S + S * i for i in range(2, LAST)}
+        h_start[0] = 2 * S
+        h_start[1] = HALF
+        h_last = placed.tile([P, S], F32, name="h_last", offset=AT_H7, align_bytes=64)
 
         def h_cols(i, lo, hi):
-            if i in h_own:
-                return h_own[i][:, lo:hi]
             if i == LAST:
-                start = x1_start + 3 * S if lo == 0 else z_end
-                return arena[:, start : start + hi - lo]
+                return h_last[:, lo:hi]
             return arena[:, h_start[i] + lo : h_start[i] + hi]
+
+        def x_tiles(i, count):
+            return arena[:, x_start + i * M : x_start + (i + count) * M].rearrange("p (t m) -> p t m", t=count)
 
         h_acc = {}
 
@@ -273,8 +272,7 @@ def tile_list_seller_trust_cache_kernel(
                         stop=(a == order[-1]),
                     )
                 h_acc[i, half] = acc
-                if (i, half) != (LAST, 1):
-                    evacuate(i, half)
+                evacuate(i, half)
 
         def scatter(i, lo, hi):
             weights = wg_first if (i, lo) == (0, 0) else wg[i % PACK]
@@ -284,15 +282,17 @@ def tile_list_seller_trust_cache_kernel(
 
         weighted = {}
 
-        def weigh(i, lo, hi):
-            if lo == 0:
-                weighted[i] = placed.tile(
-                    [P, S], F32, name="weighted%d" % i, offset=AT_HW + 4 * S * (i - LAST + 1), align_bytes=64
-                )
-            nc.gpsimd.tensor_tensor(weighted[i][:, lo:hi], h_cols(i, lo, hi), wg[i % PACK][:, lo:hi], MULT)
+        weighted_at = {3: AT_WEIGHTED3, 4: AT_WEIGHTED4, 5: AT_WB_WOVEN0, 7: AT_WEIGHTED4}
+
+        def weigh(i):
+            if i in weighted_at:
+                weighted[i] = placed.tile([P, S], F32, name="weighted%d" % i, offset=weighted_at[i], align_bytes=64)[:]
+            else:
+                weighted[i] = arena[:, :S]
+            nc.gpsimd.tensor_tensor(weighted[i], h_cols(i, 0, S), wg[i % PACK][:], MULT)
 
         def scatter_weighted(i):
-            nc.vector.tensor_copy(page[i][:].indirect(list2[:]), weighted[i][:])
+            nc.vector.tensor_copy(page[i][:].indirect(list2[:]), weighted[i])
 
         gain_root = keep.tile([P, B, PACK], F32, name="gain_root")
         gain_sign = keep.tile([P, B, PACK], F32, name="gain_sign")
@@ -304,25 +304,41 @@ def tile_list_seller_trust_cache_kernel(
             nc.scalar.activation(gain_sign[:], gains, ACT.Sign)
             nc.scalar.activation(gain_sign[:], gain_sign[:], ACT.Sign, bias=0.5)
 
-        roots = {}
+        recip = {}
 
-        def gather_page(i, lo, hi):
+        def recip67_at(lo):
+            return AT_RECIP_A + 2 * 4 * lo
+
+        def recip_parts(i, lo, hi):
+            if i >= LAST - 1:
+                parts = []
+                for first, end in pieces_in(lo, hi):
+                    width = end - first
+                    if i == LAST - 1:
+                        recip[i, first] = placed.tile(
+                            [P, 2 * width], F32, name="recip67_%d" % first, offset=recip67_at(first), align_bytes=64
+                        )
+                    parts.append((first, end, recip[LAST - 1, first][:, (i % 2) * width : (i % 2 + 1) * width]))
+                return parts
+            pair = i - i % 2
+            if (i, lo) == (pair, 0):
+                at = AT_RECIP_B if pair == 2 else AT_RECIP_A
+                recip[pair] = placed.tile([P, 2 * M], F32, name="recip%d" % pair, offset=at, align_bytes=64)
+            return [(lo, hi, recip[pair][:, (i % 2) * M + lo : (i % 2) * M + hi])]
+
+        def new_root(early):
+            if early:
+                return placed.tile([P, M], F32, name="root_early", offset=AT_ROOT, align_bytes=64)
+            return placed.tile([P, M], F32, name="root", offset=AT_V0, align_bytes=64)
+
+        def gather_page(i, lo, hi, root):
             b, t = divmod(i, PACK)
-            x = x_pass[b][:, t * M + lo : t * M + hi]
-            if lo == 0:
-                roots[i] = work.tile([P, M], F32, name="root")
-            root = roots[i][:, lo:hi]
+            x = x_tiles(i, 1)[:, 0, lo:hi]
             nc.vector.tensor_copy(x, page[i][:].indirect(entries(list3, lo, hi)))
-            size = root
-            if i == PACK + 1:
-                size = placed.tile([P, M], F32, name="size5", offset=AT_Z0 + 2 * M, align_bytes=64)[:]
-            nc.scalar.activation(size, x, ACT.Abs)
-            nc.scalar.activation(root, size, ACT.Abs_reciprocal_sqrt, bias=1.0)
-            for first, end, target in recip_parts(i):
-                if lo <= first and end <= hi:
-                    nc.scalar.activation(
-                        target, root[:, first - lo : end - lo], ACT.Square, scale=gain_root[:, b, t : t + 1]
-                    )
+            nc.scalar.activation(root[:, lo:hi], x, ACT.Abs)
+            nc.scalar.activation(root[:, lo:hi], root[:, lo:hi], ACT.Abs_reciprocal_sqrt, bias=1.0)
+            for first, end, target in recip_parts(i, lo, hi):
+                nc.scalar.activation(target, root[:, first:end], ACT.Square, scale=gain_root[:, b, t : t + 1])
 
         def weave(woven, flat):
             nc.scalar.copy(
@@ -340,8 +356,6 @@ def tile_list_seller_trust_cache_kernel(
             )
             return codes, scale
 
-        wb_rows = wb.rearrange("(b u t e) n -> b t u e n", b=B, t=PACK, e=2)
-        wb_raw = placed.tile([P, TILES * N], F32, name="wb_raw", offset=0, align_bytes=64)
         wb_woven = {}
         wb_q = {}
 
@@ -350,35 +364,36 @@ def tile_list_seller_trust_cache_kernel(
                 rows = wb_raw[:, (b * PACK + t) * N : (b * PACK + t + 1) * N]
                 nc.scalar.activation(rows, rows, ACT.Copy, scale=gain_sign[:, b, t : t + 1])
             if b == 0:
-                wb_woven[b] = placed.tile([P, M, PACK], BF16, name="wb_woven0", offset=AT_Z1, align_bytes=64)[:, :N, :]
+                wb_woven[b] = placed.tile([P, N, PACK], BF16, name="wb_woven0", offset=AT_WB_WOVEN0, align_bytes=64)[:]
             else:
                 wb_woven[b] = keep.tile([P, N, PACK], BF16, name="wb_woven1", align_bytes=64)[:]
             weave(wb_woven[b], by_tile(wb_raw[:, b * PACK * N : (b + 1) * PACK * N]))
 
-        def z_flat(flat, lo, hi):
-            nc.gpsimd.tensor_tensor(flat, by_tile(x_pass[0])[:, :, lo:hi], by_tile(recip0[:])[:, :, lo:hi], MULT)
+        z = {}
 
-        z1 = {}
-
-        def z_pair(engine, t, lo, hi, recip):
+        def z_pair(i, lo, hi, engine=nc.gpsimd):
+            b, t = divmod(i, PACK)
             if t == 0:
-                z1[lo] = placed.tile(
-                    [P, hi - lo, PACK], BF16, name="z1_%d" % lo, offset=AT_Z1 + 2 * PACK * lo, align_bytes=64
-                )
+                at = AT_Z0[lo // HALF] if b == 0 else AT_Z1 + 2 * PACK * lo
+                z[b, lo] = placed.tile([P, hi - lo, PACK], BF16, name="z%d_%d" % (b, lo), offset=at, align_bytes=64)
+            if i == LAST - 1:
+                factor = recip[i, lo][:].rearrange("p (t m) -> p t m", t=2)
+            else:
+                factor = recip[i][:].rearrange("p (t m) -> p t m", t=2)[:, :, lo:hi]
             engine.tensor_tensor(
-                z1[lo][:, :, t : t + 2].rearrange("p (c i) t -> p c t i", i=2),
-                by_tile(x_pass[1])[:, t : t + 2, lo:hi].rearrange("p t (c i) -> p c t i", i=2),
-                recip.rearrange("p t (c i) -> p c t i", i=2),
+                z[b, lo][:, :, t : t + 2].rearrange("p (c i) t -> p c t i", i=2),
+                x_tiles(i, 2)[:, :, lo:hi].rearrange("p t (c i) -> p c t i", i=2),
+                factor.rearrange("p t (c i) -> p c t i", i=2),
                 MULT,
             )
-            return z1[lo][:]
 
         def z_on_vector(lo, hi):
-            return z_pair(nc.vector, 2, lo, hi, recip67[lo][:].rearrange("p (t m) -> p t m", t=2))
+            z_pair(LAST - 1, lo, hi, nc.vector)
+            return z[1, lo][:]
 
         out_rows = out.rearrange("(n p) m -> p n m", p=P)
         out_acc = {}
-        staged = placed.tile([P, BANKS * HALF], F32, name="staged", offset=AT_TAB2, align_bytes=64)
+        staged = placed.tile([P, BANKS * HALF], F32, name="staged", offset=AT_WB, align_bytes=64)
 
         def banks_of(lo, hi):
             first = 2 * PIECES.index((lo, hi))
@@ -420,69 +435,58 @@ def tile_list_seller_trust_cache_kernel(
                 if b == B - 1:
                     store(first, end)
 
-        for i in (0, 1, 3, 2):
+        for i in range(PACK):
             first_product(i)
         scatter(0, 0, HALF)
         scatter(0, HALF, S)
         scatter(1, 0, S)
+        split_gain()
+        gather_page(0, 0, M, new_root(True))
+        gather_page(1, 0, LAG, new_root(True))
+        weigh(2)
+        weigh(3)
+        weave_wb(0)
         order_w_codes(1, nc.gpsimd)
         for i in range(PACK, TILES):
             first_product(i)
-        for i in range(TILES):
-            nc.sync.dma_start(out=wb_raw[:, i * N : (i + 1) * N], in_=wb_rows[i // PACK, i % PACK])
-        split_gain()
-        gather_page(0, 0, M)
-        gather_page(1, 0, M)
-
-        weave_wb(0)
-        load_page(4)
-        load_page(5)
-        scatter(3, 0, S)
-        scatter(2, 0, S)
-        weigh(6, 0, S)
-        weigh(7, 0, HALF)
-        gather_page(3, 0, M)
-        gather_page(2, 0, M)
         weave_wb(1)
-        load_page(6)
-        load_page(7)
-        scatter(4, 0, S)
-        scatter(5, 0, S)
-        evacuate(LAST, 1)
-        flat = [
-            by_tile(placed.tile([P, PACK * HALF], BF16, name="flat_a", offset=AT_WG + 4 * S, align_bytes=64)[:]),
-            by_tile(arena[:, z_start:z_end].bitcast(BF16)),
-        ]
-        for half in range(2):
-            z_flat(flat[half], half * HALF, (half + 1) * HALF)
-        weigh(7, HALF, S)
-        gather_page(4, 0, M)
-        gather_page(5, 0, M)
-        z0 = [
-            placed.tile([P, HALF, PACK], BF16, name="z0_%d" % half, offset=AT_Z0 + 4 * M * half, align_bytes=64)
-            for half in range(2)
-        ]
-        for half in range(2):
-            weave(z0[half][:], flat[half])
+        for i in range(2, LAST):
+            scatter_weighted(i)
+            if i == PACK:
+                weigh(LAST)
+                for lo in (0, HALF):
+                    z_pair(0, lo, lo + HALF)
+            gather_page(i - 1, LAG, M, new_root(False))
+            if i < LAST - 1:
+                gather_page(i, 0, LAG, new_root(False))
+            if i == 3:
+                wb_q[0] = quantize(wb_woven[0], N, "wb0", AT_WEIGHTED3)
+                for j in range(PACK, LAST):
+                    weigh(j)
+            if i == PACK:
+                for lo in (0, HALF):
+                    z_pair(2, lo, lo + HALF)
+            if i == PACK + 1:
+                for lo, hi in pieces_in(0, LAG):
+                    z_pair(PACK, lo, hi)
+        for lo, hi in pieces_in(LAG, M):
+            z_pair(PACK, lo, hi)
+        gather_page(LAST - 1, 0, M, new_root(False))
 
-        scatter_weighted(6)
-        wb_q[0] = quantize(wb_woven[0], N, "wb0", AT_HW)
-        for lo, hi in PIECES:
-            z_pair(nc.gpsimd, 0, lo, hi, recip45[:].rearrange("p (t m) -> p t m", t=2)[:, :, lo:hi])
-        gather_page(6, 0, M)
-        scatter_weighted(7)
-        wb_q[1] = quantize(wb_woven[1], N, "wb1", AT_RECIP - 2 * N)
+        scatter_weighted(LAST)
+        wb_q[1] = quantize(wb_woven[1], N, "wb1", AT_WB1_CODES)
+        root = new_root(False)
         for lo in range(0, M, QUARTER):
-            gather_page(LAST, lo, lo + QUARTER)
-        finish(0, 0, HALF, z0[0][:], AT_HW + 4 * S)
+            gather_page(LAST, lo, lo + QUARTER, root)
+        finish(0, 0, HALF, z[0, 0][:], AT_WEIGHTED4)
 
         for lo, hi in PIECES[:2]:
             woven = z_on_vector(lo, hi)
-            finish(0, HALF + lo, HALF + hi, z0[1][:, lo:hi, :], "recip1_%d" % lo)
+            finish(0, HALF + lo, HALF + hi, z[0, HALF][:, lo:hi, :], recip67_at(lo))
             finish(1, lo, hi, woven, None)
         woven = z_on_vector(*PIECES[2])
         for (lo, hi), following in zip(PIECES[2:], PIECES[3:]):
             woven_next = z_on_vector(*following)
-            finish(1, lo, hi, woven, "recip1_%d" % following[0])
+            finish(1, lo, hi, woven, recip67_at(following[0]))
             woven = woven_next
         finish(1, *PIECES[-1], woven, None)

@@ -38,8 +38,11 @@ AT_PAGE1 = AT_PAGE0 + 4 * T2
 AT_WG = AT_PAGE1 + 4 * T2
 AT_W1 = AT_WG + PACK * 4 * S
 AT_GAIN = AT_W1 + A * 2 * PASS
-AT_WB = AT_GAIN + 64
-AT_TAB1 = AT_WB + TILES * 4 * N
+AT_ROOT = AT_GAIN + 64
+ROOT_BYTES = 6 * 1024
+AT_WB = AT_ROOT + ROOT_BYTES
+AT_WEIGHTED7 = AT_WB + TILES * 4 * N - 64
+AT_TAB1 = AT_WEIGHTED7 + 4 * S
 AT_END = AT_TAB1 + 4 * T
 AT_TAB2 = AT_END
 AT_V0 = AT_TAB2 + 4 * T
@@ -51,8 +54,7 @@ AT_WEIGHTED4 = AT_WEIGHTED3 + 4 * S
 AT_WB_WOVEN0 = AT_WEIGHTED4 + 4 * S
 AT_RECIP_A = AT_WB_WOVEN0 + 2 * PACK * N
 AT_RECIP_B = AT_RECIP_A + 2 * 4 * M
-AT_ROOT = AT_RECIP_B + 2 * 4 * M
-AT_Z1 = AT_ROOT + 4 * M
+AT_Z1 = AT_RECIP_B + 2 * 4 * M
 AT_PAGE = [AT_PAGE0, AT_PAGE1, 0, 4 * T2, AT_TAB1, AT_TAB1 + 4 * T2, AT_TAB2, AT_TAB2 + 4 * T2]
 LAG = 768
 STRIPE = 16
@@ -209,11 +211,14 @@ def tile_list_seller_trust_cache_kernel(
             return late[:, a, lo - EARLY : hi - EARLY]
 
         wb_rows = wb.rearrange("(b u t e) n -> b t u e n", b=B, t=PACK, e=2)
-        wb_raw = placed.tile([P, TILES * N], F32, name="wb_raw", offset=AT_WB, align_bytes=64)
+        wb_raw = [
+            placed.tile([P, PACK * N], F32, name="wb_raw%d" % b, offset=AT_WB + (B - 1 - b) * PACK * 4 * N, align_bytes=64)
+            for b in range(B)
+        ]
 
         def load_wb(b):
-            for i in range(b * PACK, (b + 1) * PACK):
-                nc.sync.dma_start(out=wb_raw[:, i * N : (i + 1) * N], in_=wb_rows[b, i % PACK])
+            for t in range(PACK):
+                nc.sync.dma_start(out=wb_raw[b][:, t * N : (t + 1) * N], in_=wb_rows[b, t])
 
         gather_words(1, 0, S)
         gather_words(2, 0, HALF)
@@ -226,11 +231,13 @@ def tile_list_seller_trust_cache_kernel(
         for i in (2, 3):
             load_page(i)
             load_wg(i, 0, S)
-        load_wb(0)
         load_wg(0, 0, HALF)
-        for i in range(PACK, TILES):
-            load_page(i)
+        load_page(4)
+        load_page(5)
         load_w(1)
+        load_page(6)
+        load_page(7)
+        load_wb(0)
         load_wb(1)
 
         def bank(n, name):
@@ -282,7 +289,7 @@ def tile_list_seller_trust_cache_kernel(
 
         weighted = {}
 
-        weighted_at = {3: AT_WEIGHTED3, 4: AT_WEIGHTED4, 5: AT_WB_WOVEN0, 7: AT_WEIGHTED4}
+        weighted_at = {3: AT_WEIGHTED3, 4: AT_WEIGHTED4, 6: AT_WEIGHTED3, 7: AT_WEIGHTED7}
 
         def weigh(i):
             if i in weighted_at:
@@ -326,19 +333,21 @@ def tile_list_seller_trust_cache_kernel(
                 recip[pair] = placed.tile([P, 2 * M], F32, name="recip%d" % pair, offset=at, align_bytes=64)
             return [(lo, hi, recip[pair][:, (i % 2) * M + lo : (i % 2) * M + hi])]
 
-        def new_root(early):
-            if early:
-                return placed.tile([P, M], F32, name="root_early", offset=AT_ROOT, align_bytes=64)
-            return placed.tile([P, M], F32, name="root", offset=AT_V0, align_bytes=64)
+        def new_root(stage):
+            at, width = ((AT_ROOT, M), (AT_V0, M), (AT_ROOT, (ROOT_BYTES + 64) // 4))[stage]
+            return placed.tile([P, width], F32, name="root%d" % stage, offset=at, align_bytes=64)
 
-        def gather_page(i, lo, hi, root):
+        def gather_page(i, lo, hi, root, origin=0):
             b, t = divmod(i, PACK)
             x = x_tiles(i, 1)[:, 0, lo:hi]
             nc.vector.tensor_copy(x, page[i][:].indirect(entries(list3, lo, hi)))
-            nc.scalar.activation(root[:, lo:hi], x, ACT.Abs)
-            nc.scalar.activation(root[:, lo:hi], root[:, lo:hi], ACT.Abs_reciprocal_sqrt, bias=1.0)
+            part = root[:, lo - origin : hi - origin]
+            nc.scalar.activation(part, x, ACT.Abs)
+            nc.scalar.activation(part, part, ACT.Abs_reciprocal_sqrt, bias=1.0)
             for first, end, target in recip_parts(i, lo, hi):
-                nc.scalar.activation(target, root[:, first:end], ACT.Square, scale=gain_root[:, b, t : t + 1])
+                nc.scalar.activation(
+                    target, root[:, first - origin : end - origin], ACT.Square, scale=gain_root[:, b, t : t + 1]
+                )
 
         def weave(woven, flat):
             nc.scalar.copy(
@@ -361,13 +370,13 @@ def tile_list_seller_trust_cache_kernel(
 
         def weave_wb(b):
             for t in range(PACK):
-                rows = wb_raw[:, (b * PACK + t) * N : (b * PACK + t + 1) * N]
+                rows = wb_raw[b][:, t * N : (t + 1) * N]
                 nc.scalar.activation(rows, rows, ACT.Copy, scale=gain_sign[:, b, t : t + 1])
             if b == 0:
                 wb_woven[b] = placed.tile([P, N, PACK], BF16, name="wb_woven0", offset=AT_WB_WOVEN0, align_bytes=64)[:]
             else:
                 wb_woven[b] = keep.tile([P, N, PACK], BF16, name="wb_woven1", align_bytes=64)[:]
-            weave(wb_woven[b], by_tile(wb_raw[:, b * PACK * N : (b + 1) * PACK * N]))
+            weave(wb_woven[b], by_tile(wb_raw[b][:]))
 
         z = {}
 
@@ -386,10 +395,6 @@ def tile_list_seller_trust_cache_kernel(
                 factor.rearrange("p t (c i) -> p c t i", i=2),
                 MULT,
             )
-
-        def z_on_vector(lo, hi):
-            z_pair(LAST - 1, lo, hi, nc.vector)
-            return z[1, lo][:]
 
         out_rows = out.rearrange("(n p) m -> p n m", p=P)
         out_acc = {}
@@ -428,12 +433,18 @@ def tile_list_seller_trust_cache_kernel(
                     in_=res.rearrange("p (s w) -> p s w", s=len(blocks)),
                 )
 
-        def finish(b, lo, hi, woven, behind):
-            codes, scale = quantize(woven, hi - lo, "z%d_%d" % (b, lo), behind)
+        def multiply(b, lo, hi, quantized):
+            codes, scale = quantized
             for first, end in pieces_in(lo, hi):
                 second_product(b, first, end, codes[:, first - lo : end - lo], scale[:, first - lo : end - lo])
                 if b == B - 1:
                     store(first, end)
+
+        def quantize_z(b, lo, hi, behind):
+            return quantize(z[b, lo][:], hi - lo, "z%d_%d" % (b, lo), behind)
+
+        def finish(lo, hi, behind=None):
+            multiply(1, lo, hi, quantize_z(1, lo, hi, behind))
 
         for i in range(PACK):
             first_product(i)
@@ -441,52 +452,54 @@ def tile_list_seller_trust_cache_kernel(
         scatter(0, HALF, S)
         scatter(1, 0, S)
         split_gain()
-        gather_page(0, 0, M, new_root(True))
-        gather_page(1, 0, LAG, new_root(True))
+        gather_page(0, 0, M, new_root(0))
+        gather_page(1, 0, LAG, new_root(0))
         weigh(2)
         weigh(3)
-        weave_wb(0)
         order_w_codes(1, nc.gpsimd)
         for i in range(PACK, TILES):
             first_product(i)
+        weave_wb(0)
         weave_wb(1)
         for i in range(2, LAST):
             scatter_weighted(i)
-            if i == PACK:
-                weigh(LAST)
-                for lo in (0, HALF):
-                    z_pair(0, lo, lo + HALF)
-            gather_page(i - 1, LAG, M, new_root(False))
-            if i < LAST - 1:
-                gather_page(i, 0, LAG, new_root(False))
+            if i == 2:
+                weigh(4)
+                weigh(5)
             if i == 3:
-                wb_q[0] = quantize(wb_woven[0], N, "wb0", AT_WEIGHTED3)
-                for j in range(PACK, LAST):
-                    weigh(j)
-            if i == PACK:
+                weigh(6)
+                weigh(7)
+            gather_page(i - 1, LAG, M, new_root(1 if i == 2 else 2))
+            if i in (3, 4):
                 for lo in (0, HALF):
-                    z_pair(2, lo, lo + HALF)
+                    z_pair(2 * (i - 3), lo, lo + HALF)
+            if i < LAST - 1:
+                gather_page(i, 0, LAG, new_root(1 if i == 2 else 2))
             if i == PACK + 1:
                 for lo, hi in pieces_in(0, LAG):
                     z_pair(PACK, lo, hi)
         for lo, hi in pieces_in(LAG, M):
             z_pair(PACK, lo, hi)
-        gather_page(LAST - 1, 0, M, new_root(False))
+        gather_page(LAST - 1, 0, M, new_root(2))
 
         scatter_weighted(LAST)
-        wb_q[1] = quantize(wb_woven[1], N, "wb1", AT_WB1_CODES)
-        root = new_root(False)
-        for lo in range(0, M, QUARTER):
-            gather_page(LAST, lo, lo + QUARTER, root)
-        finish(0, 0, HALF, z[0, 0][:], AT_WEIGHTED4)
+        wb_q[0] = quantize(wb_woven[0], N, "wb0", AT_WB1_CODES)
+        root_at = [AT_ROOT + 1024 * n for n in (0, 2, 4, 5)]
+        for n, at in enumerate(root_at):
+            root = placed.tile([P, QUARTER], F32, name="root7_%d" % n, offset=at, align_bytes=64)
+            gather_page(LAST, n * QUARTER, (n + 1) * QUARTER, root, n * QUARTER)
+            if n == 1:
+                multiply(0, 0, HALF, quantize_z(0, 0, HALF, AT_WEIGHTED7 + 1024))
 
-        for lo, hi in PIECES[:2]:
-            woven = z_on_vector(lo, hi)
-            finish(0, HALF + lo, HALF + hi, z[0, HALF][:, lo:hi, :], recip67_at(lo))
-            finish(1, lo, hi, woven, None)
-        woven = z_on_vector(*PIECES[2])
+        z_pair(LAST - 1, *PIECES[0], nc.vector)
+        wb_q[1] = quantize(wb_woven[1], N, "wb1", root_at[0])
+        finish(*PIECES[0])
+        z_pair(LAST - 1, *PIECES[1], nc.vector)
+        second_half = quantize_z(0, HALF, M, root_at[1])
+        finish(*PIECES[1])
+        multiply(0, HALF, M, second_half)
+        z_pair(LAST - 1, *PIECES[2], nc.vector)
         for (lo, hi), following in zip(PIECES[2:], PIECES[3:]):
-            woven_next = z_on_vector(*following)
-            finish(1, lo, hi, woven, recip67_at(following[0]))
-            woven = woven_next
-        finish(1, *PIECES[-1], woven, None)
+            z_pair(LAST - 1, *following, nc.vector)
+            finish(lo, hi, root_at[3] if hi == LAG else None)
+        finish(*PIECES[-1])

@@ -58,7 +58,7 @@ AT_Z1 = AT_RECIP_B + 2 * 4 * M
 AT_PAGE = [AT_PAGE0, AT_PAGE1, 0, 4 * T2, AT_TAB1, AT_TAB1 + 4 * T2, AT_TAB2, AT_TAB2 + 4 * T2]
 LAG = 768
 STRIPE = 16
-PIECES = [(0, 256), (256, 512), (512, 768), (768, 896), (896, 1024)]
+PIECES = [(lo, lo + QUARTER) for lo in range(0, M, QUARTER)]
 
 
 def pieces_in(lo, hi):
@@ -402,6 +402,8 @@ def tile_list_seller_trust_cache_kernel(
 
         def banks_of(lo, hi):
             first = 2 * PIECES.index((lo, hi))
+            if hi == M:
+                return [((first + g) % BANKS, range(g, g + 1)) for g in range(N // P)]
             return [((first + g) % BANKS, range(2 * g, 2 * g + 2)) for g in range(2)]
 
         def second_product(b, lo, hi, codes, scale):
@@ -421,10 +423,10 @@ def tile_list_seller_trust_cache_kernel(
                     )
 
         def store(lo, hi):
-            width = 2 * (hi - lo)
             for g, (number, blocks) in enumerate(banks_of(lo, hi)):
+                width = len(blocks) * (hi - lo)
                 res = staged[:, PACK * lo + g * width : PACK * lo + (g + 1) * width]
-                if (lo, hi) == PIECES[-1] or ((lo, hi) == PIECES[-2] and g == 1):
+                if hi == M and g % 2 == 1:
                     nc.vector.tensor_copy(res, out_acc[lo, number][:, :width])
                 else:
                     nc.scalar.copy(res, out_acc[lo, number][:, :width])
@@ -441,7 +443,8 @@ def tile_list_seller_trust_cache_kernel(
                     store(first, end)
 
         def quantize_z(b, lo, hi, behind):
-            return quantize(z[b, lo][:], hi - lo, "z%d_%d" % (b, lo), behind)
+            first = lo - lo % HALF if b == 0 else lo
+            return quantize(z[b, first][:, lo - first : hi - first, :], hi - lo, "z%d_%d" % (b, lo), behind)
 
         def finish(lo, hi, behind=None):
             multiply(1, lo, hi, quantize_z(1, lo, hi, behind))
@@ -494,12 +497,10 @@ def tile_list_seller_trust_cache_kernel(
         z_pair(LAST - 1, *PIECES[0], nc.vector)
         wb_q[1] = quantize(wb_woven[1], N, "wb1", root_at[0])
         finish(*PIECES[0])
-        z_pair(LAST - 1, *PIECES[1], nc.vector)
-        second_half = quantize_z(0, HALF, M, root_at[1])
-        finish(*PIECES[1])
-        multiply(0, HALF, M, second_half)
-        z_pair(LAST - 1, *PIECES[2], nc.vector)
-        for (lo, hi), following in zip(PIECES[2:], PIECES[3:]):
-            z_pair(LAST - 1, *following, nc.vector)
-            finish(lo, hi, root_at[3] if hi == LAG else None)
+        for n in (1, 2):
+            z_pair(LAST - 1, *PIECES[n], nc.vector)
+            ahead = quantize_z(0, *PIECES[n + 1], root_at[n])
+            finish(*PIECES[n])
+            multiply(0, *PIECES[n + 1], ahead)
+        z_pair(LAST - 1, *PIECES[-1], nc.vector)
         finish(*PIECES[-1])

@@ -38,22 +38,23 @@ AT_PAGE1 = AT_PAGE0 + 4 * T2
 AT_WG = AT_PAGE1 + 4 * T2
 AT_W1 = AT_WG + PACK * 4 * S
 AT_GAIN = AT_W1 + A * 2 * PASS
-AT_ROOT = AT_GAIN + 64
-ROOT_BYTES = 6 * 1024
-AT_WB = AT_ROOT + ROOT_BYTES
-AT_WEIGHTED7 = AT_WB + TILES * 4 * N - 64
-AT_TAB1 = AT_WEIGHTED7 + 4 * S
+AT_WB = AT_GAIN + 64
+AT_TAB1 = AT_WB + TILES * 4 * N
 AT_END = AT_TAB1 + 4 * T
 AT_TAB2 = AT_END
 AT_V0 = AT_TAB2 + 4 * T
-AT_Z0 = (AT_V0 + 4 * S, AT_V0 + 4 * S + 6 * 1024)
-AT_H7 = AT_Z0[0] + 3 * 1024
-AT_WB1_CODES = AT_Z0[0] + 4 * 1024
-AT_WEIGHTED3 = AT_Z0[1] + 4 * 1024
+ROOT_BYTES = 6 * 1024
+AT_FLAT = (AT_PAGE0 + 2 * PACK * HALF, AT_PAGE1)
+AT_ROOT = (AT_V0, AT_FLAT[0], AT_FLAT[1])
+AT_Z0 = (AT_V0 + ROOT_BYTES, AT_PAGE0)
+AT_H7 = AT_Z0[0] + 2 * PACK * HALF
+AT_WB1_CODES = AT_H7
+AT_WEIGHTED3 = AT_H7 + 4 * S
 AT_WEIGHTED4 = AT_WEIGHTED3 + 4 * S
 AT_WB_WOVEN0 = AT_WEIGHTED4 + 4 * S
 AT_RECIP_A = AT_WB_WOVEN0 + 2 * PACK * N
 AT_RECIP_B = AT_RECIP_A + 2 * 4 * M
+AT_WEIGHTED7 = AT_RECIP_B + 4 * M
 AT_Z1 = AT_RECIP_B + 2 * 4 * M
 AT_PAGE = [AT_PAGE0, AT_PAGE1, 0, 4 * T2, AT_TAB1, AT_TAB1 + 4 * T2, AT_TAB2, AT_TAB2 + 4 * T2]
 LAG = 768
@@ -178,11 +179,11 @@ def tile_list_seller_trust_cache_kernel(
 
         w_codes = {}
 
-        def order_w_codes(b, engine):
+        def order_w_codes(b, copy):
             w_codes[b] = keep.tile([P, A, PACK, 2 * P], U8, name="w_codes", tag="w_codes%d" % b, align_bytes=64)
-            engine.tensor_copy(
-                w_codes[b][:].bitcast(I32).rearrange("p a t (c i) -> p a c t i", i=4),
-                w_raw[b].rearrange("p a (c i t) -> p a c t i", i=4, t=PACK),
+            copy(
+                w_codes[b][:].bitcast(U32).rearrange("p a t (c i) -> p a c t i", i=4),
+                w_raw[b].bitcast(U32).rearrange("p a (c i t) -> p a c t i", i=4, t=PACK),
             )
 
         v_codes = {}
@@ -199,7 +200,7 @@ def tile_list_seller_trust_cache_kernel(
         gather_words(0, 0, S)
         load_wg(0, 0, HALF, wg_first)
         load_page(0)
-        order_w_codes(0, nc.vector)
+        order_w_codes(0, nc.vector.tensor_copy)
         stage_v_scales(1, keep.tile([P, HALF], U8, name="v_scale1", align_bytes=64)[:])
         late = placed.tile([P, A, LATE], U8, name="late", offset=AT_LATE, align_bytes=64)
         nc.vector.memset(late[:].bitcast(I32), 0)
@@ -228,17 +229,18 @@ def tile_list_seller_trust_cache_kernel(
         load_wg(1, 0, S)
         for e in range(2):
             nc.sync.dma_start(out=gain_sb[e:P:2, :, 0 : 2 * PACK - 1], in_=gain_rows[:, :, e : e + 2 * PACK - 1])
-        for i in (2, 3):
-            load_page(i)
-            load_wg(i, 0, S)
-        load_wg(0, 0, HALF)
+        load_page(2)
+        load_wg(2, 0, S)
+        load_w(1)
+        load_wb(0)
+        load_page(3)
+        load_wg(3, 0, S)
+        load_wb(1)
         load_page(4)
         load_page(5)
-        load_w(1)
+        load_wg(0, 0, HALF)
         load_page(6)
         load_page(7)
-        load_wb(0)
-        load_wb(1)
 
         def bank(n, name):
             return psum.tile([P, HALF], F32, name=name, tag="bank%d" % n)
@@ -289,11 +291,13 @@ def tile_list_seller_trust_cache_kernel(
 
         weighted = {}
 
-        weighted_at = {3: AT_WEIGHTED3, 4: AT_WEIGHTED4, 6: AT_WEIGHTED3, 7: AT_WEIGHTED7}
+        weighted_at = {3: AT_WEIGHTED3, 4: AT_WEIGHTED4, 5: AT_WG, 7: AT_WEIGHTED7}
 
         def weigh(i):
             if i in weighted_at:
                 weighted[i] = placed.tile([P, S], F32, name="weighted%d" % i, offset=weighted_at[i], align_bytes=64)[:]
+            elif i == LAST - 1:
+                weighted[i] = x_tiles(1, 1)[:, 0, :]
             else:
                 weighted[i] = arena[:, :S]
             nc.gpsimd.tensor_tensor(weighted[i], h_cols(i, 0, S), wg[i % PACK][:], MULT)
@@ -333,9 +337,10 @@ def tile_list_seller_trust_cache_kernel(
                 recip[pair] = placed.tile([P, 2 * M], F32, name="recip%d" % pair, offset=at, align_bytes=64)
             return [(lo, hi, recip[pair][:, (i % 2) * M + lo : (i % 2) * M + hi])]
 
-        def new_root(stage):
-            at, width = ((AT_ROOT, M), (AT_V0, M), (AT_ROOT, (ROOT_BYTES + 64) // 4))[stage]
-            return placed.tile([P, width], F32, name="root%d" % stage, offset=at, align_bytes=64)
+        def new_root(stage, back=0, forward=0):
+            width = ((ROOT_BYTES, 4 * M, ROOT_BYTES)[stage] + back + forward) // 4
+            name = "root_%d_%d" % (stage, width)
+            return placed.tile([P, width], F32, name=name, offset=AT_ROOT[stage] - back, align_bytes=64)
 
         def gather_page(i, lo, hi, root, origin=0):
             b, t = divmod(i, PACK)
@@ -383,7 +388,7 @@ def tile_list_seller_trust_cache_kernel(
         def z_pair(i, lo, hi, engine=nc.gpsimd):
             b, t = divmod(i, PACK)
             if t == 0:
-                at = AT_Z0[lo // HALF] if b == 0 else AT_Z1 + 2 * PACK * lo
+                at = AT_Z1 + 2 * PACK * lo
                 z[b, lo] = placed.tile([P, hi - lo, PACK], BF16, name="z%d_%d" % (b, lo), offset=at, align_bytes=64)
             if i == LAST - 1:
                 factor = recip[i, lo][:].rearrange("p (t m) -> p t m", t=2)
@@ -395,6 +400,21 @@ def tile_list_seller_trust_cache_kernel(
                 factor.rearrange("p t (c i) -> p c t i", i=2),
                 MULT,
             )
+
+        flat = [
+            placed.tile([P, PACK, HALF], BF16, name="flat%d" % half, offset=AT_FLAT[half], align_bytes=64)
+            for half in range(2)
+        ]
+
+        def z_flat(i, half):
+            lo, hi = half * HALF, (half + 1) * HALF
+            factor = recip[i - i % 2][:, (i % 2) * M + lo : (i % 2) * M + hi]
+            nc.gpsimd.tensor_tensor(flat[half][:, i, :], x_tiles(i, 1)[:, 0, lo:hi], factor, MULT)
+
+        def weave_z(half):
+            lo = half * HALF
+            z[0, lo] = placed.tile([P, HALF, PACK], BF16, name="z0_%d" % lo, offset=AT_Z0[half], align_bytes=64)
+            weave(z[0, lo][:], flat[half][:])
 
         out_rows = out.rearrange("(n p) m -> p n m", p=P)
         out_acc = {}
@@ -455,13 +475,13 @@ def tile_list_seller_trust_cache_kernel(
         scatter(0, HALF, S)
         scatter(1, 0, S)
         split_gain()
+        order_w_codes(1, nc.scalar.copy)
+        for i in range(PACK, TILES):
+            first_product(i)
         gather_page(0, 0, M, new_root(0))
         gather_page(1, 0, LAG, new_root(0))
         weigh(2)
         weigh(3)
-        order_w_codes(1, nc.gpsimd)
-        for i in range(PACK, TILES):
-            first_product(i)
         weave_wb(0)
         weave_wb(1)
         for i in range(2, LAST):
@@ -471,13 +491,21 @@ def tile_list_seller_trust_cache_kernel(
                 weigh(5)
             if i == 3:
                 weigh(6)
-                weigh(7)
-            gather_page(i - 1, LAG, M, new_root(1 if i == 2 else 2))
-            if i in (3, 4):
-                for lo in (0, HALF):
-                    z_pair(2 * (i - 3), lo, lo + HALF)
+            gather_page(i - 1, LAG, M, new_root(max(0, i - PACK)))
+            if i == 2:
+                z_flat(0, 0)
+                z_flat(0, 1)
+                z_flat(1, 0)
+            if i <= PACK:
+                z_flat(i - 1, 1)
             if i < LAST - 1:
-                gather_page(i, 0, LAG, new_root(1 if i == 2 else 2))
+                gather_page(i, 0, LAG, new_root(max(0, i - PACK), back=64 * (i == PACK + 1), forward=64 * (i == PACK)))
+            if i == PACK:
+                weigh(LAST)
+            if i < PACK:
+                z_flat(i, 0)
+            if i in (PACK, PACK + 1):
+                weave_z(i - PACK)
             if i == PACK + 1:
                 for lo, hi in pieces_in(0, LAG):
                     z_pair(PACK, lo, hi)
@@ -487,7 +515,7 @@ def tile_list_seller_trust_cache_kernel(
 
         scatter_weighted(LAST)
         wb_q[0] = quantize(wb_woven[0], N, "wb0", AT_WB1_CODES)
-        root_at = [AT_ROOT + 1024 * n for n in (0, 2, 4, 5)]
+        root_at = [AT_ROOT[2] + 1024 * n for n in (0, 2, 4, 5)]
         for n, at in enumerate(root_at):
             root = placed.tile([P, QUARTER], F32, name="root7_%d" % n, offset=at, align_bytes=64)
             gather_page(LAST, n * QUARTER, (n + 1) * QUARTER, root, n * QUARTER)

@@ -317,25 +317,13 @@ def tile_list_seller_trust_cache_kernel(
 
         recip = {}
 
-        def recip67_at(lo):
-            return AT_RECIP_A + 2 * 4 * lo
+        groups = [(0, 2, AT_RECIP_A), (2, 2, AT_RECIP_B), (4, 1, AT_RECIP_A), (5, 3, AT_RECIP_A)]
 
-        def recip_parts(i, lo, hi):
-            if i >= LAST - 1:
-                parts = []
-                for first, end in pieces_in(lo, hi):
-                    width = end - first
-                    if i == LAST - 1:
-                        recip[i, first] = placed.tile(
-                            [P, 2 * width], F32, name="recip67_%d" % first, offset=recip67_at(first), align_bytes=64
-                        )
-                    parts.append((first, end, recip[LAST - 1, first][:, (i % 2) * width : (i % 2 + 1) * width]))
-                return parts
-            pair = i - i % 2
-            if (i, lo) == (pair, 0):
-                at = AT_RECIP_B if pair == 2 else AT_RECIP_A
-                recip[pair] = placed.tile([P, 2 * M], F32, name="recip%d" % pair, offset=at, align_bytes=64)
-            return [(lo, hi, recip[pair][:, (i % 2) * M + lo : (i % 2) * M + hi])]
+        def recip_rows(i, count, lo, hi):
+            first, size, at = [group for group in groups if group[0] <= i][-1]
+            if first not in recip:
+                recip[first] = placed.tile([P, size, M], F32, name="recip%d" % first, offset=at, align_bytes=64)
+            return recip[first][:, i - first : i - first + count, lo:hi]
 
         def new_root(stage, back=0, forward=0):
             width = ((ROOT_BYTES, 4 * M, ROOT_BYTES)[stage] + back + forward) // 4
@@ -349,10 +337,7 @@ def tile_list_seller_trust_cache_kernel(
             part = root[:, lo - origin : hi - origin]
             nc.scalar.activation(part, x, ACT.Abs)
             nc.scalar.activation(part, part, ACT.Abs_reciprocal_sqrt, bias=1.0)
-            for first, end, target in recip_parts(i, lo, hi):
-                nc.scalar.activation(
-                    target, root[:, first - origin : end - origin], ACT.Square, scale=gain_root[:, b, t : t + 1]
-                )
+            nc.scalar.activation(recip_rows(i, 1, lo, hi)[:, 0, :], part, ACT.Square, scale=gain_root[:, b, t : t + 1])
 
         def weave(woven, flat):
             nc.scalar.copy(
@@ -383,23 +368,22 @@ def tile_list_seller_trust_cache_kernel(
                 wb_woven[b] = keep.tile([P, N, PACK], BF16, name="wb_woven1", align_bytes=64)[:]
             weave(wb_woven[b], by_tile(wb_raw[b][:]))
 
-        z = {}
+        z = {(1, 0): placed.tile([P, M, PACK], BF16, name="z1", offset=AT_Z1, align_bytes=64)}
 
-        def z_pair(i, lo, hi, engine=nc.gpsimd):
-            b, t = divmod(i, PACK)
-            if t == 0:
-                at = AT_Z1 + 2 * PACK * lo
-                z[b, lo] = placed.tile([P, hi - lo, PACK], BF16, name="z%d_%d" % (b, lo), offset=at, align_bytes=64)
-            if i == LAST - 1:
-                factor = recip[i, lo][:].rearrange("p (t m) -> p t m", t=2)
-            else:
-                factor = recip[i][:].rearrange("p (t m) -> p t m", t=2)[:, :, lo:hi]
+        def z_cols(b, lo, hi):
+            first = lo - lo % HALF if b == 0 else 0
+            return z[b, first][:, lo - first : hi - first, :]
+
+        def z_words(engine, i, count, lo, hi):
             engine.tensor_tensor(
-                z[b, lo][:, :, t : t + 2].rearrange("p (c i) t -> p c t i", i=2),
-                x_tiles(i, 2)[:, :, lo:hi].rearrange("p t (c i) -> p c t i", i=2),
-                factor.rearrange("p t (c i) -> p c t i", i=2),
+                z_cols(1, lo, hi)[:, :, i - PACK : i - PACK + count].rearrange("p (c i) t -> p c t i", i=2),
+                x_tiles(i, count)[:, :, lo:hi].rearrange("p t (c i) -> p c t i", i=2),
+                recip_rows(i, count, lo, hi).rearrange("p t (c i) -> p c t i", i=2),
                 MULT,
             )
+
+        def last_product(lo, hi):
+            z_words(nc.vector, PACK + 1, PACK - 1, lo, hi)
 
         flat = [
             placed.tile([P, PACK, HALF], BF16, name="flat%d" % half, offset=AT_FLAT[half], align_bytes=64)
@@ -408,7 +392,7 @@ def tile_list_seller_trust_cache_kernel(
 
         def z_flat(i, half):
             lo, hi = half * HALF, (half + 1) * HALF
-            factor = recip[i - i % 2][:, (i % 2) * M + lo : (i % 2) * M + hi]
+            factor = recip_rows(i, 1, lo, hi)[:, 0, :]
             nc.gpsimd.tensor_tensor(flat[half][:, i, :], x_tiles(i, 1)[:, 0, lo:hi], factor, MULT)
 
         def weave_z(half):
@@ -463,8 +447,7 @@ def tile_list_seller_trust_cache_kernel(
                     store(first, end)
 
         def quantize_z(b, lo, hi, behind):
-            first = lo - lo % HALF if b == 0 else lo
-            return quantize(z[b, first][:, lo - first : hi - first, :], hi - lo, "z%d_%d" % (b, lo), behind)
+            return quantize(z_cols(b, lo, hi), hi - lo, "z%d_%d" % (b, lo), behind)
 
         def finish(lo, hi, behind=None):
             multiply(1, lo, hi, quantize_z(1, lo, hi, behind))
@@ -498,6 +481,8 @@ def tile_list_seller_trust_cache_kernel(
                 z_flat(1, 0)
             if i <= PACK:
                 z_flat(i - 1, 1)
+            if i == PACK + 1:
+                z_words(nc.gpsimd, PACK, 1, LAG, M)
             if i < LAST - 1:
                 gather_page(i, 0, LAG, new_root(max(0, i - PACK), back=64 * (i == PACK + 1), forward=64 * (i == PACK)))
             if i == PACK:
@@ -506,11 +491,8 @@ def tile_list_seller_trust_cache_kernel(
                 z_flat(i, 0)
             if i in (PACK, PACK + 1):
                 weave_z(i - PACK)
-            if i == PACK + 1:
-                for lo, hi in pieces_in(0, LAG):
-                    z_pair(PACK, lo, hi)
-        for lo, hi in pieces_in(LAG, M):
-            z_pair(PACK, lo, hi)
+            if i == PACK:
+                z_words(nc.gpsimd, PACK, 1, 0, LAG)
         gather_page(LAST - 1, 0, M, new_root(2))
 
         scatter_weighted(LAST)
@@ -522,13 +504,13 @@ def tile_list_seller_trust_cache_kernel(
             if n == 1:
                 multiply(0, 0, HALF, quantize_z(0, 0, HALF, AT_WEIGHTED7 + 1024))
 
-        z_pair(LAST - 1, *PIECES[0], nc.vector)
+        last_product(*PIECES[0])
         wb_q[1] = quantize(wb_woven[1], N, "wb1", root_at[0])
         finish(*PIECES[0])
         for n in (1, 2):
-            z_pair(LAST - 1, *PIECES[n], nc.vector)
+            last_product(*PIECES[n])
             ahead = quantize_z(0, *PIECES[n + 1], root_at[n])
             finish(*PIECES[n])
             multiply(0, *PIECES[n + 1], ahead)
-        z_pair(LAST - 1, *PIECES[-1], nc.vector)
+        last_product(*PIECES[-1])
         finish(*PIECES[-1])

@@ -29,16 +29,19 @@ HALF = 512
 QUARTER = 256
 ROWS = A * 16
 ROW0 = 48
-EARLY = HALF + P
-LATE = S + H - EARLY
-AT_LATE = 4 * T
-AT_WG0 = AT_LATE + A * LATE
-AT_PAGE0 = AT_WG0 + 4 * HALF
+STAGES = [(HALF, S + 2 * P), (0, HALF), (S + 2 * P, S + H)]
+AT_STAGE1 = 4 * T
+AT_WG_FIRST = AT_STAGE1 + A * HALF
+AT_W_TILE1 = AT_WG_FIRST + 4 * HALF
+AT_PAGE0 = AT_W_TILE1 + A * 2 * P
 AT_PAGE1 = AT_PAGE0 + 4 * T2
 AT_WG = AT_PAGE1 + 4 * T2
-AT_W1 = AT_WG + PACK * 4 * S
+AT_WG_PLAIN = AT_WG + PACK * 4 * S
+AT_STAGE2 = AT_WG_PLAIN + 4 * S
+AT_W_TILES23 = AT_STAGE2 + A * (H - 2 * P)
+AT_W1 = AT_W_TILES23 + A * 4 * P
 AT_GAIN = AT_W1 + A * 2 * PASS
-AT_WB = AT_GAIN + 64
+AT_WB = AT_GAIN + 128
 AT_TAB1 = AT_WB + TILES * 4 * N
 AT_END = AT_TAB1 + 4 * T
 AT_TAB2 = AT_END
@@ -88,11 +91,11 @@ def tile_list_seller_trust_cache_kernel(
 
         tab_scale_win = keep.tile([P, T], U8, name="tab_scale_win", align_bytes=64)
         w_scale_raw = placed.tile([P, H], U8, name="w_scale_raw", offset=AT_V0 - HALF - H, align_bytes=64)
-        planes = keep.tile([P, A, EARLY], U8, name="planes", align_bytes=64)
+        planes = [keep.tile([P, A, HALF + 2 * P], U8, name="planes0", align_bytes=64)]
         for rows in (slice(0, ROW0), slice(ROW0 + ROWS, P)):
             nc.vector.memset(tab_scale_win[rows, :].bitcast(I32), 0)
             nc.vector.memset(w_scale_raw[rows, :].bitcast(I32), 0)
-        nc.vector.memset(planes[:].bitcast(I32), 0)
+        nc.vector.memset(planes[0][:].bitcast(I32), 0)
 
         second_page = AT_PAGE1
         tab = [
@@ -107,15 +110,19 @@ def tile_list_seller_trust_cache_kernel(
             words = tab_words[a].rearrange("p n t -> p (n t)").bitcast(I32)
             nc.sync.dma_start(out=tab[a][:, lo:hi], in_=words[:, lo:hi])
 
-        pairs = PASS // 2
-        w_raw = [
-            keep.tile([P, A, pairs], I32, name="w_raw0", align_bytes=64)[:],
-            placed.tile([P, A, pairs], I32, name="w_raw1", offset=AT_W1, align_bytes=64)[:],
-        ]
         w_words_i32 = w4_words.rearrange("a p n -> p a n").bitcast(I32)
+        w_codes = {}
 
-        def load_w(b):
-            nc.sync.dma_start(out=w_raw[b], in_=w_words_i32[:, :, b * pairs : (b + 1) * pairs])
+        def load_w(first, count, at=None):
+            if at is None:
+                tile = keep.tile([P, A, count * 2 * P], U8, name="w_raw%d" % first, align_bytes=64)
+            else:
+                tile = placed.tile([P, A, count * 2 * P], U8, name="w_raw%d" % first, offset=at, align_bytes=64)
+            words = w_words_i32[:, :, first * P // 2 : (first + count) * P // 2]
+            nc.sync.dma_start(out=tile[:].bitcast(I32), in_=words)
+            for i in range(count):
+                w_codes[first + i] = tile[:, :, i * 2 * P : (i + 1) * 2 * P]
+            return tile
 
         wg = [
             placed.tile([P, S], F32, name="wg%d" % t, tag="wg%d" % t, offset=AT_WG + 4 * S * t, align_bytes=64)
@@ -123,21 +130,35 @@ def tile_list_seller_trust_cache_kernel(
         ]
         wgs_rows = wgs.rearrange("(u t e) j -> t u e j", t=PACK, e=2)
 
-        wg_first = placed.tile([P, HALF], F32, name="wg_first", offset=AT_WG0, align_bytes=64)
+        wg_first = placed.tile([P, HALF], F32, name="wg_first", offset=AT_WG_FIRST, align_bytes=64)
+        wg_plain = placed.tile([P, S], F32, name="wg_plain", offset=AT_WG_PLAIN, align_bytes=64)
 
-        def load_wg(t, lo, hi, tile=None):
+        def load_wg(t):
             for q in (0, 2, 1, 3):
-                nc.sync.dma_start(out=(tile or wg[t])[QUAD * q : QUAD * (q + 1), lo:hi], in_=wgs_rows[t][:, :, lo:hi])
+                nc.sync.dma_start(out=wg[t][QUAD * q : QUAD * (q + 1), :], in_=wgs_rows[t])
+
+        def load_wg_plain(tile, lo, hi):
+            nc.sync.dma_start(out=tile[:, lo:hi], in_=wgs[:, lo:hi])
 
         page_rows = page0.rearrange("(b u t e) c -> b t u e c", b=B, t=PACK, e=2)
         page = {}
 
         def load_page(i):
             page[i] = placed.tile([P, T2], F32, name="page%d" % i, offset=AT_PAGE[i], align_bytes=64)
-            nc.sync.dma_start(out=page[i][:], in_=page_rows[i // PACK, i % PACK])
+            rows = page0[i * P : (i + 1) * P, :] if i < PACK else page_rows[1, i - PACK]
+            nc.sync.dma_start(out=page[i][:], in_=rows)
 
-        gain_rows = gain.rearrange("(b u w) -> u b w", b=B, w=2 * PACK)
-        gain_sb = placed.tile([P, B, 2 * PACK], F32, name="gain_sb", offset=AT_GAIN, align_bytes=64)
+        gain_rows = gain.rearrange("(b u w) -> b u w", b=B, w=2 * PACK)
+        gain_sb = placed.tile([P, 3, 2 * PACK], F32, name="gain_sb", offset=AT_GAIN, align_bytes=64)
+
+        def load_gain():
+            with nc.allow_non_contiguous_dma(reason="one gain for each partition and row tile"):
+                nc.sync.dma_start(
+                    out=gain_sb[:, 0, 0 : 2 * PACK : 2], in_=gain[0:PASS].rearrange("(i p) -> p i", p=P)
+                )
+            nc.sync.dma_start(out=gain_sb[:, 1, 0:PACK], in_=gain[0:PASS].rearrange("(p t) -> p t", t=PACK))
+            for e in range(2):
+                nc.sync.dma_start(out=gain_sb[e:P:2, 2, 0 : 2 * PACK - 1], in_=gain_rows[1][:, e : e + 2 * PACK - 1])
 
         load_tab(0, 0, T // 2)
         for tile, rows in ((tab_scale_win, tab_scales), (w_scale_raw, w4_scales)):
@@ -146,27 +167,29 @@ def tile_list_seller_trust_cache_kernel(
             )
         nc.sync.dma_start(list1[:], offs)
         load_tab(0, T // 2, T)
-        load_w(0)
+        load_w(0, 1)
         load_tab(1)
         nc.sync.dma_start(list2[:], offs2)
-        nc.sync.dma_start(list3[:], offs3)
 
         staged_scales = keep.tile([P, S + H], U8, name="staged_scales", align_bytes=64)
 
         def stage_v_scales(half, v_scale):
             nc.vector.tensor_copy(v_scale, tab_scale_win[:].indirect(entries(list1, half * HALF, (half + 1) * HALF)))
-            first = half * (HALF + H)
+            first = (1 - half) * HALF
             nc.vector.tensor_copy(staged_scales[:, first : first + HALF].bitcast(I32), v_scale.bitcast(I32))
 
         stage_v_scales(
             0, placed.tile([P, 2 * HALF], U8, name="v_scale0", offset=AT_V0 - HALF, align_bytes=64)[:, :HALF]
         )
+        nc.vector.tensor_copy(staged_scales[:, S : S + PASS].bitcast(I32), w_scale_raw[:, :PASS].bitcast(I32))
         nc.vector.tensor_copy(
-            staged_scales[:, HALF : HALF + H].bitcast(U16).rearrange("p (b t c i) -> p b c t i", b=B, t=PACK, i=8),
-            w_scale_raw[:].bitcast(U16).rearrange("p (b c i t) -> p b c t i", b=B, i=8, t=PACK),
+            staged_scales[:, S + PASS :].bitcast(U16).rearrange("p (t c i) -> p c t i", t=PACK, i=8),
+            w_scale_raw[:, PASS:].bitcast(U16).rearrange("p (c i t) -> p c t i", i=8, t=PACK),
         )
 
-        def move_scales(queues, target, lo, hi):
+        def move_scales(queues, stage):
+            target = planes[stage]
+            lo, hi = STAGES[stage]
             for q in (0, 2, 1, 3):
                 first = ROW0 + 4 * A * q
                 queues[q % 2].dma_start(
@@ -174,42 +197,48 @@ def tile_list_seller_trust_cache_kernel(
                     in_=staged_scales[first : first + 4 * A, lo:hi].bitcast(I32),
                 )
 
-        move_scales((nc.sync, nc.scalar), planes, 0, EARLY)
+        def new_planes(at, stage):
+            lo, hi = STAGES[stage]
+            planes.append(placed.tile([P, A, hi - lo], U8, name="planes%d" % stage, offset=at, align_bytes=64))
+            nc.vector.memset(planes[stage][:].bitcast(I32), 0)
+
+        move_scales((nc.sync, nc.scalar), 0)
         load_tab(2)
 
-        w_codes = {}
-
-        def order_w_codes(b, copy):
-            w_codes[b] = keep.tile([P, A, PACK, 2 * P], U8, name="w_codes", tag="w_codes%d" % b, align_bytes=64)
-            copy(
-                w_codes[b][:].bitcast(U32).rearrange("p a t (c i) -> p a c t i", i=4),
-                w_raw[b].bitcast(U32).rearrange("p a (c i t) -> p a c t i", i=4, t=PACK),
+        def order_w_codes(raw):
+            ordered = keep.tile([P, A, PACK, 2 * P], U8, name="w_ordered", align_bytes=64)
+            nc.scalar.copy(
+                ordered[:].bitcast(U32).rearrange("p a t (c i) -> p a c t i", i=4),
+                raw[:].bitcast(U32).rearrange("p a (c i t) -> p a c t i", i=4, t=PACK),
             )
+            for t in range(PACK):
+                w_codes[PACK + t] = ordered[:, :, t, :]
 
         v_codes = {}
 
-        def gather_words(a, lo, hi):
+        def gather_words(a, lo, hi, step=S):
             if a == 0:
                 picked = placed.tile([P, hi - lo], U32, name="picked0", offset=AT_V0, align_bytes=64)
             else:
                 picked = keep.tile([P, hi - lo], U32, name="picked", tag="v_codes%d_%d" % (a, lo), align_bytes=64)
-            nc.vector.tensor_copy(picked[:], tab[a].bitcast(U32).indirect(entries(list1, lo, hi)))
+            for c in range(lo, hi, step):
+                end = min(hi, c + step)
+                window = tab[a].bitcast(U32).indirect(entries(list1, c, end))
+                nc.vector.tensor_copy(picked[:, c - lo : end - lo], window)
             for c in range(lo, hi, HALF):
                 v_codes[a, c // HALF] = picked[:, c - lo : c - lo + HALF]
 
         gather_words(0, 0, S)
-        load_wg(0, 0, HALF, wg_first)
+        load_wg_plain(wg_first, 0, HALF)
         load_page(0)
-        order_w_codes(0, nc.vector.tensor_copy)
+        load_w(1, 1, AT_W_TILE1)
         stage_v_scales(1, keep.tile([P, HALF], U8, name="v_scale1", align_bytes=64)[:])
-        late = placed.tile([P, A, LATE], U8, name="late", offset=AT_LATE, align_bytes=64)
-        nc.vector.memset(late[:].bitcast(I32), 0)
-        move_scales((nc.sync, nc.sync), late, EARLY, S + H)
+        new_planes(AT_STAGE1, 1)
+        move_scales((nc.sync, nc.sync), 1)
 
         def scales(a, lo, hi):
-            if hi <= EARLY:
-                return planes[:, a, lo:hi]
-            return late[:, a, lo - EARLY : hi - EARLY]
+            stage = [n for n, (first, end) in enumerate(STAGES) if first <= lo and hi <= end][0]
+            return planes[stage][:, a, lo - STAGES[stage][0] : hi - STAGES[stage][0]]
 
         wb_rows = wb.rearrange("(b u t e) n -> b t u e n", b=B, t=PACK, e=2)
         wb_raw = [
@@ -218,27 +247,32 @@ def tile_list_seller_trust_cache_kernel(
         ]
 
         def load_wb(b):
+            if b == 0:
+                nc.sync.dma_start(out=wb_raw[b][:], in_=wb[0:PASS, :].rearrange("(p t) n -> p (t n)", t=PACK))
+                return
             for t in range(PACK):
                 nc.sync.dma_start(out=wb_raw[b][:, t * N : (t + 1) * N], in_=wb_rows[b, t])
 
         gather_words(1, 0, S)
-        gather_words(2, 0, HALF)
+        new_planes(AT_STAGE2, 2)
+        gather_words(2, 0, HALF, QUARTER)
         gather_words(2, HALF, S)
-        load_wg(0, HALF, S)
         load_page(1)
-        load_wg(1, 0, S)
-        for e in range(2):
-            nc.sync.dma_start(out=gain_sb[e:P:2, :, 0 : 2 * PACK - 1], in_=gain_rows[:, :, e : e + 2 * PACK - 1])
+        load_wg_plain(wg_plain, HALF, S)
+        move_scales((nc.sync, nc.sync), 2)
+        load_w(2, 2, AT_W_TILES23)
+        load_gain()
         load_page(2)
-        load_wg(2, 0, S)
-        load_w(1)
-        load_wb(0)
+        nc.sync.dma_start(list3[:], offs3)
         load_page(3)
-        load_wg(3, 0, S)
+        load_wg_plain(wg_plain, 0, HALF)
+        w_raw = load_w(PACK, PACK, AT_W1)
+        load_wb(0)
         load_wb(1)
         load_page(4)
         load_page(5)
-        load_wg(0, 0, HALF)
+        for t in range(PACK):
+            load_wg(t)
         load_page(6)
         load_page(7)
 
@@ -249,7 +283,7 @@ def tile_list_seller_trust_cache_kernel(
         arena = keep.tile([P, x_start + TILES * M], F32, name="arena", align_bytes=64)
         h_start = {i: S + S * i for i in range(2, LAST)}
         h_start[0] = 2 * S
-        h_start[1] = HALF
+        h_start[1] = 0
         h_last = placed.tile([P, S], F32, name="h_last", offset=AT_H7, align_bytes=64)
 
         def h_cols(i, lo, hi):
@@ -260,31 +294,28 @@ def tile_list_seller_trust_cache_kernel(
         def x_tiles(i, count):
             return arena[:, x_start + i * M : x_start + (i + count) * M].rearrange("p (t m) -> p t m", t=count)
 
-        h_acc = {}
-
-        def evacuate(i, half):
-            nc.scalar.copy(h_cols(i, half * HALF, (half + 1) * HALF), h_acc[i, half][:])
-
-        def first_product(i):
-            b, t = divmod(i, PACK)
+        def first_product(i, halves=(0, 1)):
             order = list(range(A)) if i == 0 else [A - 1] + list(range(A - 1))
-            for half in range(2):
-                acc = bank((2 * i + half) % BANKS, "acc_h")
-                for a in order:
-                    nc.tensor.matmul_mx(
-                        out=acc[:],
-                        lhsT=w_codes[b][:, a, t, :].bitcast(FP4X4),
-                        lhsT_scale=scales(a, HALF + i * P, HALF + (i + 1) * P),
-                        rhs=v_codes[a, half].bitcast(FP8X4),
-                        rhs_scale=scales(a, half * (HALF + H), half * (HALF + H) + HALF),
-                        start=(a == order[0]),
-                        stop=(a == order[-1]),
-                    )
-                h_acc[i, half] = acc
-                evacuate(i, half)
+            for half in halves:
+                parts = [(0, 0, QUARTER), (LAST, QUARTER, HALF)] if (i, half) == (0, 0) else [(2 * i + half, 0, HALF)]
+                for number, lo, hi in parts:
+                    product_part(i, half, order, bank(number % BANKS, "acc_h")[:, : hi - lo], lo, hi)
+
+        def product_part(i, half, order, acc, lo, hi):
+            for a in order:
+                nc.tensor.matmul_mx(
+                    out=acc,
+                    lhsT=w_codes[i][:, a, :].bitcast(FP4X4),
+                    lhsT_scale=scales(a, S + i * P, S + (i + 1) * P),
+                    rhs=v_codes[a, half][:, lo:hi].bitcast(FP8X4),
+                    rhs_scale=scales(a, (1 - half) * HALF + lo, (1 - half) * HALF + hi),
+                    start=(a == order[0]),
+                    stop=(a == order[-1]),
+                )
+            nc.scalar.copy(h_cols(i, half * HALF + lo, half * HALF + hi), acc)
 
         def scatter(i, lo, hi):
-            weights = wg_first if (i, lo) == (0, 0) else wg[i % PACK]
+            weights = wg_first if lo == 0 else wg_plain
             nc.vector.tensor_tensor(
                 page[i][:].indirect(entries(list2, lo, hi)), h_cols(i, lo, hi), weights[:, lo:hi], MULT
             )
@@ -300,7 +331,7 @@ def tile_list_seller_trust_cache_kernel(
                 weighted[i] = x_tiles(1, 1)[:, 0, :]
             else:
                 weighted[i] = arena[:, :S]
-            nc.gpsimd.tensor_tensor(weighted[i], h_cols(i, 0, S), wg[i % PACK][:], MULT)
+            nc.gpsimd.tensor_tensor(weighted[i], h_cols(i, 0, S), (wg_plain if i < PACK else wg[i - PACK])[:], MULT)
 
         def scatter_weighted(i):
             nc.vector.tensor_copy(page[i][:].indirect(list2[:]), weighted[i])
@@ -309,10 +340,11 @@ def tile_list_seller_trust_cache_kernel(
         gain_sign = keep.tile([P, B, PACK], F32, name="gain_sign")
 
         def split_gain():
-            gains = gain_sb[:, :, 0 : 2 * PACK : 2]
+            gains = gain_sb[:, 0:3:2, 0 : 2 * PACK : 2]
             nc.scalar.activation(gain_root[:], gains, ACT.Abs)
             nc.scalar.activation(gain_root[:], gain_root[:], ACT.Sqrt)
-            nc.scalar.activation(gain_sign[:], gains, ACT.Sign)
+            nc.scalar.activation(gain_sign[:, 0, :], gain_sb[:, 1, 0:PACK], ACT.Sign)
+            nc.scalar.activation(gain_sign[:, 1, :], gains[:, 1, :], ACT.Sign)
             nc.scalar.activation(gain_sign[:], gain_sign[:], ACT.Sign, bias=0.5)
 
         recip = {}
@@ -393,7 +425,13 @@ def tile_list_seller_trust_cache_kernel(
         def z_flat(i, half):
             lo, hi = half * HALF, (half + 1) * HALF
             factor = recip_rows(i, 1, lo, hi)[:, 0, :]
-            nc.gpsimd.tensor_tensor(flat[half][:, i, :], x_tiles(i, 1)[:, 0, lo:hi], factor, MULT)
+            if i < 2:
+                rows = arena[:, (2 * i + half) * QUARTER : (2 * i + half + 1) * QUARTER].bitcast(BF16)
+            else:
+                at = AT_WEIGHTED3 + (2 * (i - 2) + half) * 2 * HALF
+                rows = placed.tile([P, HALF], BF16, name="z_rows%d_%d" % (i, half), offset=at, align_bytes=64)[:]
+            nc.gpsimd.tensor_tensor(rows, x_tiles(i, 1)[:, 0, lo:hi], factor, MULT)
+            nc.sync.dma_start(out=flat[half][QUAD * i : QUAD * (i + 1), :, :], in_=rows)
 
         def weave_z(half):
             lo = half * HALF
@@ -452,13 +490,14 @@ def tile_list_seller_trust_cache_kernel(
         def finish(lo, hi, behind=None):
             multiply(1, lo, hi, quantize_z(1, lo, hi, behind))
 
-        for i in range(PACK):
+        for half in range(2):
+            for i in range(2):
+                first_product(i, (half,))
+                scatter(i, half * HALF, (half + 1) * HALF)
+        for i in range(2, PACK):
             first_product(i)
-        scatter(0, 0, HALF)
-        scatter(0, HALF, S)
-        scatter(1, 0, S)
         split_gain()
-        order_w_codes(1, nc.scalar.copy)
+        order_w_codes(w_raw)
         for i in range(PACK, TILES):
             first_product(i)
         gather_page(0, 0, M, new_root(0))

@@ -30,14 +30,14 @@ QUARTER = 256
 ROWS = A * 16
 ROW0 = 48
 STAGES = [(HALF, S + 2 * P), (0, HALF), (S + 2 * P, S + H)]
-AT_STAGE1 = 4 * T
-AT_WG_FIRST = AT_STAGE1 + A * HALF
+AT_WG_FIRST = 4 * T
 AT_W_TILE1 = AT_WG_FIRST + 4 * HALF
 AT_PAGE0 = AT_W_TILE1 + A * 2 * P
 AT_PAGE1 = AT_PAGE0 + 4 * T2
 AT_WG = AT_PAGE1 + 4 * T2
 AT_WG_PLAIN = AT_WG + PACK * 4 * S
-AT_STAGE2 = AT_WG_PLAIN + 4 * S
+AT_STAGE1 = AT_WG_PLAIN + 4 * S
+AT_STAGE2 = AT_STAGE1 + A * HALF
 AT_W_TILES23 = AT_STAGE2 + A * (H - 2 * P)
 AT_W1 = AT_W_TILES23 + A * 4 * P
 AT_GAIN = AT_W1 + A * 2 * PASS
@@ -63,10 +63,6 @@ AT_PAGE = [AT_PAGE0, AT_PAGE1, 0, 4 * T2, AT_TAB1, AT_TAB1 + 4 * T2, AT_TAB2, AT
 LAG = 768
 STRIPE = 16
 PIECES = [(lo, lo + QUARTER) for lo in range(0, M, QUARTER)]
-
-
-def pieces_in(lo, hi):
-    return [(first, end) for first, end in PIECES if lo <= first and end <= hi]
 
 
 def by_tile(ap):
@@ -233,8 +229,6 @@ def tile_list_seller_trust_cache_kernel(
         load_page(0)
         load_w(1, 1, AT_W_TILE1)
         stage_v_scales(1, keep.tile([P, HALF], U8, name="v_scale1", align_bytes=64)[:])
-        new_planes(AT_STAGE1, 1)
-        move_scales((nc.sync, nc.sync), 1)
 
         def scales(a, lo, hi):
             stage = [n for n, (first, end) in enumerate(STAGES) if first <= lo and hi <= end][0]
@@ -254,10 +248,12 @@ def tile_list_seller_trust_cache_kernel(
                 nc.sync.dma_start(out=wb_raw[b][:, t * N : (t + 1) * N], in_=wb_rows[b, t])
 
         gather_words(1, 0, S)
+        new_planes(AT_STAGE1, 1)
         new_planes(AT_STAGE2, 2)
         gather_words(2, 0, HALF, QUARTER)
         gather_words(2, HALF, S)
         load_page(1)
+        move_scales((nc.sync, nc.sync), 1)
         load_wg_plain(wg_plain, HALF, S)
         move_scales((nc.sync, nc.sync), 2)
         load_w(2, 2, AT_W_TILES23)
@@ -439,7 +435,6 @@ def tile_list_seller_trust_cache_kernel(
             weave(z[0, lo][:], flat[half][:])
 
         out_rows = out.rearrange("(n p) m -> p n m", p=P)
-        out_acc = {}
         staged = placed.tile([P, BANKS * HALF], F32, name="staged", offset=AT_WB, align_bytes=64)
 
         def banks_of(lo, hi):
@@ -448,47 +443,34 @@ def tile_list_seller_trust_cache_kernel(
                 return [((first + g) % BANKS, range(g, g + 1)) for g in range(N // P)]
             return [((first + g) % BANKS, range(2 * g, 2 * g + 2)) for g in range(2)]
 
-        def second_product(b, lo, hi, codes, scale):
-            width = hi - lo
-            for number, blocks in banks_of(lo, hi):
-                if b == 0:
-                    out_acc[lo, number] = bank(number, "acc_out")
-                for s, n in enumerate(blocks):
-                    nc.tensor.matmul_mx(
-                        out=out_acc[lo, number][:, s * width : (s + 1) * width],
-                        lhsT=wb_q[b][0][:, n * P : (n + 1) * P].bitcast(FP8X4),
-                        lhsT_scale=wb_q[b][1][:, n * P : (n + 1) * P],
-                        rhs=codes.bitcast(FP8X4),
-                        rhs_scale=scale,
-                        start=(b == 0 and s == 0),
-                        stop=(b == B - 1 and n == blocks[-1]),
-                    )
-
-        def store(lo, hi):
+        def finish(lo, hi, passes):
             for g, (number, blocks) in enumerate(banks_of(lo, hi)):
+                acc = bank(number, "acc_out")
+                width = hi - lo
+                for b, (codes, scale) in enumerate(passes):
+                    for s, n in enumerate(blocks):
+                        nc.tensor.matmul_mx(
+                            out=acc[:, s * width : (s + 1) * width],
+                            lhsT=wb_q[b][0][:, n * P : (n + 1) * P].bitcast(FP8X4),
+                            lhsT_scale=wb_q[b][1][:, n * P : (n + 1) * P],
+                            rhs=codes[:].bitcast(FP8X4),
+                            rhs_scale=scale[:],
+                            start=(b == 0 and s == 0),
+                            stop=(b == B - 1 and n == blocks[-1]),
+                        )
                 width = len(blocks) * (hi - lo)
                 res = staged[:, PACK * lo + g * width : PACK * lo + (g + 1) * width]
                 if hi == M and g % 2 == 1:
-                    nc.vector.tensor_copy(res, out_acc[lo, number][:, :width])
+                    nc.vector.tensor_copy(res, acc[:, :width])
                 else:
-                    nc.scalar.copy(res, out_acc[lo, number][:, :width])
+                    nc.scalar.copy(res, acc[:, :width])
                 nc.sync.dma_start(
                     out=out_rows[:, blocks[0] : blocks[-1] + 1, lo:hi],
                     in_=res.rearrange("p (s w) -> p s w", s=len(blocks)),
                 )
 
-        def multiply(b, lo, hi, quantized):
-            codes, scale = quantized
-            for first, end in pieces_in(lo, hi):
-                second_product(b, first, end, codes[:, first - lo : end - lo], scale[:, first - lo : end - lo])
-                if b == B - 1:
-                    store(first, end)
-
-        def quantize_z(b, lo, hi, behind):
+        def quantize_z(b, lo, hi, behind=None):
             return quantize(z_cols(b, lo, hi), hi - lo, "z%d_%d" % (b, lo), behind)
-
-        def finish(lo, hi, behind=None):
-            multiply(1, lo, hi, quantize_z(1, lo, hi, behind))
 
         for half in range(2):
             for i in range(2):
@@ -540,16 +522,12 @@ def tile_list_seller_trust_cache_kernel(
         for n, at in enumerate(root_at):
             root = placed.tile([P, QUARTER], F32, name="root7_%d" % n, offset=at, align_bytes=64)
             gather_page(LAST, n * QUARTER, (n + 1) * QUARTER, root, n * QUARTER)
-            if n == 1:
-                multiply(0, 0, HALF, quantize_z(0, 0, HALF, AT_WEIGHTED7 + 1024))
+        first_pass = quantize_z(0, *PIECES[0], AT_WEIGHTED7)
 
-        last_product(*PIECES[0])
-        wb_q[1] = quantize(wb_woven[1], N, "wb1", root_at[0])
-        finish(*PIECES[0])
-        for n in (1, 2):
-            last_product(*PIECES[n])
-            ahead = quantize_z(0, *PIECES[n + 1], root_at[n])
-            finish(*PIECES[n])
-            multiply(0, *PIECES[n + 1], ahead)
-        last_product(*PIECES[-1])
-        finish(*PIECES[-1])
+        for n, piece in enumerate(PIECES):
+            last_product(*piece)
+            if n == 0:
+                wb_q[1] = quantize(wb_woven[1], N, "wb1", root_at[0])
+            else:
+                first_pass = quantize_z(0, *piece, root_at[n])
+            finish(*piece, [first_pass, quantize_z(1, *piece)])

@@ -30,7 +30,9 @@ QUARTER = 256
 ROWS = A * 16
 ROW0 = 48
 STAGES = [(HALF, S + 2 * P), (0, HALF), (S + 2 * P, S + H)]
-AT_WG_FIRST = 4 * T
+AT_TAB2 = 0
+AT_TAB0 = 4 * T
+AT_WG_FIRST = AT_TAB0 + 4 * T
 AT_W_TILE1 = AT_WG_FIRST + 4 * HALF
 AT_PAGE0 = AT_W_TILE1 + A * 2 * P
 AT_PAGE1 = AT_PAGE0 + 4 * T2
@@ -44,8 +46,7 @@ AT_GAIN = AT_W1 + A * 2 * PASS
 AT_WB = AT_GAIN + 128
 AT_TAB1 = AT_WB + TILES * 4 * N
 AT_END = AT_TAB1 + 4 * T
-AT_TAB2 = AT_END
-AT_V0 = AT_TAB2 + 4 * T
+AT_V0 = AT_END
 ROOT_BYTES = 6 * 1024
 AT_FLAT = (AT_PAGE0 + 2 * PACK * HALF, AT_PAGE1)
 AT_ROOT = (AT_V0, AT_FLAT[0], AT_FLAT[1])
@@ -59,7 +60,7 @@ AT_RECIP_A = AT_WB_WOVEN0 + 2 * PACK * N
 AT_RECIP_B = AT_RECIP_A + 2 * 4 * M
 AT_WEIGHTED7 = AT_RECIP_B + 4 * M
 AT_Z1 = AT_RECIP_B + 2 * 4 * M
-AT_PAGE = [AT_PAGE0, AT_PAGE1, 0, 4 * T2, AT_TAB1, AT_TAB1 + 4 * T2, AT_TAB2, AT_TAB2 + 4 * T2]
+AT_PAGE = [AT_PAGE0, AT_PAGE1, AT_TAB0, AT_TAB0 + 4 * T2, AT_TAB1, AT_TAB1 + 4 * T2, AT_TAB2, AT_TAB2 + 4 * T2]
 LAG = 768
 STRIPE = 16
 PIECES = [(lo, lo + QUARTER) for lo in range(0, M, QUARTER)]
@@ -86,7 +87,7 @@ def tile_list_seller_trust_cache_kernel(
             return lst[:, lo // STRIPE : hi // STRIPE]
 
         tab_scale_win = keep.tile([P, T], U8, name="tab_scale_win", align_bytes=64)
-        w_scale_raw = placed.tile([P, H], U8, name="w_scale_raw", offset=AT_V0 - HALF - H, align_bytes=64)
+        w_scale_raw = placed.tile([P, H], U8, name="w_scale_raw", offset=AT_V0, align_bytes=64)
         planes = [keep.tile([P, A, HALF + 2 * P], U8, name="planes0", align_bytes=64)]
         for rows in (slice(0, ROW0), slice(ROW0 + ROWS, P)):
             nc.vector.memset(tab_scale_win[rows, :].bitcast(I32), 0)
@@ -95,7 +96,9 @@ def tile_list_seller_trust_cache_kernel(
 
         second_page = AT_PAGE1
         tab = [
-            placed.tile([P, second_page // 4], I32, name="tab0", offset=0, align_bytes=64)[:, :T],
+            placed.tile([P, (second_page - AT_TAB0 + 64) // 4], I32, name="tab0", offset=AT_TAB0 - 64, align_bytes=64)[
+                :, 16 : 16 + T
+            ],
             placed.tile([P, (AT_END - second_page) // 4], I32, name="tab1", offset=second_page, align_bytes=64)[
                 :, (AT_TAB1 - second_page) // 4 :
             ],
@@ -156,13 +159,13 @@ def tile_list_seller_trust_cache_kernel(
             for e in range(2):
                 nc.sync.dma_start(out=gain_sb[e:P:2, 2, 0 : 2 * PACK - 1], in_=gain_rows[1][:, e : e + 2 * PACK - 1])
 
-        load_tab(0, 0, T // 2)
+        load_tab(0, 0, 3 * T // 8)
         for tile, rows in ((tab_scale_win, tab_scales), (w_scale_raw, w4_scales)):
             nc.sync.dma_start(
                 out=tile[ROW0 : ROW0 + ROWS, :].bitcast(I32), in_=rows.rearrange("a q n -> q a n").bitcast(I32)
             )
         nc.sync.dma_start(list1[:], offs)
-        load_tab(0, T // 2, T)
+        load_tab(0, 3 * T // 8, T)
         load_w(0, 1)
         load_tab(1)
         nc.sync.dma_start(list2[:], offs2)
@@ -174,14 +177,12 @@ def tile_list_seller_trust_cache_kernel(
             first = (1 - half) * HALF
             nc.vector.tensor_copy(staged_scales[:, first : first + HALF].bitcast(I32), v_scale.bitcast(I32))
 
-        stage_v_scales(
-            0, placed.tile([P, 2 * HALF], U8, name="v_scale0", offset=AT_V0 - HALF, align_bytes=64)[:, :HALF]
-        )
         nc.vector.tensor_copy(staged_scales[:, S : S + PASS].bitcast(I32), w_scale_raw[:, :PASS].bitcast(I32))
         nc.vector.tensor_copy(
             staged_scales[:, S + PASS :].bitcast(U16).rearrange("p (t c i) -> p c t i", t=PACK, i=8),
             w_scale_raw[:, PASS:].bitcast(U16).rearrange("p (c i t) -> p c t i", i=8, t=PACK),
         )
+        stage_v_scales(0, placed.tile([P, HALF], U8, name="v_scale0", offset=AT_V0 + H, align_bytes=64)[:])
 
         def move_scales(queues, stage):
             target = planes[stage]
@@ -198,8 +199,7 @@ def tile_list_seller_trust_cache_kernel(
             planes.append(placed.tile([P, A, hi - lo], U8, name="planes%d" % stage, offset=at, align_bytes=64))
             nc.vector.memset(planes[stage][:].bitcast(I32), 0)
 
-        move_scales((nc.sync, nc.scalar), 0)
-        load_tab(2)
+        move_scales((nc.scalar, nc.scalar), 0)
 
         def order_w_codes(raw):
             ordered = keep.tile([P, A, PACK, 2 * P], U8, name="w_ordered", align_bytes=64)
@@ -225,6 +225,7 @@ def tile_list_seller_trust_cache_kernel(
                 v_codes[a, c // HALF] = picked[:, c - lo : c - lo + HALF]
 
         gather_words(0, 0, S)
+        load_tab(2)
         load_wg_plain(wg_first, 0, HALF)
         load_page(0)
         load_w(1, 1, AT_W_TILE1)

@@ -258,11 +258,11 @@ def tile_list_seller_trust_cache_kernel(
         load_wg_plain(wg_plain, HALF, S)
         move_scales((nc.sync, nc.sync), 2)
         load_w(2, 2, AT_W_TILES23)
-        load_gain()
         load_page(2)
         nc.sync.dma_start(list3[:], offs3)
         load_page(3)
         load_wg_plain(wg_plain, 0, HALF)
+        load_gain()
         w_raw = load_w(PACK, PACK, AT_W1)
         load_wb(0)
         load_wb(1)

@@ -521,7 +521,8 @@ def tile_list_seller_trust_cache_kernel(
         wb_q[0] = quantize(wb_woven[0], N, "wb0", AT_WB1_CODES)
         root_at = [AT_ROOT[2] + 1024 * n for n in (0, 2, 4, 5)]
         for n, at in enumerate(root_at):
-            root = placed.tile([P, QUARTER], F32, name="root7_%d" % n, offset=at, align_bytes=64)
+            width = ROOT_BYTES // 4 if n == 0 else QUARTER
+            root = placed.tile([P, width], F32, name="root7_%d" % n, offset=at, align_bytes=64)
             gather_page(LAST, n * QUARTER, (n + 1) * QUARTER, root, n * QUARTER)
         first_pass = quantize_z(0, *PIECES[0], AT_WEIGHTED7)
 

from contextlib import ExitStack

import concourse.mybir as mybir

K, H, N, T, S, T2, M = 1536, 1024, 512, 4096, 1024, 2048, 1024
FLOPS = 2 * K * H * S + 2 * H * N * M

F32 = mybir.dt.float32
BF16 = mybir.dt.bfloat16
I32 = mybir.dt.int32
U32 = mybir.dt.uint32
U16 = mybir.dt.uint16
U8 = mybir.dt.uint8
FP8X4 = mybir.dt.float8_e4m3fn_x4
FP4X4 = mybir.dt.float4_e2m1fn_x4
MULT = mybir.AluOpType.mult
ACT = mybir.ActivationFunctionType

P = 128
QUAD = 32
PACK = 4
PASS = P * PACK
A = K // PASS
B = H // PASS
TILES = B * PACK
LAST = TILES - 1
BANKS = 8
HALF = 512
QUARTER = 256
ROWS = A * 16
ROW0 = 48
STAGES = [(HALF, S + 2 * P), (0, HALF), (S + 2 * P, S + H)]
AT_TAB2 = 0
AT_TAB0 = 4 * T
AT_WG_FIRST = AT_TAB0 + 4 * T
AT_W_TILE1 = AT_WG_FIRST + 4 * HALF
AT_PAGE0 = AT_W_TILE1 + A * 2 * P
AT_PAGE1 = AT_PAGE0 + 4 * T2
AT_WG = AT_PAGE1 + 4 * T2
AT_WG_PLAIN = AT_WG + PACK * 4 * S
AT_STAGE1 = AT_WG_PLAIN + 4 * S
AT_STAGE2 = AT_STAGE1 + A * HALF
AT_W_TILES23 = AT_STAGE2 + A * (H - 2 * P)
AT_W1 = AT_W_TILES23 + A * 4 * P
AT_GAIN = AT_W1 + A * 2 * PASS
AT_WB = AT_GAIN + 128
AT_TAB1 = AT_WB + TILES * 4 * N
AT_END = AT_TAB1 + 4 * T
AT_V0 = AT_END
ROOT_BYTES = 6 * 1024
AT_FLAT = (AT_PAGE0 + 2 * PACK * HALF, AT_PAGE1)
AT_ROOT = (AT_V0, AT_FLAT[0], AT_FLAT[1])
AT_Z0 = (AT_V0 + ROOT_BYTES, AT_PAGE0)
AT_H7 = AT_Z0[0] + 2 * PACK * HALF
AT_WB1_CODES = AT_H7
AT_WEIGHTED3 = AT_H7 + 4 * S
AT_WEIGHTED4 = AT_WEIGHTED3 + 4 * S
AT_WB_WOVEN0 = AT_WEIGHTED4 + 4 * S
AT_RECIP_A = AT_WB_WOVEN0 + 2 * PACK * N
AT_RECIP_B = AT_RECIP_A + 2 * 4 * M
AT_WEIGHTED7 = AT_RECIP_B + 4 * M
AT_Z1 = AT_RECIP_B + 2 * 4 * M
AT_PAGE = [AT_PAGE0, AT_PAGE1, AT_TAB0, AT_TAB0 + 4 * T2, AT_TAB1, AT_TAB1 + 4 * T2, AT_TAB2, AT_TAB2 + 4 * T2]
LAG = 768
STRIPE = 16
PIECES = [(lo, lo + QUARTER) for lo in range(0, M, QUARTER)]


def by_tile(ap):
    return ap.rearrange("p (t m) -> p t m", t=PACK)


def tile_list_seller_trust_cache_kernel(
    tc, tab_words, tab_scales, offs, w4_words, w4_scales, wgs, page0, offs2, offs3, gain, wb, out
):
    nc = tc.nc
    with ExitStack() as ctx:
        keep = ctx.enter_context(tc.tile_pool(name="keep", bufs=1))
        placed = ctx.enter_context(tc.tile_pool(name="placed", bufs=1))
        psum = ctx.enter_context(tc.psum_pool(name="psum", bufs=1))

        list1 = keep.tile([P, S // STRIPE], U16, name="list1")
        list2 = keep.tile([P, S // STRIPE], U16, name="list2")
        list3 = keep.tile([P, M // STRIPE], U16, name="list3")

        def entries(lst, lo, hi):
            return lst[:, lo // STRIPE : hi // STRIPE]

        tab_scale_win = keep.tile([P, T], U8, name="tab_scale_win", align_bytes=64)
        w_scale_raw = placed.tile([P, H], U8, name="w_scale_raw", offset=AT_V0, align_bytes=64)
        planes = [keep.tile([P, A, HALF + 2 * P], U8, name="planes0", align_bytes=64)]
        for rows in (slice(0, ROW0), slice(ROW0 + ROWS, P)):
            nc.vector.memset(tab_scale_win[rows, :].bitcast(I32), 0)
            nc.vector.memset(w_scale_raw[rows, :].bitcast(I32), 0)
        nc.vector.memset(planes[0][:].bitcast(I32), 0)

        second_page = AT_PAGE1
        tab = [
            placed.tile([P, (second_page - AT_TAB0 + 64) // 4], I32, name="tab0", offset=AT_TAB0 - 64, align_bytes=64)[
                :, 16 : 16 + T
            ],
            placed.tile([P, (AT_END - second_page) // 4], I32, name="tab1", offset=second_page, align_bytes=64)[
                :, (AT_TAB1 - second_page) // 4 :
            ],
            placed.tile([P, T], I32, name="tab2", offset=AT_TAB2, align_bytes=64)[:],
        ]

        def load_tab(a, lo=0, hi=T):
            words = tab_words[a].rearrange("p n t -> p (n t)").bitcast(I32)
            nc.sync.dma_start(out=tab[a][:, lo:hi], in_=words[:, lo:hi])

        w_words_i32 = w4_words.rearrange("a p n -> p a n").bitcast(I32)
        w_codes = {}

        def load_w(first, count, at=None):
            if at is None:
                tile = keep.tile([P, A, count * 2 * P], U8, name="w_raw%d" % first, align_bytes=64)
            else:
                tile = placed.tile([P, A, count * 2 * P], U8, name="w_raw%d" % first, offset=at, align_bytes=64)
            words = w_words_i32[:, :, first * P // 2 : (first + count) * P // 2]
            nc.sync.dma_start(out=tile[:].bitcast(I32), in_=words)
            for i in range(count):
                w_codes[first + i] = tile[:, :, i * 2 * P : (i + 1) * 2 * P]
            return tile

        wg = [
            placed.tile([P, S], F32, name="wg%d" % t, tag="wg%d" % t, offset=AT_WG + 4 * S * t, align_bytes=64)
            for t in range(PACK)
        ]
        wgs_rows = wgs.rearrange("(u t e) j -> t u e j", t=PACK, e=2)

        wg_first = placed.tile([P, HALF], F32, name="wg_first", offset=AT_WG_FIRST, align_bytes=64)
        wg_plain = placed.tile([P, S], F32, name="wg_plain", offset=AT_WG_PLAIN, align_bytes=64)

        def load_wg(t):
            for q in (0, 2, 1, 3):
                nc.sync.dma_start(out=wg[t][QUAD * q : QUAD * (q + 1), :], in_=wgs_rows[t])

        def load_wg_plain(tile, lo, hi):
            nc.sync.dma_start(out=tile[:, lo:hi], in_=wgs[:, lo:hi])

        page_rows = page0.rearrange("(b u t e) c -> b t u e c", b=B, t=PACK, e=2)
        page = {}

        def load_page(i):
            page[i] = placed.tile([P, T2], F32, name="page%d" % i, offset=AT_PAGE[i], align_bytes=64)
            rows = page0[i * P : (i + 1) * P, :] if i < PACK else page_rows[1, i - PACK]
            nc.sync.dma_start(out=page[i][:], in_=rows)

        gain_rows = gain.rearrange("(b u w) -> b u w", b=B, w=2 * PACK)
        gain_sb = placed.tile([P, 3, 2 * PACK], F32, name="gain_sb", offset=AT_GAIN, align_bytes=64)

        def load_gain():
            with nc.allow_non_contiguous_dma(reason="one gain for each partition and row tile"):
                nc.sync.dma_start(
                    out=gain_sb[:, 0, 0 : 2 * PACK : 2], in_=gain[0:PASS].rearrange("(i p) -> p i", p=P)
                )
            nc.sync.dma_start(out=gain_sb[:, 1, 0:PACK], in_=gain[0:PASS].rearrange("(p t) -> p t", t=PACK))
            for e in range(2):
                nc.sync.dma_start(out=gain_sb[e:P:2, 2, 0 : 2 * PACK - 1], in_=gain_rows[1][:, e : e + 2 * PACK - 1])

        load_tab(0, 0, 3 * T // 8)
        for tile, rows in ((tab_scale_win, tab_scales), (w_scale_raw, w4_scales)):
            nc.sync.dma_start(
                out=tile[ROW0 : ROW0 + ROWS, :].bitcast(I32), in_=rows.rearrange("a q n -> q a n").bitcast(I32)
            )
        nc.sync.dma_start(list1[:], offs)
        load_tab(0, 3 * T // 8, T)
        load_w(0, 1)
        load_tab(1)
        nc.sync.dma_start(list2[:], offs2)

        staged_scales = keep.tile([P, S + H], U8, name="staged_scales", align_bytes=64)

        def stage_v_scales(half, v_scale):
            nc.vector.tensor_copy(v_scale, tab_scale_win[:].indirect(entries(list1, half * HALF, (half + 1) * HALF)))
            first = (1 - half) * HALF
            nc.vector.tensor_copy(staged_scales[:, first : first + HALF].bitcast(I32), v_scale.bitcast(I32))

        nc.vector.tensor_copy(staged_scales[:, S : S + PASS].bitcast(I32), w_scale_raw[:, :PASS].bitcast(I32))
        nc.vector.tensor_copy(
            staged_scales[:, S + PASS :].bitcast(U16).rearrange("p (t c i) -> p c t i", t=PACK, i=8),
            w_scale_raw[:, PASS:].bitcast(U16).rearrange("p (c i t) -> p c t i", i=8, t=PACK),
        )
        stage_v_scales(0, placed.tile([P, HALF], U8, name="v_scale0", offset=AT_V0 + H, align_bytes=64)[:])

        def move_scales(queues, stage):
            target = planes[stage]
            lo, hi = STAGES[stage]
            for q in (0, 2, 1, 3):
                first = ROW0 + 4 * A * q
                queues[q % 2].dma_start(
                    out=target[QUAD * q : QUAD * q + 4, :, :].bitcast(I32),
                    in_=staged_scales[first : first + 4 * A, lo:hi].bitcast(I32),
                )

        def new_planes(at, stage):
            lo, hi = STAGES[stage]
            planes.append(placed.tile([P, A, hi - lo], U8, name="planes%d" % stage, offset=at, align_bytes=64))
            nc.vector.memset(planes[stage][:].bitcast(I32), 0)

        move_scales((nc.scalar, nc.scalar), 0)

        def order_w_codes(raw):
            ordered = keep.tile([P, A, PACK, 2 * P], U8, name="w_ordered", align_bytes=64)
            nc.scalar.copy(
                ordered[:].bitcast(U32).rearrange("p a t (c i) -> p a c t i", i=4),
                raw[:].bitcast(U32).rearrange("p a (c i t) -> p a c t i", i=4, t=PACK),
            )
            for t in range(PACK):
                w_codes[PACK + t] = ordered[:, :, t, :]

        v_codes = {}

        def gather_words(a, lo, hi, step=S):
            if a == 0:
                picked = placed.tile([P, hi - lo], U32, name="picked0", offset=AT_V0, align_bytes=64)
            else:
                picked = keep.tile([P, hi - lo], U32, name="picked", tag="v_codes%d_%d" % (a, lo), align_bytes=64)
            for c in range(lo, hi, step):
                end = min(hi, c + step)
                window = tab[a].bitcast(U32).indirect(entries(list1, c, end))
                nc.vector.tensor_copy(picked[:, c - lo : end - lo], window)
            for c in range(lo, hi, HALF):
                v_codes[a, c // HALF] = picked[:, c - lo : c - lo + HALF]

        gather_words(0, 0, S)
        load_tab(2)
        load_wg_plain(wg_first, 0, HALF)
        load_page(0)
        load_w(1, 1, AT_W_TILE1)
        stage_v_scales(1, keep.tile([P, HALF], U8, name="v_scale1", align_bytes=64)[:])

        def scales(a, lo, hi):
            stage = [n for n, (first, end) in enumerate(STAGES) if first <= lo and hi <= end][0]
            return planes[stage][:, a, lo - STAGES[stage][0] : hi - STAGES[stage][0]]

        wb_rows = wb.rearrange("(b u t e) n -> b t u e n", b=B, t=PACK, e=2)
        wb_raw = [
            placed.tile([P, PACK * N], F32, name="wb_raw%d" % b, offset=AT_WB + (B - 1 - b) * PACK * 4 * N, align_bytes=64)
            for b in range(B)
        ]

        def load_wb(b):
            if b == 0:
                nc.sync.dma_start(out=wb_raw[b][:], in_=wb[0:PASS, :].rearrange("(p t) n -> p (t n)", t=PACK))
                return
            for t in range(PACK):
                nc.sync.dma_start(out=wb_raw[b][:, t * N : (t + 1) * N], in_=wb_rows[b, t])

        gather_words(1, 0, S)
        new_planes(AT_STAGE1, 1)
        new_planes(AT_STAGE2, 2)
        gather_words(2, 0, HALF, QUARTER)
        gather_words(2, HALF, S)
        load_page(1)
        move_scales((nc.sync, nc.sync), 1)
        load_wg_plain(wg_plain, HALF, S)
        move_scales((nc.sync, nc.sync), 2)
        load_w(2, 2, AT_W_TILES23)
        load_page(2)
        nc.sync.dma_start(list3[:], offs3)
        load_page(3)
        load_wg_plain(wg_plain, 0, HALF)
        load_gain()
        w_raw = load_w(PACK, PACK, AT_W1)
        load_wb(0)
        load_wb(1)
        load_page(4)
        load_page(5)
        for t in range(PACK):
            load_wg(t)
        load_page(6)
        load_page(7)

        def bank(n, name):
            return psum.tile([P, HALF], F32, name=name, tag="bank%d" % n)

        x_start = S + QUARTER
        arena = keep.tile([P, x_start + TILES * M], F32, name="arena", align_bytes=64)
        h_start = {i: S + S * i for i in range(2, LAST)}
        h_start[0] = 2 * S
        h_start[1] = 0
        h_last = placed.tile([P, S], F32, name="h_last", offset=AT_H7, align_bytes=64)

        def h_cols(i, lo, hi):
            if i == LAST:
                return h_last[:, lo:hi]
            return arena[:, h_start[i] + lo : h_start[i] + hi]

        def x_tiles(i, count):
            return arena[:, x_start + i * M : x_start + (i + count) * M].rearrange("p (t m) -> p t m", t=count)

        def first_product(i, halves=(0, 1)):
            order = list(range(A)) if i == 0 else [A - 1] + list(range(A - 1))
            for half in halves:
                parts = [(0, 0, QUARTER), (LAST, QUARTER, HALF)] if (i, half) == (0, 0) else [(2 * i + half, 0, HALF)]
                for number, lo, hi in parts:
                    product_part(i, half, order, bank(number % BANKS, "acc_h")[:, : hi - lo], lo, hi)

        def product_part(i, half, order, acc, lo, hi):
            for a in order:
                nc.tensor.matmul_mx(
                    out=acc,
                    lhsT=w_codes[i][:, a, :].bitcast(FP4X4),
                    lhsT_scale=scales(a, S + i * P, S + (i + 1) * P),
                    rhs=v_codes[a, half][:, lo:hi].bitcast(FP8X4),
                    rhs_scale=scales(a, (1 - half) * HALF + lo, (1 - half) * HALF + hi),
                    start=(a == order[0]),
                    stop=(a == order[-1]),
                )
            nc.scalar.copy(h_cols(i, half * HALF + lo, half * HALF + hi), acc)

        def scatter(i, lo, hi):
            weights = wg_first if lo == 0 else wg_plain
            nc.vector.tensor_tensor(
                page[i][:].indirect(entries(list2, lo, hi)), h_cols(i, lo, hi), weights[:, lo:hi], MULT
            )

        weighted = {}

        weighted_at = {3: AT_WEIGHTED3, 4: AT_WEIGHTED4, 5: AT_WG, 7: AT_WEIGHTED7}

        def weigh(i):
            if i in weighted_at:
                weighted[i] = placed.tile([P, S], F32, name="weighted%d" % i, offset=weighted_at[i], align_bytes=64)[:]
            elif i == LAST - 1:
                weighted[i] = x_tiles(1, 1)[:, 0, :]
            else:
                weighted[i] = arena[:, :S]
            nc.gpsimd.tensor_tensor(weighted[i], h_cols(i, 0, S), (wg_plain if i < PACK else wg[i - PACK])[:], MULT)

        def scatter_weighted(i):
            nc.vector.tensor_copy(page[i][:].indirect(list2[:]), weighted[i])

        gain_root = keep.tile([P, B, PACK], F32, name="gain_root")
        gain_sign = keep.tile([P, B, PACK], F32, name="gain_sign")

        def split_gain():
            gains = gain_sb[:, 0:3:2, 0 : 2 * PACK : 2]
            nc.scalar.activation(gain_root[:], gains, ACT.Abs)
            nc.scalar.activation(gain_root[:], gain_root[:], ACT.Sqrt)
            nc.scalar.activation(gain_sign[:, 0, :], gain_sb[:, 1, 0:PACK], ACT.Sign)
            nc.scalar.activation(gain_sign[:, 1, :], gains[:, 1, :], ACT.Sign)
            nc.scalar.activation(gain_sign[:], gain_sign[:], ACT.Sign, bias=0.5)

        recip = {}

        groups = [(0, 2, AT_RECIP_A), (2, 2, AT_RECIP_B), (4, 1, AT_RECIP_A), (5, 3, AT_RECIP_A)]

        def recip_rows(i, count, lo, hi):
            first, size, at = [group for group in groups if group[0] <= i][-1]
            if first not in recip:
                recip[first] = placed.tile([P, size, M], F32, name="recip%d" % first, offset=at, align_bytes=64)
            return recip[first][:, i - first : i - first + count, lo:hi]

        def new_root(stage, back=0, forward=0):
            width = ((ROOT_BYTES, 4 * M, ROOT_BYTES)[stage] + back + forward) // 4
            name = "root_%d_%d" % (stage, width)
            return placed.tile([P, width], F32, name=name, offset=AT_ROOT[stage] - back, align_bytes=64)

        def gather_page(i, lo, hi, root, origin=0):
            b, t = divmod(i, PACK)
            x = x_tiles(i, 1)[:, 0, lo:hi]
            nc.vector.tensor_copy(x, page[i][:].indirect(entries(list3, lo, hi)))
            part = root[:, lo - origin : hi - origin]
            nc.scalar.activation(part, x, ACT.Abs)
            nc.scalar.activation(part, part, ACT.Abs_reciprocal_sqrt, bias=1.0)
            nc.scalar.activation(recip_rows(i, 1, lo, hi)[:, 0, :], part, ACT.Square, scale=gain_root[:, b, t : t + 1])

        def weave(woven, flat):
            nc.scalar.copy(
                woven.rearrange("p (c i) t -> p c t i", i=4), flat.rearrange("p t (c i) -> p c t i", i=4)
            )

        def quantize(woven, width, name, behind):
            if isinstance(behind, int):
                codes = placed.tile([P, width], U32, name=name + "_codes", offset=behind, align_bytes=64)
            else:
                codes = keep.tile([P, width], U32, name=name + "_codes", tag=behind or name, align_bytes=64)
            scale = keep.tile([P, width], U8, name=name + "_scale", align_bytes=64)
            nc.vector.quantize_mx(
                out=codes[:].bitcast(FP8X4), scales=scale[:], in_=woven.rearrange("p w t -> p (w t)")
            )
            return codes, scale

        wb_woven = {}
        wb_q = {}

        def weave_wb(b):
            for t in range(PACK):
                rows = wb_raw[b][:, t * N : (t + 1) * N]
                nc.scalar.activation(rows, rows, ACT.Copy, scale=gain_sign[:, b, t : t + 1])
            if b == 0:
                wb_woven[b] = placed.tile([P, N, PACK], BF16, name="wb_woven0", offset=AT_WB_WOVEN0, align_bytes=64)[:]
            else:
                wb_woven[b] = keep.tile([P, N, PACK], BF16, name="wb_woven1", align_bytes=64)[:]
            weave(wb_woven[b], by_tile(wb_raw[b][:]))

        z = {(1, 0): placed.tile([P, M, PACK], BF16, name="z1", offset=AT_Z1, align_bytes=64)}

        def z_cols(b, lo, hi):
            first = lo - lo % HALF if b == 0 else 0
            return z[b, first][:, lo - first : hi - first, :]

        def z_words(engine, i, count, lo, hi):
            engine.tensor_tensor(
                z_cols(1, lo, hi)[:, :, i - PACK : i - PACK + count].rearrange("p (c i) t -> p c t i", i=2),
                x_tiles(i, count)[:, :, lo:hi].rearrange("p t (c i) -> p c t i", i=2),
                recip_rows(i, count, lo, hi).rearrange("p t (c i) -> p c t i", i=2),
                MULT,
            )

        def last_product(lo, hi):
            z_words(nc.vector, PACK + 1, PACK - 1, lo, hi)

        flat = [
            placed.tile([P, PACK, HALF], BF16, name="flat%d" % half, offset=AT_FLAT[half], align_bytes=64)
            for half in range(2)
        ]

        def z_flat(i, half):
            lo, hi = half * HALF, (half + 1) * HALF
            factor = recip_rows(i, 1, lo, hi)[:, 0, :]
            if i < 2:
                rows = arena[:, (2 * i + half) * QUARTER : (2 * i + half + 1) * QUARTER].bitcast(BF16)
            else:
                at = AT_WEIGHTED3 + (2 * (i - 2) + half) * 2 * HALF
                rows = placed.tile([P, HALF], BF16, name="z_rows%d_%d" % (i, half), offset=at, align_bytes=64)[:]
            nc.gpsimd.tensor_tensor(rows, x_tiles(i, 1)[:, 0, lo:hi], factor, MULT)
            nc.sync.dma_start(out=flat[half][QUAD * i : QUAD * (i + 1), :, :], in_=rows)

        def weave_z(half):
            lo = half * HALF
            z[0, lo] = placed.tile([P, HALF, PACK], BF16, name="z0_%d" % lo, offset=AT_Z0[half], align_bytes=64)
            weave(z[0, lo][:], flat[half][:])

        out_rows = out.rearrange("(n p) m -> p n m", p=P)
        staged = placed.tile([P, BANKS * HALF], F32, name="staged", offset=AT_WB, align_bytes=64)

        def banks_of(lo, hi):
            first = 2 * PIECES.index((lo, hi))
            if hi == M:
                return [((first + g) % BANKS, range(g, g + 1)) for g in range(N // P)]
            return [((first + g) % BANKS, range(2 * g, 2 * g + 2)) for g in range(2)]

        def finish(lo, hi, passes):
            for g, (number, blocks) in enumerate(banks_of(lo, hi)):
                acc = bank(number, "acc_out")
                width = hi - lo
                for b, (codes, scale) in enumerate(passes):
                    for s, n in enumerate(blocks):
                        nc.tensor.matmul_mx(
                            out=acc[:, s * width : (s + 1) * width],
                            lhsT=wb_q[b][0][:, n * P : (n + 1) * P].bitcast(FP8X4),
                            lhsT_scale=wb_q[b][1][:, n * P : (n + 1) * P],
                            rhs=codes[:].bitcast(FP8X4),
                            rhs_scale=scale[:],
                            start=(b == 0 and s == 0),
                            stop=(b == B - 1 and n == blocks[-1]),
                        )
                width = len(blocks) * (hi - lo)
                res = staged[:, PACK * lo + g * width : PACK * lo + (g + 1) * width]
                if hi == M and g % 2 == 1:
                    nc.vector.tensor_copy(res, acc[:, :width])
                else:
                    nc.scalar.copy(res, acc[:, :width])
                nc.sync.dma_start(
                    out=out_rows[:, blocks[0] : blocks[-1] + 1, lo:hi],
                    in_=res.rearrange("p (s w) -> p s w", s=len(blocks)),
                )

        def quantize_z(b, lo, hi, behind=None):
            return quantize(z_cols(b, lo, hi), hi - lo, "z%d_%d" % (b, lo), behind)

        for half in range(2):
            for i in range(2):
                first_product(i, (half,))
                scatter(i, half * HALF, (half + 1) * HALF)
        for i in range(2, PACK):
            first_product(i)
        split_gain()
        order_w_codes(w_raw)
        for i in range(PACK, TILES):
            first_product(i)
        gather_page(0, 0, M, new_root(0))
        gather_page(1, 0, LAG, new_root(0))
        weigh(2)
        weigh(3)
        weave_wb(0)
        weave_wb(1)
        for i in range(2, LAST):
            scatter_weighted(i)
            if i == 2:
                weigh(4)
                weigh(5)
            if i == 3:
                weigh(6)
            gather_page(i - 1, LAG, M, new_root(max(0, i - PACK)))
            if i == 2:
                z_flat(0, 0)
                z_flat(0, 1)
                z_flat(1, 0)
            if i <= PACK:
                z_flat(i - 1, 1)
            if i == PACK + 1:
                z_words(nc.gpsimd, PACK, 1, LAG, M)
            if i < LAST - 1:
                gather_page(i, 0, LAG, new_root(max(0, i - PACK), back=64 * (i == PACK + 1), forward=64 * (i == PACK)))
            if i == PACK:
                weigh(LAST)
            if i < PACK:
                z_flat(i, 0)
            if i in (PACK, PACK + 1):
                weave_z(i - PACK)
            if i == PACK:
                z_words(nc.gpsimd, PACK, 1, 0, LAG)
        gather_page(LAST - 1, 0, M, new_root(2))

        scatter_weighted(LAST)
        wb_q[0] = quantize(wb_woven[0], N, "wb0", AT_WB1_CODES)
        root_at = [AT_ROOT[2] + 1024 * n for n in (0, 2, 4, 5)]
        for n, at in enumerate(root_at):
            width = ROOT_BYTES // 4 if n == 0 else QUARTER
            root = placed.tile([P, width], F32, name="root7_%d" % n, offset=at, align_bytes=64)
            gather_page(LAST, n * QUARTER, (n + 1) * QUARTER, root, n * QUARTER)
        first_pass = quantize_z(0, *PIECES[0], AT_WEIGHTED7)

        for n, piece in enumerate(PIECES):
            last_product(*piece)
            if n == 0:
                wb_q[1] = quantize(wb_woven[1], N, "wb1", root_at[0])
            else:
                first_pass = quantize_z(0, *piece, root_at[n])
            finish(*piece, [first_pass, quantize_z(1, *piece)])
